import numpy as np
import ml_dtypes


def mxq(x, axis, fmt="e4m3"):
    dtype, down = {"e4m3": (ml_dtypes.float8_e4m3fn, 7), "e5m2": (ml_dtypes.float8_e5m2, 14)}[fmt]
    v = np.moveaxis(np.asarray(x, np.float32).astype(ml_dtypes.bfloat16).astype(np.float64), axis, -1)
    blocks = v.reshape(v.shape[:-1] + (-1, 32))
    amax = np.abs(blocks).max(-1, keepdims=True)
    byte = np.maximum(np.where(amax > 0, np.frexp(amax)[1] - 1 + 127, 0) - down, 1)
    scale = np.exp2(byte - 127.0)
    codes = (blocks / scale).astype(np.float32).astype(dtype).astype(np.float64)
    return np.moveaxis((codes * scale).reshape(v.shape), -1, axis)


WIDE = False


def mx_kscale(k):
    if not WIDE:
        return np.ones(k)
    levels = np.array([10, -10, 5, -5, 0])
    if k % 512:
        return np.exp2(np.random.permutation(np.resize(levels, k // 32))).repeat(32)
    a = np.empty((k // 512, 16))
    for p in range(k // 512):
        a[p, :8] = np.random.permutation(np.resize(levels, 8))
        for g in range(8):
            far = levels[np.abs(levels - a[p, g]) >= 10]
            a[p, g + 8] = far[np.random.randint(len(far))]
    return np.exp2(a.ravel()).repeat(32)


def f64(x):
    return np.asarray(x).astype(np.float64)


def striped(idx):
    return np.tile(idx.reshape(-1, 16).T, (8, 1)).astype(np.uint16)


def unstriped(offs):
    return offs[:16].T.reshape(-1).astype(np.int64)


E2M1 = np.array([0.0, 0.5, 1.0, 1.5, 2.0, 3.0, 4.0, 6.0, -0.0, -0.5, -1.0, -1.5, -2.0, -3.0, -4.0, -6.0])


def pack_weight(w, fmt):
    k, n = w.shape
    w = f64(np.asarray(w, np.float32).astype(ml_dtypes.bfloat16)).reshape(k // 32, 32, n)
    amax = np.abs(w).max(1)
    if fmt == "e4m3":
        byte = np.frexp(amax)[1] - 1 + 127 - 7
    else:
        mant, ex = np.frexp(amax / 6.0)
        byte = np.where(mant > 0.5, ex, ex - 1) + 127
    byte = np.clip(np.where(amax > 0, byte, 1), 1, 254)
    scaled = (w * np.exp2(127.0 - byte)[:, None, :]).reshape(k, n).astype(np.float32)
    by_word = np.ascontiguousarray(scaled.reshape(k // 512, 128, 4, n).transpose(0, 1, 3, 2))
    if fmt == "e4m3":
        words = by_word.astype(ml_dtypes.float8_e4m3fn).view(np.uint8)
    else:
        c = by_word.astype(ml_dtypes.float4_e2m1fn).view(np.uint8) & 0xF
        words = (c[..., 0::2] | (c[..., 1::2] << 4)).reshape(k // 512, 128, 2 * n)
    return np.ascontiguousarray(words), np.ascontiguousarray(byte.astype(np.uint8).reshape(k // 512, 16, n))


def unpack_weight(words, scales, fmt):
    g, _, n = scales.shape
    words = np.ascontiguousarray(words).reshape(g, 128, n, -1)
    if fmt == "e4m3":
        vals = words.view(ml_dtypes.float8_e4m3fn).astype(np.float64)
    else:
        nib = np.empty((g, 128, n, 4), np.uint8)
        nib[..., 0::2] = words & 0xF
        nib[..., 1::2] = words >> 4
        vals = E2M1[nib]
    vals = vals * np.repeat(np.exp2(scales.astype(np.float64) - 127.0), 8, axis=1)[..., None]
    return vals.transpose(0, 1, 3, 2).reshape(g * 512, n)


def gelu(v):
    return 0.5 * v * (1.0 + np.tanh(np.sqrt(2.0 / np.pi) * (v + 0.044715 * v**3)))


def often(T, S):
    return np.random.permutation(T)[(T * np.random.uniform(0, 1, S) ** 4).astype(np.int64)]


def bf(x):
    return np.asarray(x, np.float32).astype(ml_dtypes.bfloat16)


def planes(Y):
    n, m = Y.shape
    b = f64(bf(Y)).reshape(n // 32, 32, m)
    amax = np.abs(b).max(1)
    byte = np.clip(np.where(amax > 0, np.frexp(amax)[1] - 1 + 127 - 7, 1), 1, 254)
    codes = (b * np.exp2(127.0 - byte)[:, None, :]).reshape(n, m).astype(np.float32).astype(ml_dtypes.float8_e4m3fn).view(np.uint8)
    words = codes.reshape(n // 512, 128, 4, m).transpose(0, 1, 3, 2)
    return np.ascontiguousarray(words), np.ascontiguousarray(byte.astype(np.uint8).reshape(n // 512, 16, m))


K, K2, H, N, T, S = 1024, 512, 512, 1024, 4096, 1024

def setup_inputs():
    n = np.random.standard_normal
    s = mx_kscale(K)[:, None]
    s2 = mx_kscale(K2)[:, None]
    u = mx_kscale(H)[:, None]
    tab_words, tab_scales = pack_weight(n((K, T)) * s, "e4m3")
    tab2_words, tab2_scales = pack_weight(n((K2, T)) * s2, "e2m1")
    w1_words, w1_scales = pack_weight(n((K, H)) / np.sqrt(K) / s, "e2m1")
    w3_words, w3_scales = pack_weight(n((K2, H)) / np.sqrt(K2) / s2 * u.T, "e4m3")
    amp = np.exp(0.8 * n(N))
    return {
        "tab_words": tab_words, "tab_scales": tab_scales,
        "tab2_words": tab2_words, "tab2_scales": tab2_scales,
        "offs": striped(often(T, S)),
        "offs2": striped(often(T, S)),
        "w1_words": w1_words, "w1_scales": w1_scales,
        "w2": (n((K, H)) / np.sqrt(K) / s).astype(np.float32),
        "w3_words": w3_words, "w3_scales": w3_scales,
        "w4": (n((H, N)) / np.sqrt(H) / u * amp[None, :]).astype(np.float32),
        "lo": (-amp * np.random.uniform(0.6, 1.4, N)).astype(np.float32),
        "hi": (amp * np.random.uniform(0.8, 1.8, N)).astype(np.float32),
    }

def reference(tab_words, tab_scales, tab2_words, tab2_scales, offs, offs2,
              w1_words, w1_scales, w2, w3_words, w3_scales, w4, lo, hi):
    v = unpack_weight(tab_words, tab_scales, "e4m3")[:, unstriped(offs)]
    v2 = unpack_weight(tab2_words, tab2_scales, "e2m1")[:, unstriped(offs2)]
    a = unpack_weight(w1_words, w1_scales, "e2m1").T @ v
    b = mxq(f64(w2), 0, "e4m3").T @ v
    wind = unpack_weight(w3_words, w3_scales, "e4m3").T @ v2
    act = 0.5 * b * (1.0 + np.tanh(0.7978845608028654 * (b + 0.044715 * b ** 3)))
    h = (a + act) * wind
    e = mxq(f64(w4), 0, "e4m3").T @ mxq(h, 0, "e4m3")
    y = np.minimum(np.maximum(e, f64(lo)[:, None]), f64(hi)[:, None])
    words, scales = planes(y)
    return y, words, scales

@@ -1,0 +1,307 @@
+from contextlib import ExitStack
+
+import concourse.mybir as mybir
+
+K, K2, H, N, T, S = 1024, 512, 512, 1024, 4096, 1024
+FLOPS = 2 * S * (2 * K * H + K2 * H + H * N)
+
+F32 = mybir.dt.float32
+BF16 = mybir.dt.bfloat16
+I32 = mybir.dt.int32
+U32 = mybir.dt.uint32
+U16 = mybir.dt.uint16
+U8 = mybir.dt.uint8
+FP8X4 = mybir.dt.float8_e4m3fn_x4
+FP4X4 = mybir.dt.float4_e2m1fn_x4
+ALU = mybir.AluOpType
+GELU = mybir.ActivationFunctionType.Gelu_apprx_tanh
+
+P = 128
+PACK = 4
+QUADS = 4
+CHUNK = 128
+BANK = 512
+BLOCKS = ((0, 512), (512, 256), (768, 256))
+
+
+def tile_list_wildfire_cell_tasking_kernel(
+    tc, tab_words, tab_scales, tab2_words, tab2_scales, offs, offs2,
+    w1_words, w1_scales, w2, w3_words, w3_scales, w4, lo, hi, out_0, out_1, out_2,
+):
+    nc = tc.nc
+    with ExitStack() as ctx:
+        keep = ctx.enter_context(tc.tile_pool(name="keep", bufs=1))
+        ring = ctx.enter_context(tc.tile_pool(name="ring", bufs=3))
+        psum = ctx.enter_context(tc.psum_pool(name="psum", bufs=2))
+
+        def held(name, shape, dtype, tag=None):
+            return keep.tile(shape, dtype, name=name, tag=tag or name, align_bytes=64)
+
+        wind_sc_win = held("wind_sc_win", [P, T], U8, tag="shared_a")
+        fuel_sc_win = held("fuel_sc_win", [P, T], U8, tag="shared_b")
+        wsc_raw = held("wsc_raw", [P, 3, H], U8)
+        fuel_sc1 = held("fuel_sc1", [P, S], U8)
+        nc.vector.memset(wind_sc_win[:].bitcast(I32), 0)
+        nc.vector.memset(fuel_sc_win[:].bitcast(I32), 0)
+        nc.vector.memset(wsc_raw[:].rearrange("p a c -> p (a c)").bitcast(I32), 0)
+        nc.vector.memset(fuel_sc1[:].bitcast(I32), 0)
+
+        offs2_sb = keep.tile([P, S // 16], U16, name="offs2_sb")
+        offs_sb = keep.tile([P, S // 16], U16, name="offs_sb")
+        nc.sync.dma_start(offs2_sb[:], offs2)
+        nc.sync.dma_start(offs_sb[:], offs)
+        lo_sb = held("lo_sb", [P, 2, PACK], F32)
+        hi_sb = held("hi_sb", [P, 2, PACK], F32)
+        nc.sync.dma_start(lo_sb[:], lo.rearrange("(g p t) -> p g t", g=2, t=PACK))
+        nc.sync.dma_start(hi_sb[:], hi.rearrange("(g p t) -> p g t", g=2, t=PACK))
+        wind_win = held("wind_win", [P, T], U16, tag="shared_c")
+        nc.sync.dma_start(wind_win[:].bitcast(I32), tab2_words[0].bitcast(I32))
+        wraw = held("wraw", [P, 2 * H], I32, tag="shared_d")
+        nc.sync.dma_start(
+            wraw[:, 0:H].rearrange("p (a w) -> p a w", a=2),
+            w1_words.rearrange("a p n -> p a n").bitcast(I32),
+        )
+        nc.sync.dma_start(wraw[:, H : 2 * H], w3_words[0].rearrange("p c i -> p (c i)").bitcast(I32))
+        fuel_win0 = held("fuel_win0", [P, T], I32)
+        nc.sync.dma_start(fuel_win0[:], tab_words[0].rearrange("p t i -> p (t i)").bitcast(I32))
+        for q in range(QUADS):
+            nc.scalar.dma_start(
+                wind_sc_win[32 * q : 32 * q + 4, :].bitcast(I32),
+                tab2_scales[0, 4 * q : 4 * q + 4, :].bitcast(I32),
+            )
+        for q in range(QUADS):
+            nc.gpsimd.dma_start(
+                fuel_sc_win[32 * q : 32 * q + 8, :].bitcast(I32),
+                tab_scales[:, 4 * q : 4 * q + 4, :].bitcast(I32),
+            )
+        for q in range(QUADS):
+            nc.scalar.dma_start(
+                wsc_raw[32 * q : 32 * q + 4, 0:2, :].bitcast(I32),
+                w1_scales[:, 4 * q : 4 * q + 4, :].rearrange("a r c -> r a c").bitcast(I32),
+            )
+            nc.scalar.dma_start(
+                wsc_raw[32 * q : 32 * q + 4, 2, :].bitcast(I32),
+                w3_scales[0, 4 * q : 4 * q + 4, :].bitcast(I32),
+            )
+
+        wind_codes = held("wind_codes", [P, S], U16)
+        nc.vector.tensor_copy(wind_codes[:], wind_win[:].indirect(offs2_sb[:]))
+        w1_codes = held("w1_codes", [P, 2 * 2 * H], U8)
+        w3_codes = held("w3_codes", [P, H], I32)
+        nc.vector.tensor_copy(
+            w1_codes[:].bitcast(I32).rearrange("p (a t b h) -> p a t b h", a=2, t=PACK, h=4),
+            wraw[:, 0:H].rearrange("p (a b t h) -> p a t b h", a=2, t=PACK, h=4),
+        )
+        nc.vector.tensor_copy(
+            w3_codes[:].rearrange("p (t b i) -> p t b i", t=PACK, i=8),
+            wraw[:, H : 2 * H].rearrange("p (b t i) -> p t b i", t=PACK, i=8),
+        )
+        w2_raw = []
+        for a, tag in ((0, "shared_c"), (1, "shared_d")):
+            raw = held("w2_raw%d" % a, [P, PACK, H], F32, tag=tag)
+            nc.sync.dma_start(raw[:], w2[512 * a : 512 * (a + 1), :].rearrange("(p j) c -> p j c", j=PACK))
+            w2_raw.append(raw)
+        wind_sc = held("wind_sc", [P, S], U8)
+        nc.vector.tensor_copy(wind_sc[:], wind_sc_win[:].indirect(offs2_sb[:]))
+        fuel_win1 = held("fuel_win1", [P, T], I32, tag="shared_a")
+        nc.sync.dma_start(fuel_win1[:], tab_words[1].rearrange("p t i -> p (t i)").bitcast(I32))
+
+        fuel_sc0 = held("fuel_sc0", [P, S], U8)
+        nc.vector.tensor_copy(fuel_sc0[:], fuel_sc_win[:].indirect(offs_sb[:]))
+        nc.gpsimd.dma_start(fuel_sc1[0:100, :].bitcast(I32), fuel_sc0[4:104, :].bitcast(I32))
+        w4_raw = held("w4_raw", [P, PACK, N], F32, tag="shared_b")
+        w4_rows = w4.rearrange("(b j i) n -> j b i n", j=PACK, i=8)
+        for j in range(PACK):
+            nc.sync.dma_start(w4_raw[:, j, :], w4_rows[j])
+
+        fuel_codes0 = held("fuel_codes0", [P, S], U32)
+        fuel_codes1 = held("fuel_codes1", [P, S], U32)
+        nc.vector.tensor_copy(fuel_codes0[:], fuel_win0[:].bitcast(U32).indirect(offs_sb[:]))
+
+        wsc = held("wsc", [P, 3 * H], U8)
+        nc.vector.tensor_copy(
+            wsc[:].bitcast(I32).rearrange("p (a t b h) -> p a t b h", a=3, t=PACK, h=2),
+            wsc_raw[:].rearrange("p a c -> p (a c)").bitcast(I32).rearrange("p (a b t h) -> p a t b h", a=3, t=PACK, h=2),
+        )
+
+        w2_codes, w2_sc = [], []
+        for a in range(2):
+            rounded = held("w2_bf%d" % a, [P, PACK * H], BF16)
+            dst = rounded[:].rearrange("p (t b h l j) -> p t b h j l", t=PACK, h=2, l=4, j=PACK)
+            src = w2_raw[a][:].rearrange("p j (b t h l) -> p t b h j l", t=PACK, h=2, l=4)
+            for t in range(PACK):
+                nc.scalar.copy(dst[:, t], src[:, t])
+            codes = held("w2_codes%d" % a, [P, H], U32)
+            scales = held("w2_sc%d" % a, [P, H], U8)
+            nc.vector.quantize_mx(out=codes[:].bitcast(FP8X4), scales=scales[:], in_=rounded[:])
+            w2_codes.append(codes)
+            w2_sc.append(scales)
+
+        for half in range(2):
+            nc.vector.tensor_copy(
+                fuel_codes1[:, 512 * half : 512 * (half + 1)],
+                fuel_win1[:].bitcast(U32).indirect(offs_sb[:, 32 * half : 32 * (half + 1)]),
+            )
+        fuel_codes = (fuel_codes0, fuel_codes1)
+        fuel_sc = (fuel_sc0, fuel_sc1)
+
+        h_bf = [held("h_bf%d" % b, [P, PACK * w], BF16) for b, (c0, w) in enumerate(BLOCKS)]
+        h_codes = [held("h_codes%d" % b, [P, w], U32) for b, (c0, w) in enumerate(BLOCKS)]
+        h_sc = [held("h_sc%d" % b, [P, w], U8) for b, (c0, w) in enumerate(BLOCKS)]
+        w4_bf = [held("w4_bf%d" % g, [P, PACK * 512], BF16) for g in range(2)]
+        w4_codes = [held("w4_codes%d" % g, [P, 512], U32) for g in range(2)]
+        w4_sc = [held("w4_sc%d" % g, [P, 512], U8) for g in range(2)]
+        y_sc = held("y_sc", [P, 2, S], U8)
+        pending = {}
+        y_tiles = {}
+
+        def dealt(bank):
+            return bank[:].rearrange("p (t m) -> p m t", t=PACK)
+
+        def woven(ap):
+            return ap.rearrange("p (m t) -> p m t", t=PACK)
+
+        def fuel_sum(c):
+            cols = slice(CHUNK * c, CHUNK * (c + 1))
+            b_bank = psum.tile([P, BANK], F32, name="b_bank")
+            a_bank = psum.tile([P, BANK], F32, name="a_bank")
+            w_bank = psum.tile([P, BANK], F32, name="w_bank")
+            for t in range(PACK):
+                rows = slice(P * t, P * (t + 1))
+                for a in range(2):
+                    nc.tensor.matmul_mx(
+                        out=b_bank[:, rows], lhsT=w2_codes[a][:, rows].bitcast(FP8X4), lhsT_scale=w2_sc[a][:, rows],
+                        rhs=fuel_codes[a][:, cols].bitcast(FP8X4), rhs_scale=fuel_sc[a][:, cols],
+                        start=(a == 0), stop=(a == 1),
+                    )
+            act = ring.tile([P, BANK], F32, name="act")
+            nc.scalar.activation(out=woven(act[:]), in_=dealt(b_bank), func=GELU)
+            for t in range(PACK):
+                rows = slice(P * t, P * (t + 1))
+                for a in range(2):
+                    first = a * H + P * t
+                    nc.tensor.matmul_mx(
+                        out=a_bank[:, rows], lhsT=w1_codes[:, 2 * first : 2 * (first + P)].bitcast(FP4X4),
+                        lhsT_scale=wsc[:, first : first + P],
+                        rhs=fuel_codes[a][:, cols].bitcast(FP8X4), rhs_scale=fuel_sc[a][:, cols],
+                        start=(a == 0), stop=(a == 1),
+                    )
+            fuel = ring.tile([P, BANK], F32, name="fuel")
+            nc.vector.tensor_tensor(woven(fuel[:]), dealt(a_bank), woven(act[:]), ALU.add)
+            for t in range(PACK):
+                rows = slice(P * t, P * (t + 1))
+                nc.tensor.matmul_mx(
+                    out=w_bank[:, rows], lhsT=w3_codes[:, rows].bitcast(FP8X4),
+                    lhsT_scale=wsc[:, 2 * H + P * t : 2 * H + P * (t + 1)],
+                    rhs=wind_codes[:, cols].bitcast(FP4X4), rhs_scale=wind_sc[:, cols],
+                    start=True, stop=True,
+                )
+            pending[c] = (fuel, w_bank)
+
+        def meet_wind(c):
+            fuel, w_bank = pending[c]
+            b = max(i for i, (c0, w) in enumerate(BLOCKS) if c0 <= CHUNK * c)
+            first = PACK * (CHUNK * c - BLOCKS[b][0])
+            nc.vector.tensor_tensor(woven(h_bf[b][:, first : first + BANK]), dealt(w_bank), woven(fuel[:]), ALU.mult)
+
+        def quantise_h(b):
+            nc.vector.quantize_mx(out=h_codes[b][:].bitcast(FP8X4), scales=h_sc[b][:], in_=h_bf[b][:])
+
+        def round_w4(g, piece):
+            ms = slice(32 * piece, 32 * (piece + 1))
+            dst = w4_bf[g][:].rearrange("p (t m j) -> p m j t", t=PACK, j=PACK)
+            src = w4_raw[:, :, 512 * g : 512 * (g + 1)].rearrange("p j (m t) -> p m j t", t=PACK)
+            nc.scalar.copy(dst[:, ms], src[:, ms])
+
+        def quantise_w4(g):
+            nc.vector.quantize_mx(out=w4_codes[g][:].bitcast(FP8X4), scales=w4_sc[g][:], in_=w4_bf[g][:])
+
+        def task_rows(b, g, ts):
+            c0, w = BLOCKS[b]
+            if (b, g) not in y_tiles:
+                y_tiles[(b, g)] = held("y%d_%d" % (b, g), [P, PACK, w], F32)
+            y = y_tiles[(b, g)]
+            per_bank = BANK // w
+            for i in range(0, len(ts), per_bank):
+                e_bank = psum.tile([P, BANK], F32, name="e_bank")
+                for s, t in enumerate(ts[i : i + per_bank]):
+                    rows = slice(P * t, P * (t + 1))
+                    nc.tensor.matmul_mx(
+                        out=e_bank[:, w * s : w * (s + 1)], lhsT=w4_codes[g][:, rows].bitcast(FP8X4),
+                        lhsT_scale=w4_sc[g][:, rows], rhs=h_codes[b][:].bitcast(FP8X4), rhs_scale=h_sc[b][:],
+                        start=True, stop=True,
+                    )
+                for s, t in enumerate(ts[i : i + per_bank]):
+                    nc.vector.tensor_scalar(
+                        y[:, t, :], e_bank[:, w * s : w * (s + 1)],
+                        lo_sb[:, g, t : t + 1], hi_sb[:, g, t : t + 1], ALU.max, ALU.min,
+                    )
+
+        def weave_y(b, g, copy):
+            c0, w = BLOCKS[b]
+            y = y_tiles[(b, g)]
+            nc.sync.dma_start(
+                out_0[512 * g : 512 * (g + 1), c0 : c0 + w].rearrange("(p t) m -> p t m", t=PACK), y[:]
+            )
+            y_bf = held("y_bf%d_%d" % (b, g), [P, PACK * w], BF16)
+            copy(
+                y_bf[:].rearrange("p (m l t) -> p m t l", l=4, t=PACK),
+                y[:].rearrange("p t (m l) -> p m t l", l=4),
+            )
+            y_tiles[(b, g, "bf")] = y_bf
+
+        def quantise_y(b, g):
+            c0, w = BLOCKS[b]
+            y_codes = held("y_codes%d_%d" % (b, g), [P, w], U32)
+            nc.vector.quantize_mx(
+                out=y_codes[:].bitcast(FP8X4), scales=y_sc[:, g, c0 : c0 + w], in_=y_tiles[(b, g, "bf")][:]
+            )
+            nc.sync.dma_start(
+                out_1[g, :, c0 : c0 + w, :].rearrange("p m t -> p (m t)").bitcast(I32), y_codes[:].bitcast(I32)
+            )
+
+        for c in range(4):
+            fuel_sum(c)
+            if c > 0:
+                meet_wind(c - 1)
+            if c >= 2:
+                for piece in range(4):
+                    round_w4(c - 2, piece)
+                quantise_w4(c - 2)
+        fuel_sum(4)
+        meet_wind(3)
+        quantise_h(0)
+        fuel_sum(5)
+        meet_wind(4)
+        task_rows(0, 0, (0, 1))
+        fuel_sum(6)
+        meet_wind(5)
+        task_rows(0, 0, (2, 3))
+        weave_y(0, 0, nc.scalar.copy)
+        quantise_h(1)
+        fuel_sum(7)
+        meet_wind(6)
+        task_rows(0, 1, (0, 1))
+        meet_wind(7)
+        task_rows(0, 1, (2, 3))
+        weave_y(0, 1, nc.scalar.copy)
+        quantise_h(2)
+        quantise_y(0, 0)
+        task_rows(1, 0, (0, 1, 2, 3))
+        weave_y(1, 0, nc.scalar.copy)
+        task_rows(1, 1, (0, 1, 2, 3))
+        weave_y(1, 1, nc.scalar.copy)
+        quantise_y(0, 1)
+        task_rows(2, 0, (0, 1, 2, 3))
+        weave_y(2, 0, nc.scalar.copy)
+        quantise_y(1, 0)
+        task_rows(2, 1, (0, 1, 2, 3))
+        quantise_y(1, 1)
+        weave_y(2, 1, nc.vector.tensor_copy)
+        quantise_y(2, 0)
+        quantise_y(2, 1)
+        for q in range(QUADS):
+            nc.sync.dma_start(
+                out_2[:, 4 * q : 4 * q + 4, :].rearrange("g r m -> r g m").bitcast(I32),
+                y_sc[32 * q : 32 * q + 4, :, :].bitcast(I32),
+            )

@@ -43,8 +43,8 @@ def tile_list_wildfire_cell_tasking_kernel(
         fuel_sc1 = held("fuel_sc1", [P, S], U8)
         nc.vector.memset(wind_sc_win[:].bitcast(I32), 0)
         nc.vector.memset(fuel_sc_win[:].bitcast(I32), 0)
-        nc.vector.memset(wsc_raw[:].rearrange("p a c -> p (a c)").bitcast(I32), 0)
-        nc.vector.memset(fuel_sc1[:].bitcast(I32), 0)
+        nc.gpsimd.memset(wsc_raw[:].rearrange("p a c -> p (a c)").bitcast(I32), 0)
+        nc.gpsimd.memset(fuel_sc1[:].bitcast(I32), 0)
 
         offs2_sb = keep.tile([P, S // 16], U16, name="offs2_sb")
         offs_sb = keep.tile([P, S // 16], U16, name="offs_sb")
@@ -52,17 +52,16 @@ def tile_list_wildfire_cell_tasking_kernel(
         nc.sync.dma_start(offs_sb[:], offs)
         lo_sb = held("lo_sb", [P, 2, PACK], F32)
         hi_sb = held("hi_sb", [P, 2, PACK], F32)
-        nc.sync.dma_start(lo_sb[:], lo.rearrange("(g p t) -> p g t", g=2, t=PACK))
-        nc.sync.dma_start(hi_sb[:], hi.rearrange("(g p t) -> p g t", g=2, t=PACK))
         wind_win = held("wind_win", [P, T], U16, tag="shared_c")
         nc.sync.dma_start(wind_win[:].bitcast(I32), tab2_words[0].bitcast(I32))
-        wraw = held("wraw", [P, 2 * H], I32, tag="shared_d")
+        w1_raw = held("w1_raw", [P, H], I32, tag="shared_d")
+        w3_raw = held("w3_raw", [P, H], I32, tag="shared_e")
         nc.sync.dma_start(
-            wraw[:, 0:H].rearrange("p (a w) -> p a w", a=2),
+            w1_raw[:].rearrange("p (a w) -> p a w", a=2),
             w1_words.rearrange("a p n -> p a n").bitcast(I32),
         )
-        nc.sync.dma_start(wraw[:, H : 2 * H], w3_words[0].rearrange("p c i -> p (c i)").bitcast(I32))
-        fuel_win0 = held("fuel_win0", [P, T], I32)
+        nc.sync.dma_start(w3_raw[:], w3_words[0].rearrange("p c i -> p (c i)").bitcast(I32))
+        fuel_win0 = held("fuel_win0", [P, T], I32, tag="shared_f")
         nc.sync.dma_start(fuel_win0[:], tab_words[0].rearrange("p t i -> p (t i)").bitcast(I32))
         for q in range(QUADS):
             nc.scalar.dma_start(
@@ -70,19 +69,22 @@ def tile_list_wildfire_cell_tasking_kernel(
                 tab2_scales[0, 4 * q : 4 * q + 4, :].bitcast(I32),
             )
         for q in range(QUADS):
-            nc.gpsimd.dma_start(
+            nc.scalar.dma_start(
                 fuel_sc_win[32 * q : 32 * q + 8, :].bitcast(I32),
                 tab_scales[:, 4 * q : 4 * q + 4, :].bitcast(I32),
             )
         for q in range(QUADS):
-            nc.scalar.dma_start(
+            nc.gpsimd.dma_start(
                 wsc_raw[32 * q : 32 * q + 4, 0:2, :].bitcast(I32),
                 w1_scales[:, 4 * q : 4 * q + 4, :].rearrange("a r c -> r a c").bitcast(I32),
             )
-            nc.scalar.dma_start(
+            nc.gpsimd.dma_start(
                 wsc_raw[32 * q : 32 * q + 4, 2, :].bitcast(I32),
                 w3_scales[0, 4 * q : 4 * q + 4, :].bitcast(I32),
             )
+
+        nc.gpsimd.dma_start(lo_sb[:], lo.rearrange("(g p t) -> p g t", g=2, t=PACK))
+        nc.gpsimd.dma_start(hi_sb[:], hi.rearrange("(g p t) -> p g t", g=2, t=PACK))
 
         wind_codes = held("wind_codes", [P, S], U16)
         nc.vector.tensor_copy(wind_codes[:], wind_win[:].indirect(offs2_sb[:]))
@@ -90,35 +92,30 @@ def tile_list_wildfire_cell_tasking_kernel(
         w3_codes = held("w3_codes", [P, H], I32)
         nc.vector.tensor_copy(
             w1_codes[:].bitcast(I32).rearrange("p (a t b h) -> p a t b h", a=2, t=PACK, h=4),
-            wraw[:, 0:H].rearrange("p (a b t h) -> p a t b h", a=2, t=PACK, h=4),
+            w1_raw[:].rearrange("p (a b t h) -> p a t b h", a=2, t=PACK, h=4),
         )
         nc.vector.tensor_copy(
             w3_codes[:].rearrange("p (t b i) -> p t b i", t=PACK, i=8),
-            wraw[:, H : 2 * H].rearrange("p (b t i) -> p t b i", t=PACK, i=8),
+            w3_raw[:].rearrange("p (b t i) -> p t b i", t=PACK, i=8),
         )
         w2_raw = []
         for a, tag in ((0, "shared_c"), (1, "shared_d")):
             raw = held("w2_raw%d" % a, [P, PACK, H], F32, tag=tag)
             nc.sync.dma_start(raw[:], w2[512 * a : 512 * (a + 1), :].rearrange("(p j) c -> p j c", j=PACK))
             w2_raw.append(raw)
-        wind_sc = held("wind_sc", [P, S], U8)
+        wind_sc = held("wind_sc", [P, S], U8, tag="shared_e")
         nc.vector.tensor_copy(wind_sc[:], wind_sc_win[:].indirect(offs2_sb[:]))
         fuel_win1 = held("fuel_win1", [P, T], I32, tag="shared_a")
         nc.sync.dma_start(fuel_win1[:], tab_words[1].rearrange("p t i -> p (t i)").bitcast(I32))
 
-        fuel_sc0 = held("fuel_sc0", [P, S], U8)
-        nc.vector.tensor_copy(fuel_sc0[:], fuel_sc_win[:].indirect(offs_sb[:]))
-        nc.gpsimd.dma_start(fuel_sc1[0:100, :].bitcast(I32), fuel_sc0[4:104, :].bitcast(I32))
-        w4_raw = held("w4_raw", [P, PACK, N], F32, tag="shared_b")
-        w4_rows = w4.rearrange("(b j i) n -> j b i n", j=PACK, i=8)
-        for j in range(PACK):
-            nc.sync.dma_start(w4_raw[:, j, :], w4_rows[j])
-
         fuel_codes0 = held("fuel_codes0", [P, S], U32)
         fuel_codes1 = held("fuel_codes1", [P, S], U32)
         nc.vector.tensor_copy(fuel_codes0[:], fuel_win0[:].bitcast(U32).indirect(offs_sb[:]))
+        fuel_sc0 = held("fuel_sc0", [P, S], U8, tag="shared_f")
+        nc.vector.tensor_copy(fuel_sc0[:], fuel_sc_win[:].indirect(offs_sb[:]))
+        nc.sync.dma_start(fuel_sc1[0:100, :].bitcast(I32), fuel_sc0[4:104, :].bitcast(I32))
 
-        wsc = held("wsc", [P, 3 * H], U8)
+        wsc = held("wsc", [P, 3 * H], U8, tag="shared_b")
         nc.vector.tensor_copy(
             wsc[:].bitcast(I32).rearrange("p (a t b h) -> p a t b h", a=3, t=PACK, h=2),
             wsc_raw[:].rearrange("p a c -> p (a c)").bitcast(I32).rearrange("p (a b t h) -> p a t b h", a=3, t=PACK, h=2),
@@ -127,8 +124,8 @@ def tile_list_wildfire_cell_tasking_kernel(
         w2_codes, w2_sc = [], []
         for a in range(2):
             rounded = held("w2_bf%d" % a, [P, PACK * H], BF16)
-            dst = rounded[:].rearrange("p (t b h l j) -> p t b h j l", t=PACK, h=2, l=4, j=PACK)
-            src = w2_raw[a][:].rearrange("p j (b t h l) -> p t b h j l", t=PACK, h=2, l=4)
+            dst = rounded[:].rearrange("p (t b h l j) -> p t b h j l", t=PACK, h=4, l=2, j=PACK)
+            src = w2_raw[a][:].rearrange("p j (b t h l) -> p t b h j l", t=PACK, h=4, l=2)
             for t in range(PACK):
                 nc.scalar.copy(dst[:, t], src[:, t])
             codes = held("w2_codes%d" % a, [P, H], U32)
@@ -136,6 +133,12 @@ def tile_list_wildfire_cell_tasking_kernel(
             nc.vector.quantize_mx(out=codes[:].bitcast(FP8X4), scales=scales[:], in_=rounded[:])
             w2_codes.append(codes)
             w2_sc.append(scales)
+
+        w4_rows = w4.rearrange("(b j i) n -> j b i n", j=PACK, i=8)
+        w4_raw = held("w4_raw", [P, 2, PACK, 512], F32, tag="wsc_raw")
+        for g in range(2):
+            for j in range(PACK):
+                nc.sync.dma_start(w4_raw[:, g, j, :], w4_rows[j, :, :, 512 * g : 512 * (g + 1)])
 
         for half in range(2):
             nc.vector.tensor_copy(
@@ -148,46 +151,42 @@ def tile_list_wildfire_cell_tasking_kernel(
         h_bf = [held("h_bf%d" % b, [P, PACK * w], BF16) for b, (c0, w) in enumerate(BLOCKS)]
         h_codes = [held("h_codes%d" % b, [P, w], U32) for b, (c0, w) in enumerate(BLOCKS)]
         h_sc = [held("h_sc%d" % b, [P, w], U8) for b, (c0, w) in enumerate(BLOCKS)]
-        w4_bf = [held("w4_bf%d" % g, [P, PACK * 512], BF16) for g in range(2)]
+        w4_bf = {}
         w4_codes = [held("w4_codes%d" % g, [P, 512], U32) for g in range(2)]
         w4_sc = [held("w4_sc%d" % g, [P, 512], U8) for g in range(2)]
         y_sc = held("y_sc", [P, 2, S], U8)
-        pending = {}
+        fuel = [held("fuel%d" % half, [P, PACK, BANK], F32) for half in range(2)]
         y_tiles = {}
 
-        def dealt(bank):
-            return bank[:].rearrange("p (t m) -> p m t", t=PACK)
-
-        def woven(ap):
-            return ap.rearrange("p (m t) -> p m t", t=PACK)
-
-        def fuel_sum(c):
-            cols = slice(CHUNK * c, CHUNK * (c + 1))
+        def fuel_sum(half, t):
+            cols = slice(BANK * half, BANK * (half + 1))
+            rows = slice(P * t, P * (t + 1))
             b_bank = psum.tile([P, BANK], F32, name="b_bank")
             a_bank = psum.tile([P, BANK], F32, name="a_bank")
+            for a in range(2):
+                nc.tensor.matmul_mx(
+                    out=b_bank[:], lhsT=w2_codes[a][:, rows].bitcast(FP8X4), lhsT_scale=w2_sc[a][:, rows],
+                    rhs=fuel_codes[a][:, cols].bitcast(FP8X4), rhs_scale=fuel_sc0[4 * a : P, cols],
+                    start=(a == 0), stop=(a == 1),
+                )
+            if half == 0 and t % 2 == 1:
+                act = held("act%d" % t, [P, BANK], F32, tag="w4_bf%d" % (t // 2))
+            else:
+                act = ring.tile([P, BANK], F32, name="act")
+            nc.scalar.activation(out=act[:], in_=b_bank[:], func=GELU)
+            for a in range(2):
+                first = a * H + P * t
+                nc.tensor.matmul_mx(
+                    out=a_bank[:], lhsT=w1_codes[:, 2 * first : 2 * (first + P)].bitcast(FP4X4),
+                    lhsT_scale=wsc[:, first : first + P],
+                    rhs=fuel_codes[a][:, cols].bitcast(FP8X4), rhs_scale=fuel_sc[a][:, cols],
+                    start=(a == 0), stop=(a == 1),
+                )
+            nc.vector.tensor_tensor(fuel[half][:, t, :], a_bank[:], act[:], ALU.add)
+
+        def meet_wind(c):
+            cols = slice(CHUNK * c, CHUNK * (c + 1))
             w_bank = psum.tile([P, BANK], F32, name="w_bank")
-            for t in range(PACK):
-                rows = slice(P * t, P * (t + 1))
-                for a in range(2):
-                    nc.tensor.matmul_mx(
-                        out=b_bank[:, rows], lhsT=w2_codes[a][:, rows].bitcast(FP8X4), lhsT_scale=w2_sc[a][:, rows],
-                        rhs=fuel_codes[a][:, cols].bitcast(FP8X4), rhs_scale=fuel_sc[a][:, cols],
-                        start=(a == 0), stop=(a == 1),
-                    )
-            act = ring.tile([P, BANK], F32, name="act")
-            nc.scalar.activation(out=woven(act[:]), in_=dealt(b_bank), func=GELU)
-            for t in range(PACK):
-                rows = slice(P * t, P * (t + 1))
-                for a in range(2):
-                    first = a * H + P * t
-                    nc.tensor.matmul_mx(
-                        out=a_bank[:, rows], lhsT=w1_codes[:, 2 * first : 2 * (first + P)].bitcast(FP4X4),
-                        lhsT_scale=wsc[:, first : first + P],
-                        rhs=fuel_codes[a][:, cols].bitcast(FP8X4), rhs_scale=fuel_sc[a][:, cols],
-                        start=(a == 0), stop=(a == 1),
-                    )
-            fuel = ring.tile([P, BANK], F32, name="fuel")
-            nc.vector.tensor_tensor(woven(fuel[:]), dealt(a_bank), woven(act[:]), ALU.add)
             for t in range(PACK):
                 rows = slice(P * t, P * (t + 1))
                 nc.tensor.matmul_mx(
@@ -196,21 +195,25 @@ def tile_list_wildfire_cell_tasking_kernel(
                     rhs=wind_codes[:, cols].bitcast(FP4X4), rhs_scale=wind_sc[:, cols],
                     start=True, stop=True,
                 )
-            pending[c] = (fuel, w_bank)
-
-        def meet_wind(c):
-            fuel, w_bank = pending[c]
             b = max(i for i, (c0, w) in enumerate(BLOCKS) if c0 <= CHUNK * c)
             first = PACK * (CHUNK * c - BLOCKS[b][0])
-            nc.vector.tensor_tensor(woven(h_bf[b][:, first : first + BANK]), dealt(w_bank), woven(fuel[:]), ALU.mult)
+            half, part = divmod(c, PACK)
+            nc.vector.tensor_tensor(
+                h_bf[b][:, first : first + BANK].rearrange("p (m l t) -> p m t l", l=2, t=PACK),
+                w_bank[:].rearrange("p (t m l) -> p m t l", l=2, t=PACK),
+                fuel[half][:, :, CHUNK * part : CHUNK * (part + 1)].rearrange("p t (m l) -> p m t l", l=2),
+                ALU.mult,
+            )
 
         def quantise_h(b):
             nc.vector.quantize_mx(out=h_codes[b][:].bitcast(FP8X4), scales=h_sc[b][:], in_=h_bf[b][:])
 
         def round_w4(g, piece):
             ms = slice(32 * piece, 32 * (piece + 1))
+            if piece == 0:
+                w4_bf[g] = held("w4_bf%d" % g, [P, PACK * 512], BF16)
             dst = w4_bf[g][:].rearrange("p (t m j) -> p m j t", t=PACK, j=PACK)
-            src = w4_raw[:, :, 512 * g : 512 * (g + 1)].rearrange("p j (m t) -> p m j t", t=PACK)
+            src = w4_raw[:, g].rearrange("p j (m t) -> p m j t", t=PACK)
             nc.scalar.copy(dst[:, ms], src[:, ms])
 
         def quantise_w4(g):
@@ -245,8 +248,8 @@ def tile_list_wildfire_cell_tasking_kernel(
             )
             y_bf = held("y_bf%d_%d" % (b, g), [P, PACK * w], BF16)
             copy(
-                y_bf[:].rearrange("p (m l t) -> p m t l", l=4, t=PACK),
-                y[:].rearrange("p t (m l) -> p m t l", l=4),
+                y_bf[:].rearrange("p (m l t) -> p m t l", l=2, t=PACK),
+                y[:].rearrange("p t (m l) -> p m t l", l=2),
             )
             y_tiles[(b, g, "bf")] = y_bf
 
@@ -260,33 +263,42 @@ def tile_list_wildfire_cell_tasking_kernel(
                 out_1[g, :, c0 : c0 + w, :].rearrange("p m t -> p (m t)").bitcast(I32), y_codes[:].bitcast(I32)
             )
 
-        for c in range(4):
-            fuel_sum(c)
-            if c > 0:
-                meet_wind(c - 1)
-            if c >= 2:
-                for piece in range(4):
-                    round_w4(c - 2, piece)
-                quantise_w4(c - 2)
-        fuel_sum(4)
+        fuel_sum(0, 0)
+        fuel_sum(0, 1)
+        fuel_sum(0, 2)
+        round_w4(0, 0)
+        round_w4(0, 1)
+        fuel_sum(0, 3)
+        round_w4(0, 2)
+        round_w4(0, 3)
+        meet_wind(0)
+        meet_wind(1)
+        fuel_sum(1, 0)
+        round_w4(1, 0)
+        round_w4(1, 1)
+        meet_wind(2)
         meet_wind(3)
+        quantise_w4(0)
         quantise_h(0)
-        fuel_sum(5)
-        meet_wind(4)
+        fuel_sum(1, 1)
+        round_w4(1, 2)
+        round_w4(1, 3)
         task_rows(0, 0, (0, 1))
-        fuel_sum(6)
-        meet_wind(5)
+        fuel_sum(1, 2)
         task_rows(0, 0, (2, 3))
         weave_y(0, 0, nc.scalar.copy)
-        quantise_h(1)
-        fuel_sum(7)
-        meet_wind(6)
+        fuel_sum(1, 3)
+        quantise_w4(1)
         task_rows(0, 1, (0, 1))
-        meet_wind(7)
+        meet_wind(4)
+        meet_wind(5)
         task_rows(0, 1, (2, 3))
         weave_y(0, 1, nc.scalar.copy)
-        quantise_h(2)
+        quantise_h(1)
+        meet_wind(6)
+        meet_wind(7)
         quantise_y(0, 0)
+        quantise_h(2)
         task_rows(1, 0, (0, 1, 2, 3))
         weave_y(1, 0, nc.scalar.copy)
         task_rows(1, 1, (0, 1, 2, 3))

@@ -44,14 +44,12 @@ def tile_list_wildfire_cell_tasking_kernel(
         nc.vector.memset(wind_sc_win[:].bitcast(I32), 0)
         nc.vector.memset(fuel_sc_win[:].bitcast(I32), 0)
         nc.gpsimd.memset(wsc_raw[:].rearrange("p a c -> p (a c)").bitcast(I32), 0)
-        nc.gpsimd.memset(fuel_sc1[:].bitcast(I32), 0)
+        nc.vector.memset(fuel_sc1[:].bitcast(I32), 0)
 
         offs2_sb = keep.tile([P, S // 16], U16, name="offs2_sb")
         offs_sb = keep.tile([P, S // 16], U16, name="offs_sb")
         nc.sync.dma_start(offs2_sb[:], offs2)
         nc.sync.dma_start(offs_sb[:], offs)
-        lo_sb = held("lo_sb", [P, 2, PACK], F32)
-        hi_sb = held("hi_sb", [P, 2, PACK], F32)
         wind_win = held("wind_win", [P, T], U16, tag="shared_c")
         nc.sync.dma_start(wind_win[:].bitcast(I32), tab2_words[0].bitcast(I32))
         w1_raw = held("w1_raw", [P, H], I32, tag="shared_d")
@@ -83,8 +81,6 @@ def tile_list_wildfire_cell_tasking_kernel(
                 w3_scales[0, 4 * q : 4 * q + 4, :].bitcast(I32),
             )
 
-        nc.gpsimd.dma_start(lo_sb[:], lo.rearrange("(g p t) -> p g t", g=2, t=PACK))
-        nc.gpsimd.dma_start(hi_sb[:], hi.rearrange("(g p t) -> p g t", g=2, t=PACK))
 
         wind_codes = held("wind_codes", [P, S], U16)
         nc.vector.tensor_copy(wind_codes[:], wind_win[:].indirect(offs2_sb[:]))
@@ -139,6 +135,11 @@ def tile_list_wildfire_cell_tasking_kernel(
         for g in range(2):
             for j in range(PACK):
                 nc.sync.dma_start(w4_raw[:, g, j, :], w4_rows[j, :, :, 512 * g : 512 * (g + 1)])
+
+        lo_sb = held("lo_sb", [P, 2, PACK], F32, tag="shared_c")
+        hi_sb = held("hi_sb", [P, 2, PACK], F32, tag="shared_d")
+        nc.sync.dma_start(lo_sb[:], lo.rearrange("(g p t) -> p g t", g=2, t=PACK))
+        nc.sync.dma_start(hi_sb[:], hi.rearrange("(g p t) -> p g t", g=2, t=PACK))
 
         for half in range(2):
             nc.vector.tensor_copy(
@@ -239,13 +240,13 @@ def tile_list_wildfire_cell_tasking_kernel(
                         y[:, t, :], e_bank[:, w * s : w * (s + 1)],
                         lo_sb[:, g, t : t + 1], hi_sb[:, g, t : t + 1], ALU.max, ALU.min,
                     )
+            rows_out = out_0[512 * g : 512 * (g + 1), c0 : c0 + w].rearrange("(p t) m -> p t m", t=PACK)
+            for t in ts[::2]:
+                nc.sync.dma_start(rows_out[:, t : t + 2, :], y[:, t : t + 2, :])
 
         def weave_y(b, g, copy):
             c0, w = BLOCKS[b]
             y = y_tiles[(b, g)]
-            nc.sync.dma_start(
-                out_0[512 * g : 512 * (g + 1), c0 : c0 + w].rearrange("(p t) m -> p t m", t=PACK), y[:]
-            )
             y_bf = held("y_bf%d_%d" % (b, g), [P, PACK * w], BF16)
             copy(
                 y_bf[:].rearrange("p (m l t) -> p m t l", l=2, t=PACK),

@@ -18,9 +18,14 @@ GELU = mybir.ActivationFunctionType.Gelu_apprx_tanh
 
 P = 128
 PACK = 4
-QUADS = 4
-CHUNK = 128
+PASS = P * PACK
+QUAD = 32
 BANK = 512
+CHUNK = BANK // PACK
+W4_PIECE = 32
+
+COL_W3, COL_FUEL, COL_W1, COL_WIND, COL_END = 0, H, H + S, 2 * H + S, 2 * H + 2 * S
+
 BLOCKS = ((0, 512), (512, 256), (768, 256))
 
 
@@ -32,289 +37,279 @@ def tile_list_wildfire_cell_tasking_kernel(
     with ExitStack() as ctx:
         keep = ctx.enter_context(tc.tile_pool(name="keep", bufs=1))
         ring = ctx.enter_context(tc.tile_pool(name="ring", bufs=3))
-        psum = ctx.enter_context(tc.psum_pool(name="psum", bufs=2))
+        psum = ctx.enter_context(tc.psum_pool(name="psum", bufs=8))
 
         def held(name, shape, dtype, tag=None):
             return keep.tile(shape, dtype, name=name, tag=tag or name, align_bytes=64)
 
-        wind_sc_win = held("wind_sc_win", [P, T], U8, tag="shared_a")
-        fuel_sc_win = held("fuel_sc_win", [P, T], U8, tag="shared_b")
-        wsc_raw = held("wsc_raw", [P, 3, H], U8)
-        fuel_sc1 = held("fuel_sc1", [P, S], U8)
-        nc.vector.memset(wind_sc_win[:].bitcast(I32), 0)
+        wsc_raw = held("wsc_raw", [P, 2, H], U8)
+        fuel_sc_win = held("fuel_sc_win", [P, T], U8)
+        wind_sc_win = held("wind_sc_win", [P, T], U8, tag="wind_scales_then_codes")
+        planes = [held("planes0", [P, COL_WIND], U8), held("planes1", [P, COL_END], U8)]
+        nc.vector.memset(wsc_raw[:].rearrange("p a c -> p (a c)").bitcast(I32), 0)
         nc.vector.memset(fuel_sc_win[:].bitcast(I32), 0)
-        nc.gpsimd.memset(wsc_raw[:].rearrange("p a c -> p (a c)").bitcast(I32), 0)
-        nc.vector.memset(fuel_sc1[:].bitcast(I32), 0)
+        nc.vector.memset(wind_sc_win[:].bitcast(I32), 0)
+        nc.vector.memset(planes[0][:].bitcast(I32), 0)
+        nc.vector.memset(planes[1][:, COL_FUEL:].bitcast(I32), 0)
 
         offs2_sb = keep.tile([P, S // 16], U16, name="offs2_sb")
         offs_sb = keep.tile([P, S // 16], U16, name="offs_sb")
-        nc.sync.dma_start(offs2_sb[:], offs2)
-        nc.sync.dma_start(offs_sb[:], offs)
-        wind_win = held("wind_win", [P, T], U16, tag="shared_c")
-        nc.sync.dma_start(wind_win[:].bitcast(I32), tab2_words[0].bitcast(I32))
-        w1_raw = held("w1_raw", [P, H], I32, tag="shared_d")
-        w3_raw = held("w3_raw", [P, H], I32, tag="shared_e")
+        w1_raw = held("w1_raw", [P, H], I32, tag="w1_then_fuel0_then_w4")
+        w3_raw = held("w3_raw", [P, H], I32, tag="w3_then_w2_then_bounds")
         nc.sync.dma_start(
             w1_raw[:].rearrange("p (a w) -> p a w", a=2),
             w1_words.rearrange("a p n -> p a n").bitcast(I32),
         )
+        nc.sync.dma_start(offs2_sb[:], offs2)
+        nc.sync.dma_start(offs_sb[:], offs)
         nc.sync.dma_start(w3_raw[:], w3_words[0].rearrange("p c i -> p (c i)").bitcast(I32))
-        fuel_win0 = held("fuel_win0", [P, T], I32, tag="shared_f")
-        nc.sync.dma_start(fuel_win0[:], tab_words[0].rearrange("p t i -> p (t i)").bitcast(I32))
-        for q in range(QUADS):
-            nc.scalar.dma_start(
-                wind_sc_win[32 * q : 32 * q + 4, :].bitcast(I32),
-                tab2_scales[0, 4 * q : 4 * q + 4, :].bitcast(I32),
-            )
-        for q in range(QUADS):
-            nc.scalar.dma_start(
-                fuel_sc_win[32 * q : 32 * q + 8, :].bitcast(I32),
-                tab_scales[:, 4 * q : 4 * q + 4, :].bitcast(I32),
-            )
-        for q in range(QUADS):
-            nc.gpsimd.dma_start(
-                wsc_raw[32 * q : 32 * q + 4, 0:2, :].bitcast(I32),
-                w1_scales[:, 4 * q : 4 * q + 4, :].rearrange("a r c -> r a c").bitcast(I32),
-            )
-            nc.gpsimd.dma_start(
-                wsc_raw[32 * q : 32 * q + 4, 2, :].bitcast(I32),
-                w3_scales[0, 4 * q : 4 * q + 4, :].bitcast(I32),
-            )
+        wind_win = held("wind_win", [P, T], U16)
+        nc.sync.dma_start(wind_win[:].bitcast(I32), tab2_words[0].bitcast(I32))
 
+        nc.sync.dma_start(wsc_raw[0:64:4, 0, :].bitcast(I32), w3_scales[0].bitcast(I32))
+        nc.sync.dma_start(wsc_raw[0:P:4, 1, :].bitcast(I32), w1_scales.rearrange("a q c -> (a q) c").bitcast(I32))
+        nc.sync.dma_start(fuel_sc_win[0:P:4, :].bitcast(I32), tab_scales.rearrange("a q t -> (a q) t").bitcast(I32))
+        nc.sync.dma_start(wind_sc_win[64:P:4, :].bitcast(I32), tab2_scales[0].bitcast(I32))
 
-        wind_codes = held("wind_codes", [P, S], U16)
-        nc.vector.tensor_copy(wind_codes[:], wind_win[:].indirect(offs2_sb[:]))
         w1_codes = held("w1_codes", [P, 2 * 2 * H], U8)
         w3_codes = held("w3_codes", [P, H], I32)
         nc.vector.tensor_copy(
-            w1_codes[:].bitcast(I32).rearrange("p (a t b h) -> p a t b h", a=2, t=PACK, h=4),
-            w1_raw[:].rearrange("p (a b t h) -> p a t b h", a=2, t=PACK, h=4),
+            w1_codes[:].bitcast(I32).rearrange("p (a t b e) -> p a t b e", a=2, t=PACK, e=4),
+            w1_raw[:].rearrange("p (a b t e) -> p a t b e", a=2, t=PACK, e=4),
         )
+        fuel_win0 = held("fuel_win0", [P, T], I32, tag="w1_then_fuel0_then_w4")
+        nc.sync.dma_start(fuel_win0[:], tab_words[0].rearrange("p t i -> p (t i)").bitcast(I32))
         nc.vector.tensor_copy(
-            w3_codes[:].rearrange("p (t b i) -> p t b i", t=PACK, i=8),
-            w3_raw[:].rearrange("p (b t i) -> p t b i", t=PACK, i=8),
+            w3_codes[:].rearrange("p (t b e) -> p t b e", t=PACK, e=8),
+            w3_raw[:].rearrange("p (b t e) -> p t b e", t=PACK, e=8),
         )
-        w2_raw = []
-        for a, tag in ((0, "shared_c"), (1, "shared_d")):
-            raw = held("w2_raw%d" % a, [P, PACK, H], F32, tag=tag)
-            nc.sync.dma_start(raw[:], w2[512 * a : 512 * (a + 1), :].rearrange("(p j) c -> p j c", j=PACK))
-            w2_raw.append(raw)
-        wind_sc = held("wind_sc", [P, S], U8, tag="shared_e")
-        nc.vector.tensor_copy(wind_sc[:], wind_sc_win[:].indirect(offs2_sb[:]))
-        fuel_win1 = held("fuel_win1", [P, T], I32, tag="shared_a")
+        w2_raw = held("w2_raw", [P, 2, PACK, H], F32, tag="w3_then_w2_then_bounds")
+        for a in (1, 0):
+            nc.sync.dma_start(w2_raw[:, a], w2[PASS * a : PASS * (a + 1), :].rearrange("(p j) c -> p j c", j=PACK))
+
+        spread = held("spread", [P, COL_END], U8)
+        for i, col in ((0, COL_W3), (1, COL_W1)):
+            nc.vector.tensor_copy(
+                spread[:, col : col + H].bitcast(I32).rearrange("p (t b e) -> p t b e", t=PACK, e=2),
+                wsc_raw[:, i, :].bitcast(I32).rearrange("p (b t e) -> p t b e", t=PACK, e=2),
+            )
+
+        def place_rows(a, first, end):
+            for i in range(4):
+                nc.sync.dma_start(
+                    planes[a][i:P:QUAD, first:end].bitcast(I32),
+                    spread[64 * a + 4 * i : 64 * (a + 1) : 16, first:end].bitcast(I32),
+                )
+
+        fuel_sc_rows = held("fuel_sc_rows", [P, S], U8)
+        nc.vector.tensor_copy(fuel_sc_rows[:], fuel_sc_win[:].indirect(offs_sb[:]))
+        nc.vector.tensor_copy(spread[:, COL_FUEL:COL_W1].bitcast(I32), fuel_sc_rows[:].bitcast(I32))
+        place_rows(0, COL_W3, COL_WIND)
+        wind_sc_rows = held("wind_sc_rows", [P, S], U8, tag="wind_rows_then_fuel1")
+        nc.vector.tensor_copy(wind_sc_rows[:], wind_sc_win[:].indirect(offs2_sb[:]))
+        nc.vector.tensor_copy(spread[:, COL_WIND:COL_END].bitcast(I32), wind_sc_rows[:].bitcast(I32))
+        fuel_win1 = held("fuel_win1", [P, T], I32, tag="wind_rows_then_fuel1")
         nc.sync.dma_start(fuel_win1[:], tab_words[1].rearrange("p t i -> p (t i)").bitcast(I32))
+        place_rows(1, COL_FUEL, COL_END)
+        fuel_sc = [planes[a][:, COL_FUEL:COL_W1] for a in range(2)]
+        w1_sc = [planes[a][:, COL_W1:COL_WIND] for a in range(2)]
+        w3_sc = planes[0][:, COL_W3:COL_FUEL]
+        wind_sc = planes[1][:, COL_WIND:COL_END]
 
-        fuel_codes0 = held("fuel_codes0", [P, S], U32)
-        fuel_codes1 = held("fuel_codes1", [P, S], U32)
-        nc.vector.tensor_copy(fuel_codes0[:], fuel_win0[:].bitcast(U32).indirect(offs_sb[:]))
-        fuel_sc0 = held("fuel_sc0", [P, S], U8, tag="shared_f")
-        nc.vector.tensor_copy(fuel_sc0[:], fuel_sc_win[:].indirect(offs_sb[:]))
-        nc.sync.dma_start(fuel_sc1[0:100, :].bitcast(I32), fuel_sc0[4:104, :].bitcast(I32))
+        wind_codes = held("wind_codes", [P, S], U16, tag="wind_scales_then_codes")
+        nc.vector.tensor_copy(wind_codes[:], wind_win[:].indirect(offs2_sb[:]))
+        fuel_codes = [held("fuel_codes%d" % a, [P, S], U32) for a in range(2)]
+        nc.vector.tensor_copy(fuel_codes[0][:], fuel_win0[:].bitcast(U32).indirect(offs_sb[:]))
 
-        wsc = held("wsc", [P, 3 * H], U8, tag="shared_b")
-        nc.vector.tensor_copy(
-            wsc[:].bitcast(I32).rearrange("p (a t b h) -> p a t b h", a=3, t=PACK, h=2),
-            wsc_raw[:].rearrange("p a c -> p (a c)").bitcast(I32).rearrange("p (a b t h) -> p a t b h", a=3, t=PACK, h=2),
-        )
-
-        w2_codes, w2_sc = [], []
-        for a in range(2):
-            rounded = held("w2_bf%d" % a, [P, PACK * H], BF16)
-            dst = rounded[:].rearrange("p (t b h l j) -> p t b h j l", t=PACK, h=4, l=2, j=PACK)
-            src = w2_raw[a][:].rearrange("p j (b t h l) -> p t b h j l", t=PACK, h=4, l=2)
+        w2_codes, w2_sc = {}, {}
+        for a in (1, 0):
+            w2_bf = held("w2_bf%d" % a, [P, PACK * H], BF16)
+            dst = w2_bf[:].rearrange("p (t b u l j) -> p t b u j l", t=PACK, u=4, l=2, j=PACK)
+            src = w2_raw[:, a].rearrange("p j (b t u l) -> p t b u j l", t=PACK, u=4, l=2)
             for t in range(PACK):
                 nc.scalar.copy(dst[:, t], src[:, t])
-            codes = held("w2_codes%d" % a, [P, H], U32)
-            scales = held("w2_sc%d" % a, [P, H], U8)
-            nc.vector.quantize_mx(out=codes[:].bitcast(FP8X4), scales=scales[:], in_=rounded[:])
-            w2_codes.append(codes)
-            w2_sc.append(scales)
+            w2_codes[a] = held("w2_codes%d" % a, [P, H], U32)
+            w2_sc[a] = held("w2_sc%d" % a, [P, H], U8)
+            nc.vector.quantize_mx(out=w2_codes[a][:].bitcast(FP8X4), scales=w2_sc[a][:], in_=w2_bf[:])
 
         w4_rows = w4.rearrange("(b j i) n -> j b i n", j=PACK, i=8)
-        w4_raw = held("w4_raw", [P, 2, PACK, 512], F32, tag="wsc_raw")
+        w4_raw = held("w4_raw", [P, 2, PACK, PASS], F32, tag="w1_then_fuel0_then_w4")
         for g in range(2):
             for j in range(PACK):
-                nc.sync.dma_start(w4_raw[:, g, j, :], w4_rows[j, :, :, 512 * g : 512 * (g + 1)])
-
-        lo_sb = held("lo_sb", [P, 2, PACK], F32, tag="shared_c")
-        hi_sb = held("hi_sb", [P, 2, PACK], F32, tag="shared_d")
-        nc.sync.dma_start(lo_sb[:], lo.rearrange("(g p t) -> p g t", g=2, t=PACK))
-        nc.sync.dma_start(hi_sb[:], hi.rearrange("(g p t) -> p g t", g=2, t=PACK))
+                nc.sync.dma_start(w4_raw[:, g, j, :], w4_rows[j, :, :, PASS * g : PASS * (g + 1)])
+        bounds = held("bounds", [P, 2, 2, PACK], F32, tag="w3_then_w2_then_bounds")
+        nc.sync.dma_start(bounds[:, 0], lo.rearrange("(g p t) -> p g t", g=2, t=PACK))
+        nc.sync.dma_start(bounds[:, 1], hi.rearrange("(g p t) -> p g t", g=2, t=PACK))
 
         for half in range(2):
             nc.vector.tensor_copy(
-                fuel_codes1[:, 512 * half : 512 * (half + 1)],
-                fuel_win1[:].bitcast(U32).indirect(offs_sb[:, 32 * half : 32 * (half + 1)]),
+                fuel_codes[1][:, BANK * half : BANK * (half + 1)],
+                fuel_win1[:].bitcast(U32).indirect(offs_sb[:, BANK // 16 * half : BANK // 16 * (half + 1)]),
             )
-        fuel_codes = (fuel_codes0, fuel_codes1)
-        fuel_sc = (fuel_sc0, fuel_sc1)
 
-        h_bf = [held("h_bf%d" % b, [P, PACK * w], BF16) for b, (c0, w) in enumerate(BLOCKS)]
-        h_codes = [held("h_codes%d" % b, [P, w], U32) for b, (c0, w) in enumerate(BLOCKS)]
-        h_sc = [held("h_sc%d" % b, [P, w], U8) for b, (c0, w) in enumerate(BLOCKS)]
-        w4_bf = {}
-        w4_codes = [held("w4_codes%d" % g, [P, 512], U32) for g in range(2)]
-        w4_sc = [held("w4_sc%d" % g, [P, 512], U8) for g in range(2)]
+        h_bf = [held("h_bf%d" % blk, [P, PACK * w], BF16) for blk, (c0, w) in enumerate(BLOCKS)]
+        h_codes = [held("h_codes%d" % blk, [P, w], U32) for blk, (c0, w) in enumerate(BLOCKS)]
+        h_sc = [held("h_sc%d" % blk, [P, w], U8) for blk, (c0, w) in enumerate(BLOCKS)]
+        w4_codes = [held("w4_codes%d" % g, [P, PASS], U32) for g in range(2)]
+        w4_sc = [held("w4_sc%d" % g, [P, PASS], U8) for g in range(2)]
         y_sc = held("y_sc", [P, 2, S], U8)
         fuel = [held("fuel%d" % half, [P, PACK, BANK], F32) for half in range(2)]
-        y_tiles = {}
+        w4_bf, y_f32, y_bf = {}, {}, {}
 
         def fuel_sum(half, t):
             cols = slice(BANK * half, BANK * (half + 1))
             rows = slice(P * t, P * (t + 1))
-            b_bank = psum.tile([P, BANK], F32, name="b_bank")
-            a_bank = psum.tile([P, BANK], F32, name="a_bank")
+            gelu_bank = psum.tile([P, BANK], F32, name="gelu_bank", tag="bank")
+            plain_bank = psum.tile([P, BANK], F32, name="plain_bank", tag="bank")
             for a in range(2):
                 nc.tensor.matmul_mx(
-                    out=b_bank[:], lhsT=w2_codes[a][:, rows].bitcast(FP8X4), lhsT_scale=w2_sc[a][:, rows],
-                    rhs=fuel_codes[a][:, cols].bitcast(FP8X4), rhs_scale=fuel_sc0[4 * a : P, cols],
+                    out=gelu_bank[:], lhsT=w2_codes[a][:, rows].bitcast(FP8X4), lhsT_scale=w2_sc[a][:, rows],
+                    rhs=fuel_codes[a][:, cols].bitcast(FP8X4), rhs_scale=fuel_sc[a][:, cols],
                     start=(a == 0), stop=(a == 1),
                 )
             if half == 0 and t % 2 == 1:
                 act = held("act%d" % t, [P, BANK], F32, tag="w4_bf%d" % (t // 2))
             else:
                 act = ring.tile([P, BANK], F32, name="act")
-            nc.scalar.activation(out=act[:], in_=b_bank[:], func=GELU)
+            nc.scalar.activation(out=act[:], in_=gelu_bank[:], func=GELU)
             for a in range(2):
                 first = a * H + P * t
                 nc.tensor.matmul_mx(
-                    out=a_bank[:], lhsT=w1_codes[:, 2 * first : 2 * (first + P)].bitcast(FP4X4),
-                    lhsT_scale=wsc[:, first : first + P],
+                    out=plain_bank[:], lhsT=w1_codes[:, 2 * first : 2 * (first + P)].bitcast(FP4X4),
+                    lhsT_scale=w1_sc[a][:, rows],
                     rhs=fuel_codes[a][:, cols].bitcast(FP8X4), rhs_scale=fuel_sc[a][:, cols],
                     start=(a == 0), stop=(a == 1),
                 )
-            nc.vector.tensor_tensor(fuel[half][:, t, :], a_bank[:], act[:], ALU.add)
+            nc.vector.tensor_tensor(fuel[half][:, t, :], plain_bank[:], act[:], ALU.add)
 
-        def meet_wind(c):
-            cols = slice(CHUNK * c, CHUNK * (c + 1))
-            w_bank = psum.tile([P, BANK], F32, name="w_bank")
+        def meet_wind(chunk):
+            cols = slice(CHUNK * chunk, CHUNK * (chunk + 1))
+            wind_bank = psum.tile([P, BANK], F32, name="wind_bank", tag="bank")
             for t in range(PACK):
                 rows = slice(P * t, P * (t + 1))
                 nc.tensor.matmul_mx(
-                    out=w_bank[:, rows], lhsT=w3_codes[:, rows].bitcast(FP8X4),
-                    lhsT_scale=wsc[:, 2 * H + P * t : 2 * H + P * (t + 1)],
+                    out=wind_bank[:, rows], lhsT=w3_codes[:, rows].bitcast(FP8X4), lhsT_scale=w3_sc[:, rows],
                     rhs=wind_codes[:, cols].bitcast(FP4X4), rhs_scale=wind_sc[:, cols],
                     start=True, stop=True,
                 )
-            b = max(i for i, (c0, w) in enumerate(BLOCKS) if c0 <= CHUNK * c)
-            first = PACK * (CHUNK * c - BLOCKS[b][0])
-            half, part = divmod(c, PACK)
+            blk = max(i for i, (c0, w) in enumerate(BLOCKS) if c0 <= CHUNK * chunk)
+            first = PACK * (CHUNK * chunk - BLOCKS[blk][0])
+            half, part = divmod(chunk, PACK)
             nc.vector.tensor_tensor(
-                h_bf[b][:, first : first + BANK].rearrange("p (m l t) -> p m t l", l=2, t=PACK),
-                w_bank[:].rearrange("p (t m l) -> p m t l", l=2, t=PACK),
+                h_bf[blk][:, first : first + BANK].rearrange("p (m l t) -> p m t l", l=2, t=PACK),
+                wind_bank[:].rearrange("p (t m l) -> p m t l", l=2, t=PACK),
                 fuel[half][:, :, CHUNK * part : CHUNK * (part + 1)].rearrange("p t (m l) -> p m t l", l=2),
                 ALU.mult,
             )
 
-        def quantise_h(b):
-            nc.vector.quantize_mx(out=h_codes[b][:].bitcast(FP8X4), scales=h_sc[b][:], in_=h_bf[b][:])
+        def quantise_h(blk):
+            nc.vector.quantize_mx(out=h_codes[blk][:].bitcast(FP8X4), scales=h_sc[blk][:], in_=h_bf[blk][:])
 
-        def round_w4(g, piece):
-            ms = slice(32 * piece, 32 * (piece + 1))
-            if piece == 0:
-                w4_bf[g] = held("w4_bf%d" % g, [P, PACK * 512], BF16)
+        def round_w4(g, pieces):
+            if g not in w4_bf:
+                w4_bf[g] = held("w4_bf%d" % g, [P, PACK * PASS], BF16)
             dst = w4_bf[g][:].rearrange("p (t m j) -> p m j t", t=PACK, j=PACK)
             src = w4_raw[:, g].rearrange("p j (m t) -> p m j t", t=PACK)
-            nc.scalar.copy(dst[:, ms], src[:, ms])
+            for piece in pieces:
+                ms = slice(W4_PIECE * piece, W4_PIECE * (piece + 1))
+                nc.scalar.copy(dst[:, ms], src[:, ms])
 
         def quantise_w4(g):
             nc.vector.quantize_mx(out=w4_codes[g][:].bitcast(FP8X4), scales=w4_sc[g][:], in_=w4_bf[g][:])
 
-        def task_rows(b, g, ts):
-            c0, w = BLOCKS[b]
-            if (b, g) not in y_tiles:
-                y_tiles[(b, g)] = held("y%d_%d" % (b, g), [P, PACK, w], F32)
-            y = y_tiles[(b, g)]
+        def task_rows(blk, g, ts):
+            c0, w = BLOCKS[blk]
+            if (blk, g) not in y_f32:
+                y_f32[(blk, g)] = held("y%d_%d" % (blk, g), [P, PACK, w], F32)
+            y = y_f32[(blk, g)]
             per_bank = BANK // w
             for i in range(0, len(ts), per_bank):
-                e_bank = psum.tile([P, BANK], F32, name="e_bank")
+                task_bank = psum.tile([P, BANK], F32, name="task_bank", tag="bank")
                 for s, t in enumerate(ts[i : i + per_bank]):
                     rows = slice(P * t, P * (t + 1))
                     nc.tensor.matmul_mx(
-                        out=e_bank[:, w * s : w * (s + 1)], lhsT=w4_codes[g][:, rows].bitcast(FP8X4),
-                        lhsT_scale=w4_sc[g][:, rows], rhs=h_codes[b][:].bitcast(FP8X4), rhs_scale=h_sc[b][:],
+                        out=task_bank[:, w * s : w * (s + 1)], lhsT=w4_codes[g][:, rows].bitcast(FP8X4),
+                        lhsT_scale=w4_sc[g][:, rows], rhs=h_codes[blk][:].bitcast(FP8X4), rhs_scale=h_sc[blk][:],
                         start=True, stop=True,
                     )
+                sums = task_bank
+                if blk == 0 and ts[i] < PACK - 1:
+                    sums = ring.tile([P, BANK], F32, name="sums")
+                    nc.scalar.copy(sums[:], task_bank[:])
                 for s, t in enumerate(ts[i : i + per_bank]):
                     nc.vector.tensor_scalar(
-                        y[:, t, :], e_bank[:, w * s : w * (s + 1)],
-                        lo_sb[:, g, t : t + 1], hi_sb[:, g, t : t + 1], ALU.max, ALU.min,
+                        y[:, t, :], sums[:, w * s : w * (s + 1)],
+                        bounds[:, 0, g, t : t + 1], bounds[:, 1, g, t : t + 1], ALU.max, ALU.min,
                     )
-            rows_out = out_0[512 * g : 512 * (g + 1), c0 : c0 + w].rearrange("(p t) m -> p t m", t=PACK)
-            for t in ts[::2]:
-                nc.sync.dma_start(rows_out[:, t : t + 2, :], y[:, t : t + 2, :])
+            rows_out = out_0[PASS * g : PASS * (g + 1), c0 : c0 + w].rearrange("(p t) m -> p t m", t=PACK)
+            nc.sync.dma_start(rows_out[:, ts[0] : ts[-1] + 1, :], y[:, ts[0] : ts[-1] + 1, :])
 
-        def weave_y(b, g, copy):
-            c0, w = BLOCKS[b]
-            y = y_tiles[(b, g)]
-            y_bf = held("y_bf%d_%d" % (b, g), [P, PACK * w], BF16)
-            copy(
-                y_bf[:].rearrange("p (m l t) -> p m t l", l=2, t=PACK),
-                y[:].rearrange("p t (m l) -> p m t l", l=2),
-            )
-            y_tiles[(b, g, "bf")] = y_bf
+        def round_y(blk, g, copy):
+            c0, w = BLOCKS[blk]
+            y_bf[(blk, g)] = held("y_bf%d_%d" % (blk, g), [P, PACK * w], BF16)
+            dst = y_bf[(blk, g)][:].rearrange("p (m l t) -> p m t l", l=2, t=PACK)
+            src = y_f32[(blk, g)][:].rearrange("p t (m l) -> p m t l", l=2)
+            for m0 in range(0, w // 2, P):
+                copy(dst[:, m0 : m0 + P], src[:, m0 : m0 + P])
 
-        def quantise_y(b, g):
-            c0, w = BLOCKS[b]
-            y_codes = held("y_codes%d_%d" % (b, g), [P, w], U32)
+        def quantise_y(blk, g):
+            c0, w = BLOCKS[blk]
+            y_codes = held("y_codes%d_%d" % (blk, g), [P, w], U32)
             nc.vector.quantize_mx(
-                out=y_codes[:].bitcast(FP8X4), scales=y_sc[:, g, c0 : c0 + w], in_=y_tiles[(b, g, "bf")][:]
+                out=y_codes[:].bitcast(FP8X4), scales=y_sc[:, g, c0 : c0 + w], in_=y_bf[(blk, g)][:]
             )
             nc.sync.dma_start(
                 out_1[g, :, c0 : c0 + w, :].rearrange("p m t -> p (m t)").bitcast(I32), y_codes[:].bitcast(I32)
             )
 
-        fuel_sum(0, 0)
-        fuel_sum(0, 1)
-        fuel_sum(0, 2)
-        round_w4(0, 0)
-        round_w4(0, 1)
+        for t in range(3):
+            fuel_sum(0, t)
+        round_w4(0, (0, 1))
         fuel_sum(0, 3)
-        round_w4(0, 2)
-        round_w4(0, 3)
+        round_w4(0, (2, 3))
         meet_wind(0)
         meet_wind(1)
         fuel_sum(1, 0)
-        round_w4(1, 0)
-        round_w4(1, 1)
+        round_w4(1, (0, 1))
         meet_wind(2)
         meet_wind(3)
         quantise_w4(0)
         quantise_h(0)
+
         fuel_sum(1, 1)
-        round_w4(1, 2)
-        round_w4(1, 3)
+        round_w4(1, (2, 3))
         task_rows(0, 0, (0, 1))
         fuel_sum(1, 2)
         task_rows(0, 0, (2, 3))
-        weave_y(0, 0, nc.scalar.copy)
+        round_y(0, 0, nc.scalar.copy)
         fuel_sum(1, 3)
         quantise_w4(1)
         task_rows(0, 1, (0, 1))
         meet_wind(4)
         meet_wind(5)
         task_rows(0, 1, (2, 3))
-        weave_y(0, 1, nc.scalar.copy)
+        round_y(0, 1, nc.scalar.copy)
         quantise_h(1)
         meet_wind(6)
         meet_wind(7)
         quantise_y(0, 0)
         quantise_h(2)
-        task_rows(1, 0, (0, 1, 2, 3))
-        weave_y(1, 0, nc.scalar.copy)
-        task_rows(1, 1, (0, 1, 2, 3))
-        weave_y(1, 1, nc.scalar.copy)
+
+        every_slice = tuple(range(PACK))
+        task_rows(1, 0, every_slice)
+        round_y(1, 0, nc.scalar.copy)
+        task_rows(1, 1, every_slice)
+        round_y(1, 1, nc.scalar.copy)
         quantise_y(0, 1)
-        task_rows(2, 0, (0, 1, 2, 3))
-        weave_y(2, 0, nc.scalar.copy)
+        task_rows(2, 0, every_slice)
+        round_y(2, 0, nc.scalar.copy)
         quantise_y(1, 0)
-        task_rows(2, 1, (0, 1, 2, 3))
+        task_rows(2, 1, every_slice)
         quantise_y(1, 1)
-        weave_y(2, 1, nc.vector.tensor_copy)
+        round_y(2, 1, nc.vector.tensor_copy)
         quantise_y(2, 0)
         quantise_y(2, 1)
-        for q in range(QUADS):
-            nc.sync.dma_start(
-                out_2[:, 4 * q : 4 * q + 4, :].rearrange("g r m -> r g m").bitcast(I32),
-                y_sc[32 * q : 32 * q + 4, :, :].bitcast(I32),
-            )
+
+        scale_rows = out_2.rearrange("g (q i) m -> i q g m", i=4)
+        for i in range(4):
+            nc.sync.dma_start(scale_rows[i].bitcast(I32), y_sc[i:P:QUAD, :, :].bitcast(I32))

@@ -26,6 +26,8 @@ W4_PIECE = 32
 
 COL_W3, COL_FUEL, COL_W1, COL_WIND, COL_END = 0, H, H + S, 2 * H + S, 2 * H + 2 * S
 
+W4_AFTER = ((0, 0), (0, 3))
+EMPTIED = ((0, 0, 0), (0, 0, 1), (0, 0, 2), (0, 1, 0), (0, 1, 1), (0, 1, 2))
 BLOCKS = ((0, 512), (512, 256), (768, 256))
 
 
@@ -44,10 +46,10 @@ def tile_list_wildfire_cell_tasking_kernel(
 
         wsc_raw = held("wsc_raw", [P, 2, H], U8)
         fuel_sc_win = held("fuel_sc_win", [P, T], U8)
-        wind_sc_win = held("wind_sc_win", [P, T], U8, tag="wind_scales_then_codes")
+        wind_sc_win = held("wind_sc_win", [P, T], U8)
         planes = [held("planes0", [P, COL_WIND], U8), held("planes1", [P, COL_END], U8)]
-        nc.vector.memset(wsc_raw[:].rearrange("p a c -> p (a c)").bitcast(I32), 0)
         nc.vector.memset(fuel_sc_win[:].bitcast(I32), 0)
+        nc.vector.memset(wsc_raw[:].rearrange("p a c -> p (a c)").bitcast(I32), 0)
         nc.vector.memset(wind_sc_win[:].bitcast(I32), 0)
         nc.vector.memset(planes[0][:].bitcast(I32), 0)
         nc.vector.memset(planes[1][:, COL_FUEL:].bitcast(I32), 0)
@@ -60,15 +62,15 @@ def tile_list_wildfire_cell_tasking_kernel(
             w1_raw[:].rearrange("p (a w) -> p a w", a=2),
             w1_words.rearrange("a p n -> p a n").bitcast(I32),
         )
-        nc.sync.dma_start(offs2_sb[:], offs2)
         nc.sync.dma_start(offs_sb[:], offs)
         nc.sync.dma_start(w3_raw[:], w3_words[0].rearrange("p c i -> p (c i)").bitcast(I32))
-        wind_win = held("wind_win", [P, T], U16)
-        nc.sync.dma_start(wind_win[:].bitcast(I32), tab2_words[0].bitcast(I32))
+        nc.sync.dma_start(offs2_sb[:], offs2)
+        w2_raw = {0: held("w2_raw0", [P, PACK, H], F32)}
+        nc.sync.dma_start(w2_raw[0][:], w2[:PASS, :].rearrange("(p j) c -> p j c", j=PACK))
 
+        nc.sync.dma_start(fuel_sc_win[0:P:4, :].bitcast(I32), tab_scales.rearrange("a q t -> (a q) t").bitcast(I32))
         nc.sync.dma_start(wsc_raw[0:64:4, 0, :].bitcast(I32), w3_scales[0].bitcast(I32))
         nc.sync.dma_start(wsc_raw[0:P:4, 1, :].bitcast(I32), w1_scales.rearrange("a q c -> (a q) c").bitcast(I32))
-        nc.sync.dma_start(fuel_sc_win[0:P:4, :].bitcast(I32), tab_scales.rearrange("a q t -> (a q) t").bitcast(I32))
         nc.sync.dma_start(wind_sc_win[64:P:4, :].bitcast(I32), tab2_scales[0].bitcast(I32))
 
         w1_codes = held("w1_codes", [P, 2 * 2 * H], U8)
@@ -83,9 +85,8 @@ def tile_list_wildfire_cell_tasking_kernel(
             w3_codes[:].rearrange("p (t b e) -> p t b e", t=PACK, e=8),
             w3_raw[:].rearrange("p (b t e) -> p t b e", t=PACK, e=8),
         )
-        w2_raw = held("w2_raw", [P, 2, PACK, H], F32, tag="w3_then_w2_then_bounds")
-        for a in (1, 0):
-            nc.sync.dma_start(w2_raw[:, a], w2[PASS * a : PASS * (a + 1), :].rearrange("(p j) c -> p j c", j=PACK))
+        w2_raw[1] = held("w2_raw1", [P, PACK, H], F32, tag="w3_then_w2_then_bounds")
+        nc.sync.dma_start(w2_raw[1][:], w2[PASS:, :].rearrange("(p j) c -> p j c", j=PACK))
 
         spread = held("spread", [P, COL_END], U8)
         for i, col in ((0, COL_W3), (1, COL_W1)):
@@ -101,31 +102,31 @@ def tile_list_wildfire_cell_tasking_kernel(
                     spread[64 * a + 4 * i : 64 * (a + 1) : 16, first:end].bitcast(I32),
                 )
 
-        fuel_sc_rows = held("fuel_sc_rows", [P, S], U8)
+        fuel_sc_rows = held("fuel_sc_rows", [P, S], U8, tag="fuel_rows_then_fuel1")
         nc.vector.tensor_copy(fuel_sc_rows[:], fuel_sc_win[:].indirect(offs_sb[:]))
         nc.vector.tensor_copy(spread[:, COL_FUEL:COL_W1].bitcast(I32), fuel_sc_rows[:].bitcast(I32))
         place_rows(0, COL_W3, COL_WIND)
-        wind_sc_rows = held("wind_sc_rows", [P, S], U8, tag="wind_rows_then_fuel1")
+        fuel_win1 = held("fuel_win1", [P, T], I32, tag="fuel_rows_then_fuel1")
+        nc.sync.dma_start(fuel_win1[:], tab_words[1].rearrange("p t i -> p (t i)").bitcast(I32))
+        wind_sc_rows = held("wind_sc_rows", [P, S], U8, tag="wind_rows_then_wind")
         nc.vector.tensor_copy(wind_sc_rows[:], wind_sc_win[:].indirect(offs2_sb[:]))
         nc.vector.tensor_copy(spread[:, COL_WIND:COL_END].bitcast(I32), wind_sc_rows[:].bitcast(I32))
-        fuel_win1 = held("fuel_win1", [P, T], I32, tag="wind_rows_then_fuel1")
-        nc.sync.dma_start(fuel_win1[:], tab_words[1].rearrange("p t i -> p (t i)").bitcast(I32))
         place_rows(1, COL_FUEL, COL_END)
+        wind_win = held("wind_win", [P, T], U16, tag="wind_rows_then_wind")
+        nc.sync.dma_start(wind_win[:].bitcast(I32), tab2_words[0].bitcast(I32))
         fuel_sc = [planes[a][:, COL_FUEL:COL_W1] for a in range(2)]
         w1_sc = [planes[a][:, COL_W1:COL_WIND] for a in range(2)]
         w3_sc = planes[0][:, COL_W3:COL_FUEL]
         wind_sc = planes[1][:, COL_WIND:COL_END]
 
-        wind_codes = held("wind_codes", [P, S], U16, tag="wind_scales_then_codes")
-        nc.vector.tensor_copy(wind_codes[:], wind_win[:].indirect(offs2_sb[:]))
-        fuel_codes = [held("fuel_codes%d" % a, [P, S], U32) for a in range(2)]
+        fuel_codes = {0: held("fuel_codes0", [P, S], U32)}
         nc.vector.tensor_copy(fuel_codes[0][:], fuel_win0[:].bitcast(U32).indirect(offs_sb[:]))
 
         w2_codes, w2_sc = {}, {}
-        for a in (1, 0):
+        for a in range(2):
             w2_bf = held("w2_bf%d" % a, [P, PACK * H], BF16)
             dst = w2_bf[:].rearrange("p (t b u l j) -> p t b u j l", t=PACK, u=4, l=2, j=PACK)
-            src = w2_raw[:, a].rearrange("p j (b t u l) -> p t b u j l", t=PACK, u=4, l=2)
+            src = w2_raw[a][:].rearrange("p j (b t u l) -> p t b u j l", t=PACK, u=4, l=2)
             for t in range(PACK):
                 nc.scalar.copy(dst[:, t], src[:, t])
             w2_codes[a] = held("w2_codes%d" % a, [P, H], U32)
@@ -141,6 +142,7 @@ def tile_list_wildfire_cell_tasking_kernel(
         nc.sync.dma_start(bounds[:, 0], lo.rearrange("(g p t) -> p g t", g=2, t=PACK))
         nc.sync.dma_start(bounds[:, 1], hi.rearrange("(g p t) -> p g t", g=2, t=PACK))
 
+        fuel_codes[1] = held("fuel_codes1", [P, S], U32, tag="w2_bf1")
         for half in range(2):
             nc.vector.tensor_copy(
                 fuel_codes[1][:, BANK * half : BANK * (half + 1)],
@@ -156,31 +158,47 @@ def tile_list_wildfire_cell_tasking_kernel(
         fuel = [held("fuel%d" % half, [P, PACK, BANK], F32) for half in range(2)]
         w4_bf, y_f32, y_bf = {}, {}, {}
 
-        def fuel_sum(half, t):
+        banks = {}
+
+        def fuel_pass(half, t, plain, a):
             cols = slice(BANK * half, BANK * (half + 1))
             rows = slice(P * t, P * (t + 1))
-            gelu_bank = psum.tile([P, BANK], F32, name="gelu_bank", tag="bank")
-            plain_bank = psum.tile([P, BANK], F32, name="plain_bank", tag="bank")
-            for a in range(2):
-                nc.tensor.matmul_mx(
-                    out=gelu_bank[:], lhsT=w2_codes[a][:, rows].bitcast(FP8X4), lhsT_scale=w2_sc[a][:, rows],
-                    rhs=fuel_codes[a][:, cols].bitcast(FP8X4), rhs_scale=fuel_sc[a][:, cols],
-                    start=(a == 0), stop=(a == 1),
-                )
-            if half == 0 and t % 2 == 1:
-                act = held("act%d" % t, [P, BANK], F32, tag="w4_bf%d" % (t // 2))
+            first = a * H + P * t
+            if a == 0:
+                banks[(half, t, plain)] = psum.tile([P, BANK], F32, name="fuel_bank", tag="bank")
+            if plain:
+                codes, scales = w1_codes[:, 2 * first : 2 * (first + P)].bitcast(FP4X4), w1_sc[a][:, rows]
+            else:
+                codes, scales = w2_codes[a][:, rows].bitcast(FP8X4), w2_sc[a][:, rows]
+            nc.tensor.matmul_mx(
+                out=banks[(half, t, plain)][:], lhsT=codes, lhsT_scale=scales,
+                rhs=fuel_codes[a][:, cols].bitcast(FP8X4), rhs_scale=fuel_sc[a][:, cols],
+                start=(a == 0), stop=(a == 1),
+            )
+
+        for t in range(PACK):
+            fuel_pass(0, t, False, 0)
+            fuel_pass(0, t, True, 0)
+
+        def fuel_sum(half, t):
+            for a in range(1 - half, 2):
+                fuel_pass(half, t, False, a)
+            if (half, t) in W4_AFTER:
+                act = held("act%d_%d" % (half, t), [P, BANK], F32, tag="w4_bf%d" % W4_AFTER.index((half, t)))
             else:
                 act = ring.tile([P, BANK], F32, name="act")
-            nc.scalar.activation(out=act[:], in_=gelu_bank[:], func=GELU)
-            for a in range(2):
-                first = a * H + P * t
-                nc.tensor.matmul_mx(
-                    out=plain_bank[:], lhsT=w1_codes[:, 2 * first : 2 * (first + P)].bitcast(FP4X4),
-                    lhsT_scale=w1_sc[a][:, rows],
-                    rhs=fuel_codes[a][:, cols].bitcast(FP8X4), rhs_scale=fuel_sc[a][:, cols],
-                    start=(a == 0), stop=(a == 1),
-                )
-            nc.vector.tensor_tensor(fuel[half][:, t, :], plain_bank[:], act[:], ALU.add)
+            nc.scalar.activation(out=act[:], in_=banks[(half, t, False)][:], func=GELU)
+            for a in range(1 - half, 2):
+                fuel_pass(half, t, True, a)
+            nc.vector.tensor_tensor(fuel[half][:, t, :], banks[(half, t, True)][:], act[:], ALU.add)
+
+        wind_codes = {}
+
+        def gather_wind(half):
+            wind_codes[half] = held("wind_codes%d" % half, [P, BANK], U16, tag=("fuel_rows_then_fuel1", "w4_bf0")[half])
+            nc.vector.tensor_copy(
+                wind_codes[half][:], wind_win[:].indirect(offs2_sb[:, BANK // 16 * half : BANK // 16 * (half + 1)])
+            )
 
         def meet_wind(chunk):
             cols = slice(CHUNK * chunk, CHUNK * (chunk + 1))
@@ -189,7 +207,7 @@ def tile_list_wildfire_cell_tasking_kernel(
                 rows = slice(P * t, P * (t + 1))
                 nc.tensor.matmul_mx(
                     out=wind_bank[:, rows], lhsT=w3_codes[:, rows].bitcast(FP8X4), lhsT_scale=w3_sc[:, rows],
-                    rhs=wind_codes[:, cols].bitcast(FP4X4), rhs_scale=wind_sc[:, cols],
+                    rhs=wind_codes[chunk // PACK][:, CHUNK * (chunk % PACK) : CHUNK * (chunk % PACK + 1)].bitcast(FP4X4), rhs_scale=wind_sc[:, cols],
                     start=True, stop=True,
                 )
             blk = max(i for i, (c0, w) in enumerate(BLOCKS) if c0 <= CHUNK * chunk)
@@ -233,7 +251,7 @@ def tile_list_wildfire_cell_tasking_kernel(
                         start=True, stop=True,
                     )
                 sums = task_bank
-                if blk == 0 and ts[i] < PACK - 1:
+                if (blk, g, ts[i]) in EMPTIED:
                     sums = ring.tile([P, BANK], F32, name="sums")
                     nc.scalar.copy(sums[:], task_bank[:])
                 for s, t in enumerate(ts[i : i + per_bank]):
@@ -262,6 +280,7 @@ def tile_list_wildfire_cell_tasking_kernel(
                 out_1[g, :, c0 : c0 + w, :].rearrange("p m t -> p (m t)").bitcast(I32), y_codes[:].bitcast(I32)
             )
 
+        gather_wind(0)
         for t in range(3):
             fuel_sum(0, t)
         round_w4(0, (0, 1))
@@ -275,6 +294,7 @@ def tile_list_wildfire_cell_tasking_kernel(
         meet_wind(3)
         quantise_w4(0)
         quantise_h(0)
+        gather_wind(1)
 
         fuel_sum(1, 1)
         round_w4(1, (2, 3))

@@ -125,8 +125,8 @@ def tile_list_wildfire_cell_tasking_kernel(
         w2_codes, w2_sc = {}, {}
         for a in range(2):
             w2_bf = held("w2_bf%d" % a, [P, PACK * H], BF16)
-            dst = w2_bf[:].rearrange("p (t b u l j) -> p t b u j l", t=PACK, u=4, l=2, j=PACK)
-            src = w2_raw[a][:].rearrange("p j (b t u l) -> p t b u j l", t=PACK, u=4, l=2)
+            dst = w2_bf[:].rearrange("p (t b u l j) -> p t b u j l", t=PACK, u=2, l=4, j=PACK)
+            src = w2_raw[a][:].rearrange("p j (b t u l) -> p t b u j l", t=PACK, u=2, l=4)
             for t in range(PACK):
                 nc.scalar.copy(dst[:, t], src[:, t])
             w2_codes[a] = held("w2_codes%d" % a, [P, H], U32)
@@ -265,10 +265,10 @@ def tile_list_wildfire_cell_tasking_kernel(
         def round_y(blk, g, copy):
             c0, w = BLOCKS[blk]
             y_bf[(blk, g)] = held("y_bf%d_%d" % (blk, g), [P, PACK * w], BF16)
-            dst = y_bf[(blk, g)][:].rearrange("p (m l t) -> p m t l", l=2, t=PACK)
-            src = y_f32[(blk, g)][:].rearrange("p t (m l) -> p m t l", l=2)
-            for m0 in range(0, w // 2, P):
-                copy(dst[:, m0 : m0 + P], src[:, m0 : m0 + P])
+            dst = y_bf[(blk, g)][:].rearrange("p (m l t) -> p m t l", l=4, t=PACK)
+            src = y_f32[(blk, g)][:].rearrange("p t (m l) -> p m t l", l=4)
+            for m0 in range(0, w // 4, 64):
+                copy(dst[:, m0 : m0 + 64], src[:, m0 : m0 + 64])
 
         def quantise_y(blk, g):
             c0, w = BLOCKS[blk]

@@ -27,7 +27,7 @@ W4_PIECE = 32
 COL_W3, COL_FUEL, COL_W1, COL_WIND, COL_END = 0, H, H + S, 2 * H + S, 2 * H + 2 * S
 
 W4_AFTER = ((0, 0), (0, 3))
-EMPTIED = ((0, 0, 0), (0, 0, 1), (0, 0, 2), (0, 1, 0), (0, 1, 1), (0, 1, 2))
+EMPTIED = ((0, 0, 2), (0, 0, 3), (0, 1, 0), (0, 1, 1), (0, 1, 2), (0, 1, 3), (1, 0, 0), (1, 1, 0))
 BLOCKS = ((0, 512), (512, 256), (768, 256))
 
 
@@ -39,7 +39,7 @@ def tile_list_wildfire_cell_tasking_kernel(
     with ExitStack() as ctx:
         keep = ctx.enter_context(tc.tile_pool(name="keep", bufs=1))
         ring = ctx.enter_context(tc.tile_pool(name="ring", bufs=3))
-        psum = ctx.enter_context(tc.psum_pool(name="psum", bufs=8))
+        psum = ctx.enter_context(tc.psum_pool(name="psum", bufs=4))
 
         def held(name, shape, dtype, tag=None):
             return keep.tile(shape, dtype, name=name, tag=tag or name, align_bytes=64)
@@ -165,7 +165,7 @@ def tile_list_wildfire_cell_tasking_kernel(
             rows = slice(P * t, P * (t + 1))
             first = a * H + P * t
             if a == 0:
-                banks[(half, t, plain)] = psum.tile([P, BANK], F32, name="fuel_bank", tag="bank")
+                banks[(half, t, plain)] = psum.tile([P, BANK], F32, name="fuel_bank", tag="plain" if plain else "gelu")
             if plain:
                 codes, scales = w1_codes[:, 2 * first : 2 * (first + P)].bitcast(FP4X4), w1_sc[a][:, rows]
             else:
@@ -180,17 +180,19 @@ def tile_list_wildfire_cell_tasking_kernel(
             fuel_pass(0, t, False, 0)
             fuel_pass(0, t, True, 0)
 
-        def fuel_sum(half, t):
+        act = {}
+
+        def fuel_gelu(half, t):
             for a in range(1 - half, 2):
                 fuel_pass(half, t, False, a)
-            if (half, t) in W4_AFTER:
-                act = held("act%d_%d" % (half, t), [P, BANK], F32, tag="w4_bf%d" % W4_AFTER.index((half, t)))
-            else:
-                act = ring.tile([P, BANK], F32, name="act")
-            nc.scalar.activation(out=act[:], in_=banks[(half, t, False)][:], func=GELU)
+            tag = "w4_bf%d" % W4_AFTER.index((half, t)) if (half, t) in W4_AFTER else None
+            act[(half, t)] = held("act%d_%d" % (half, t), [P, BANK], F32, tag=tag)
+            nc.scalar.activation(out=act[(half, t)][:], in_=banks[(half, t, False)][:], func=GELU)
+
+        def fuel_sum(half, t):
             for a in range(1 - half, 2):
                 fuel_pass(half, t, True, a)
-            nc.vector.tensor_tensor(fuel[half][:, t, :], banks[(half, t, True)][:], act[:], ALU.add)
+            nc.vector.tensor_tensor(fuel[half][:, t, :], banks[(half, t, True)][:], act[(half, t)][:], ALU.add)
 
         wind_codes = {}
 
@@ -202,7 +204,7 @@ def tile_list_wildfire_cell_tasking_kernel(
 
         def meet_wind(chunk):
             cols = slice(CHUNK * chunk, CHUNK * (chunk + 1))
-            wind_bank = psum.tile([P, BANK], F32, name="wind_bank", tag="bank")
+            wind_bank = psum.tile([P, BANK], F32, name="wind_bank", tag="plain")
             for t in range(PACK):
                 rows = slice(P * t, P * (t + 1))
                 nc.tensor.matmul_mx(
@@ -214,9 +216,9 @@ def tile_list_wildfire_cell_tasking_kernel(
             first = PACK * (CHUNK * chunk - BLOCKS[blk][0])
             half, part = divmod(chunk, PACK)
             nc.vector.tensor_tensor(
-                h_bf[blk][:, first : first + BANK].rearrange("p (m l t) -> p m t l", l=2, t=PACK),
-                wind_bank[:].rearrange("p (t m l) -> p m t l", l=2, t=PACK),
-                fuel[half][:, :, CHUNK * part : CHUNK * (part + 1)].rearrange("p t (m l) -> p m t l", l=2),
+                h_bf[blk][:, first : first + BANK].rearrange("p (m l t) -> p m t l", l=4, t=PACK),
+                wind_bank[:].rearrange("p (t m l) -> p m t l", l=4, t=PACK),
+                fuel[half][:, :, CHUNK * part : CHUNK * (part + 1)].rearrange("p t (m l) -> p m t l", l=4),
                 ALU.mult,
             )
 
@@ -242,7 +244,7 @@ def tile_list_wildfire_cell_tasking_kernel(
             y = y_f32[(blk, g)]
             per_bank = BANK // w
             for i in range(0, len(ts), per_bank):
-                task_bank = psum.tile([P, BANK], F32, name="task_bank", tag="bank")
+                task_bank = psum.tile([P, BANK], F32, name="task_bank", tag="plain" if blk == 2 else "gelu")
                 for s, t in enumerate(ts[i : i + per_bank]):
                     rows = slice(P * t, P * (t + 1))
                     nc.tensor.matmul_mx(
@@ -270,63 +272,68 @@ def tile_list_wildfire_cell_tasking_kernel(
             for m0 in range(0, w // 4, 64):
                 copy(dst[:, m0 : m0 + 64], src[:, m0 : m0 + 64])
 
+        y_codes = [held("y_codes%d" % blk, [P, 2, w], U32) for blk, (c0, w) in enumerate(BLOCKS)]
+
         def quantise_y(blk, g):
             c0, w = BLOCKS[blk]
-            y_codes = held("y_codes%d_%d" % (blk, g), [P, w], U32)
             nc.vector.quantize_mx(
-                out=y_codes[:].bitcast(FP8X4), scales=y_sc[:, g, c0 : c0 + w], in_=y_bf[(blk, g)][:]
+                out=y_codes[blk][:, g, :].bitcast(FP8X4), scales=y_sc[:, g, c0 : c0 + w], in_=y_bf[(blk, g)][:]
             )
-            nc.sync.dma_start(
-                out_1[g, :, c0 : c0 + w, :].rearrange("p m t -> p (m t)").bitcast(I32), y_codes[:].bitcast(I32)
-            )
+            if blk == 0:
+                nc.sync.dma_start(
+                    out_1[g, :, c0 : c0 + w, :].rearrange("p m t -> p (m t)").bitcast(I32),
+                    y_codes[blk][:, g, :].bitcast(I32),
+                )
+            elif g == 1:
+                nc.sync.dma_start(
+                    out_1[:, :, c0 : c0 + w, :].rearrange("g p m t -> p g (m t)").bitcast(I32),
+                    y_codes[blk][:].bitcast(I32),
+                )
 
         gather_wind(0)
-        for t in range(3):
+        for t in range(PACK):
+            fuel_gelu(0, t)
             fuel_sum(0, t)
-        round_w4(0, (0, 1))
-        fuel_sum(0, 3)
-        round_w4(0, (2, 3))
-        meet_wind(0)
-        meet_wind(1)
-        fuel_sum(1, 0)
-        round_w4(1, (0, 1))
-        meet_wind(2)
-        meet_wind(3)
-        quantise_w4(0)
+        round_w4(0, range(PACK))
+        for t in range(PACK):
+            fuel_gelu(1, t)
+        round_w4(1, range(PACK))
+        for chunk in range(PACK):
+            meet_wind(chunk)
         quantise_h(0)
+        quantise_w4(0)
         gather_wind(1)
 
-        fuel_sum(1, 1)
-        round_w4(1, (2, 3))
         task_rows(0, 0, (0, 1))
-        fuel_sum(1, 2)
-        task_rows(0, 0, (2, 3))
-        round_y(0, 0, nc.scalar.copy)
-        fuel_sum(1, 3)
+        fuel_sum(1, 0)
+        fuel_sum(1, 1)
         quantise_w4(1)
-        task_rows(0, 1, (0, 1))
+        task_rows(0, 0, (2, 3))
+        fuel_sum(1, 2)
+        fuel_sum(1, 3)
         meet_wind(4)
         meet_wind(5)
-        task_rows(0, 1, (2, 3))
-        round_y(0, 1, nc.scalar.copy)
         quantise_h(1)
-        meet_wind(6)
-        meet_wind(7)
-        quantise_y(0, 0)
-        quantise_h(2)
-
+        task_rows(0, 1, (0, 1))
+        task_rows(0, 1, (2, 3))
+        round_y(0, 0, nc.scalar.copy)
         every_slice = tuple(range(PACK))
         task_rows(1, 0, every_slice)
-        round_y(1, 0, nc.scalar.copy)
+        meet_wind(6)
         task_rows(1, 1, every_slice)
-        round_y(1, 1, nc.scalar.copy)
-        quantise_y(0, 1)
+        meet_wind(7)
+        quantise_h(2)
+        quantise_y(0, 0)
         task_rows(2, 0, every_slice)
-        round_y(2, 0, nc.scalar.copy)
-        quantise_y(1, 0)
         task_rows(2, 1, every_slice)
-        quantise_y(1, 1)
+        round_y(0, 1, nc.scalar.copy)
+        round_y(1, 0, nc.scalar.copy)
+        round_y(1, 1, nc.scalar.copy)
+        round_y(2, 0, nc.scalar.copy)
+        quantise_y(0, 1)
         round_y(2, 1, nc.vector.tensor_copy)
+        quantise_y(1, 0)
+        quantise_y(1, 1)
         quantise_y(2, 0)
         quantise_y(2, 1)
 

@@ -264,11 +264,15 @@ def tile_list_wildfire_cell_tasking_kernel(
             rows_out = out_0[PASS * g : PASS * (g + 1), c0 : c0 + w].rearrange("(p t) m -> p t m", t=PACK)
             nc.sync.dma_start(rows_out[:, ts[0] : ts[-1] + 1, :], y[:, ts[0] : ts[-1] + 1, :])
 
-        def round_y(blk, g, copy):
+        def round_y(blk, g, copy, other=None):
             c0, w = BLOCKS[blk]
             y_bf[(blk, g)] = held("y_bf%d_%d" % (blk, g), [P, PACK * w], BF16)
             dst = y_bf[(blk, g)][:].rearrange("p (m l t) -> p m t l", l=4, t=PACK)
             src = y_f32[(blk, g)][:].rearrange("p t (m l) -> p m t l", l=4)
+            if other is not None:
+                copy(dst[:, : w // 8], src[:, : w // 8])
+                other(dst[:, w // 8 :], src[:, w // 8 :])
+                return
             for m0 in range(0, w // 4, 64):
                 copy(dst[:, m0 : m0 + 64], src[:, m0 : m0 + 64])
 
@@ -311,10 +315,10 @@ def tile_list_wildfire_cell_tasking_kernel(
         task_rows(0, 0, (2, 3))
         fuel_sum(1, 2)
         fuel_sum(1, 3)
+        task_rows(0, 1, (0, 1))
         meet_wind(4)
         meet_wind(5)
         quantise_h(1)
-        task_rows(0, 1, (0, 1))
         task_rows(0, 1, (2, 3))
         round_y(0, 0, nc.scalar.copy)
         every_slice = tuple(range(PACK))
@@ -331,7 +335,7 @@ def tile_list_wildfire_cell_tasking_kernel(
         round_y(1, 1, nc.scalar.copy)
         round_y(2, 0, nc.scalar.copy)
         quantise_y(0, 1)
-        round_y(2, 1, nc.vector.tensor_copy)
+        round_y(2, 1, nc.vector.tensor_copy, nc.scalar.copy)
         quantise_y(1, 0)
         quantise_y(1, 1)
         quantise_y(2, 0)

@@ -38,7 +38,7 @@ def tile_list_wildfire_cell_tasking_kernel(
     nc = tc.nc
     with ExitStack() as ctx:
         keep = ctx.enter_context(tc.tile_pool(name="keep", bufs=1))
-        ring = ctx.enter_context(tc.tile_pool(name="ring", bufs=3))
+        ring = ctx.enter_context(tc.tile_pool(name="ring", bufs=8))
         psum = ctx.enter_context(tc.psum_pool(name="psum", bufs=4))
 
         def held(name, shape, dtype, tag=None):
@@ -324,9 +324,9 @@ def tile_list_wildfire_cell_tasking_kernel(
         every_slice = tuple(range(PACK))
         task_rows(1, 0, every_slice)
         meet_wind(6)
-        task_rows(1, 1, every_slice)
         meet_wind(7)
         quantise_h(2)
+        task_rows(1, 1, every_slice)
         quantise_y(0, 0)
         task_rows(2, 0, every_slice)
         task_rows(2, 1, every_slice)

@@ -26,9 +26,9 @@ W4_PIECE = 32
 
 COL_W3, COL_FUEL, COL_W1, COL_WIND, COL_END = 0, H, H + S, 2 * H + S, 2 * H + 2 * S
 
-W4_AFTER = ((0, 0), (0, 3))
-EMPTIED = ((0, 0, 2), (0, 0, 3), (0, 1, 0), (0, 1, 1), (0, 1, 2), (0, 1, 3), (1, 0, 0), (1, 1, 0))
 BLOCKS = ((0, 512), (512, 256), (768, 256))
+
+EMPTIED = tuple((0, g, t) for g in range(2) for t in range(PACK))[1:] + ((1, 0, 0),)
 
 
 def tile_list_wildfire_cell_tasking_kernel(
@@ -38,7 +38,7 @@ def tile_list_wildfire_cell_tasking_kernel(
     nc = tc.nc
     with ExitStack() as ctx:
         keep = ctx.enter_context(tc.tile_pool(name="keep", bufs=1))
-        ring = ctx.enter_context(tc.tile_pool(name="ring", bufs=8))
+        ring = ctx.enter_context(tc.tile_pool(name="ring", bufs=len(EMPTIED)))
         psum = ctx.enter_context(tc.psum_pool(name="psum", bufs=4))
 
         def held(name, shape, dtype, tag=None):
@@ -165,7 +165,8 @@ def tile_list_wildfire_cell_tasking_kernel(
             rows = slice(P * t, P * (t + 1))
             first = a * H + P * t
             if a == 0:
-                banks[(half, t, plain)] = psum.tile([P, BANK], F32, name="fuel_bank", tag="plain" if plain else "gelu")
+                ring_tag = "plain" if plain else "gelu"
+                banks[(half, t, plain)] = psum.tile([P, BANK], F32, name="fuel_bank", tag=ring_tag)
             if plain:
                 codes, scales = w1_codes[:, 2 * first : 2 * (first + P)].bitcast(FP4X4), w1_sc[a][:, rows]
             else:
@@ -182,11 +183,12 @@ def tile_list_wildfire_cell_tasking_kernel(
 
         act = {}
 
+        act_tags = {(0, 0): "w4_bf0", (0, PACK - 1): "w4_bf1"}
+
         def fuel_gelu(half, t):
             for a in range(1 - half, 2):
                 fuel_pass(half, t, False, a)
-            tag = "w4_bf%d" % W4_AFTER.index((half, t)) if (half, t) in W4_AFTER else None
-            act[(half, t)] = held("act%d_%d" % (half, t), [P, BANK], F32, tag=tag)
+            act[(half, t)] = held("act%d_%d" % (half, t), [P, BANK], F32, tag=act_tags.get((half, t)))
             nc.scalar.activation(out=act[(half, t)][:], in_=banks[(half, t, False)][:], func=GELU)
 
         def fuel_sum(half, t):
@@ -197,42 +199,41 @@ def tile_list_wildfire_cell_tasking_kernel(
         wind_codes = {}
 
         def gather_wind(half):
-            wind_codes[half] = held("wind_codes%d" % half, [P, BANK], U16, tag=("fuel_rows_then_fuel1", "w4_bf0")[half])
-            nc.vector.tensor_copy(
-                wind_codes[half][:], wind_win[:].indirect(offs2_sb[:, BANK // 16 * half : BANK // 16 * (half + 1)])
-            )
+            tag = ("fuel_rows_then_fuel1", "w4_bf0")[half]
+            wind_codes[half] = held("wind_codes%d" % half, [P, BANK], U16, tag=tag)
+            entries = offs2_sb[:, BANK // 16 * half : BANK // 16 * (half + 1)]
+            nc.vector.tensor_copy(wind_codes[half][:], wind_win[:].indirect(entries))
 
         def meet_wind(chunk):
+            half, part = divmod(chunk, PACK)
             cols = slice(CHUNK * chunk, CHUNK * (chunk + 1))
+            cols_in_half = slice(CHUNK * part, CHUNK * (part + 1))
             wind_bank = psum.tile([P, BANK], F32, name="wind_bank", tag="plain")
             for t in range(PACK):
                 rows = slice(P * t, P * (t + 1))
                 nc.tensor.matmul_mx(
                     out=wind_bank[:, rows], lhsT=w3_codes[:, rows].bitcast(FP8X4), lhsT_scale=w3_sc[:, rows],
-                    rhs=wind_codes[chunk // PACK][:, CHUNK * (chunk % PACK) : CHUNK * (chunk % PACK + 1)].bitcast(FP4X4), rhs_scale=wind_sc[:, cols],
+                    rhs=wind_codes[half][:, cols_in_half].bitcast(FP4X4), rhs_scale=wind_sc[:, cols],
                     start=True, stop=True,
                 )
             blk = max(i for i, (c0, w) in enumerate(BLOCKS) if c0 <= CHUNK * chunk)
             first = PACK * (CHUNK * chunk - BLOCKS[blk][0])
-            half, part = divmod(chunk, PACK)
             nc.vector.tensor_tensor(
                 h_bf[blk][:, first : first + BANK].rearrange("p (m l t) -> p m t l", l=4, t=PACK),
                 wind_bank[:].rearrange("p (t m l) -> p m t l", l=4, t=PACK),
-                fuel[half][:, :, CHUNK * part : CHUNK * (part + 1)].rearrange("p t (m l) -> p m t l", l=4),
+                fuel[half][:, :, cols_in_half].rearrange("p t (m l) -> p m t l", l=4),
                 ALU.mult,
             )
 
         def quantise_h(blk):
             nc.vector.quantize_mx(out=h_codes[blk][:].bitcast(FP8X4), scales=h_sc[blk][:], in_=h_bf[blk][:])
 
-        def round_w4(g, pieces):
-            if g not in w4_bf:
-                w4_bf[g] = held("w4_bf%d" % g, [P, PACK * PASS], BF16)
+        def round_w4(g):
+            w4_bf[g] = held("w4_bf%d" % g, [P, PACK * PASS], BF16)
             dst = w4_bf[g][:].rearrange("p (t m j) -> p m j t", t=PACK, j=PACK)
             src = w4_raw[:, g].rearrange("p j (m t) -> p m j t", t=PACK)
-            for piece in pieces:
-                ms = slice(W4_PIECE * piece, W4_PIECE * (piece + 1))
-                nc.scalar.copy(dst[:, ms], src[:, ms])
+            for m0 in range(0, P, W4_PIECE):
+                nc.scalar.copy(dst[:, m0 : m0 + W4_PIECE], src[:, m0 : m0 + W4_PIECE])
 
         def quantise_w4(g):
             nc.vector.quantize_mx(out=w4_codes[g][:].bitcast(FP8X4), scales=w4_sc[g][:], in_=w4_bf[g][:])
@@ -244,7 +245,8 @@ def tile_list_wildfire_cell_tasking_kernel(
             y = y_f32[(blk, g)]
             per_bank = BANK // w
             for i in range(0, len(ts), per_bank):
-                task_bank = psum.tile([P, BANK], F32, name="task_bank", tag="plain" if blk == 2 else "gelu")
+                ring_tag = "plain" if blk == len(BLOCKS) - 1 else "gelu"
+                task_bank = psum.tile([P, BANK], F32, name="task_bank", tag=ring_tag)
                 for s, t in enumerate(ts[i : i + per_bank]):
                     rows = slice(P * t, P * (t + 1))
                     nc.tensor.matmul_mx(
@@ -264,17 +266,14 @@ def tile_list_wildfire_cell_tasking_kernel(
             rows_out = out_0[PASS * g : PASS * (g + 1), c0 : c0 + w].rearrange("(p t) m -> p t m", t=PACK)
             nc.sync.dma_start(rows_out[:, ts[0] : ts[-1] + 1, :], y[:, ts[0] : ts[-1] + 1, :])
 
-        def round_y(blk, g, copy, other=None):
+        def round_y(blk, g, copies):
             c0, w = BLOCKS[blk]
             y_bf[(blk, g)] = held("y_bf%d_%d" % (blk, g), [P, PACK * w], BF16)
             dst = y_bf[(blk, g)][:].rearrange("p (m l t) -> p m t l", l=4, t=PACK)
             src = y_f32[(blk, g)][:].rearrange("p t (m l) -> p m t l", l=4)
-            if other is not None:
-                copy(dst[:, : w // 8], src[:, : w // 8])
-                other(dst[:, w // 8 :], src[:, w // 8 :])
-                return
-            for m0 in range(0, w // 4, 64):
-                copy(dst[:, m0 : m0 + 64], src[:, m0 : m0 + 64])
+            share = w // 4 // len(copies)
+            for i, copy in enumerate(copies):
+                copy(dst[:, share * i : share * (i + 1)], src[:, share * i : share * (i + 1)])
 
         y_codes = [held("y_codes%d" % blk, [P, 2, w], U32) for blk, (c0, w) in enumerate(BLOCKS)]
 
@@ -298,10 +297,10 @@ def tile_list_wildfire_cell_tasking_kernel(
         for t in range(PACK):
             fuel_gelu(0, t)
             fuel_sum(0, t)
-        round_w4(0, range(PACK))
+        round_w4(0)
         for t in range(PACK):
             fuel_gelu(1, t)
-        round_w4(1, range(PACK))
+        round_w4(1)
         for chunk in range(PACK):
             meet_wind(chunk)
         quantise_h(0)
@@ -320,7 +319,7 @@ def tile_list_wildfire_cell_tasking_kernel(
         meet_wind(5)
         quantise_h(1)
         task_rows(0, 1, (2, 3))
-        round_y(0, 0, nc.scalar.copy)
+        round_y(0, 0, (nc.scalar.copy, nc.scalar.copy))
         every_slice = tuple(range(PACK))
         task_rows(1, 0, every_slice)
         meet_wind(6)
@@ -330,12 +329,12 @@ def tile_list_wildfire_cell_tasking_kernel(
         quantise_y(0, 0)
         task_rows(2, 0, every_slice)
         task_rows(2, 1, every_slice)
-        round_y(0, 1, nc.scalar.copy)
-        round_y(1, 0, nc.scalar.copy)
-        round_y(1, 1, nc.scalar.copy)
-        round_y(2, 0, nc.scalar.copy)
+        round_y(0, 1, (nc.scalar.copy, nc.scalar.copy))
+        round_y(1, 0, (nc.scalar.copy,))
+        round_y(1, 1, (nc.scalar.copy,))
+        round_y(2, 0, (nc.scalar.copy,))
         quantise_y(0, 1)
-        round_y(2, 1, nc.vector.tensor_copy, nc.scalar.copy)
+        round_y(2, 1, (nc.vector.tensor_copy, nc.scalar.copy))
         quantise_y(1, 0)
         quantise_y(1, 1)
         quantise_y(2, 0)

@@ -28,7 +28,10 @@ COL_W3, COL_FUEL, COL_W1, COL_WIND, COL_END = 0, H, H + S, 2 * H + S, 2 * H + 2 
 
 BLOCKS = ((0, 512), (512, 256), (768, 256))
 
-EMPTIED = tuple((0, g, t) for g in range(2) for t in range(PACK))[1:] + ((1, 0, 0),)
+H_PIECE = 256
+
+EMPTIED_BLOCK = 0
+EMPTIED_BANKS = 2 * PACK
 
 
 def tile_list_wildfire_cell_tasking_kernel(
@@ -38,32 +41,29 @@ def tile_list_wildfire_cell_tasking_kernel(
     nc = tc.nc
     with ExitStack() as ctx:
         keep = ctx.enter_context(tc.tile_pool(name="keep", bufs=1))
-        ring = ctx.enter_context(tc.tile_pool(name="ring", bufs=len(EMPTIED)))
+        laid = ctx.enter_context(tc.tile_pool(name="laid", bufs=1))
+        ring = ctx.enter_context(tc.tile_pool(name="ring", bufs=EMPTIED_BANKS))
         psum = ctx.enter_context(tc.psum_pool(name="psum", bufs=4))
 
         def held(name, shape, dtype, tag=None):
             return keep.tile(shape, dtype, name=name, tag=tag or name, align_bytes=64)
 
-        wsc_raw = held("wsc_raw", [P, 2, H], U8)
+        wsc_raw = held("wsc_raw", [P, 2, H], U8, tag="wsc_then_w2_then_bounds")
         fuel_sc_win = held("fuel_sc_win", [P, T], U8)
         wind_sc_win = held("wind_sc_win", [P, T], U8)
         planes = [held("planes0", [P, COL_WIND], U8), held("planes1", [P, COL_END], U8)]
         nc.vector.memset(fuel_sc_win[:].bitcast(I32), 0)
         nc.vector.memset(wsc_raw[:].rearrange("p a c -> p (a c)").bitcast(I32), 0)
         nc.vector.memset(wind_sc_win[:].bitcast(I32), 0)
-        nc.vector.memset(planes[0][:].bitcast(I32), 0)
-        nc.vector.memset(planes[1][:, COL_FUEL:].bitcast(I32), 0)
 
         offs2_sb = keep.tile([P, S // 16], U16, name="offs2_sb")
         offs_sb = keep.tile([P, S // 16], U16, name="offs_sb")
         w1_raw = held("w1_raw", [P, H], I32, tag="w1_then_fuel0_then_w4")
-        w3_raw = held("w3_raw", [P, H], I32, tag="w3_then_w2_then_bounds")
         nc.sync.dma_start(
             w1_raw[:].rearrange("p (a w) -> p a w", a=2),
             w1_words.rearrange("a p n -> p a n").bitcast(I32),
         )
         nc.sync.dma_start(offs_sb[:], offs)
-        nc.sync.dma_start(w3_raw[:], w3_words[0].rearrange("p c i -> p (c i)").bitcast(I32))
         nc.sync.dma_start(offs2_sb[:], offs2)
         w2_raw = {0: held("w2_raw0", [P, PACK, H], F32)}
         nc.sync.dma_start(w2_raw[0][:], w2[:PASS, :].rearrange("(p j) c -> p j c", j=PACK))
@@ -81,12 +81,9 @@ def tile_list_wildfire_cell_tasking_kernel(
         )
         fuel_win0 = held("fuel_win0", [P, T], I32, tag="w1_then_fuel0_then_w4")
         nc.sync.dma_start(fuel_win0[:], tab_words[0].rearrange("p t i -> p (t i)").bitcast(I32))
-        nc.vector.tensor_copy(
-            w3_codes[:].rearrange("p (t b e) -> p t b e", t=PACK, e=8),
-            w3_raw[:].rearrange("p (b t e) -> p t b e", t=PACK, e=8),
-        )
-        w2_raw[1] = held("w2_raw1", [P, PACK, H], F32, tag="w3_then_w2_then_bounds")
-        nc.sync.dma_start(w2_raw[1][:], w2[PASS:, :].rearrange("(p j) c -> p j c", j=PACK))
+
+        nc.vector.memset(planes[0][:].bitcast(I32), 0)
+        nc.vector.memset(planes[1][:, COL_FUEL:].bitcast(I32), 0)
 
         spread = held("spread", [P, COL_END], U8)
         for i, col in ((0, COL_W3), (1, COL_W1)):
@@ -94,6 +91,9 @@ def tile_list_wildfire_cell_tasking_kernel(
                 spread[:, col : col + H].bitcast(I32).rearrange("p (t b e) -> p t b e", t=PACK, e=2),
                 wsc_raw[:, i, :].bitcast(I32).rearrange("p (b t e) -> p t b e", t=PACK, e=2),
             )
+
+        w2_raw[1] = held("w2_raw1", [P, PACK, H], F32, tag="wsc_then_w2_then_bounds")
+        nc.sync.dma_start(w2_raw[1][:], w2[PASS:, :].rearrange("(p j) c -> p j c", j=PACK))
 
         def place_rows(a, first, end):
             for i in range(4):
@@ -108,12 +108,15 @@ def tile_list_wildfire_cell_tasking_kernel(
         place_rows(0, COL_W3, COL_WIND)
         fuel_win1 = held("fuel_win1", [P, T], I32, tag="fuel_rows_then_fuel1")
         nc.sync.dma_start(fuel_win1[:], tab_words[1].rearrange("p t i -> p (t i)").bitcast(I32))
-        wind_sc_rows = held("wind_sc_rows", [P, S], U8, tag="wind_rows_then_wind")
+        wind_sc_rows = laid.tile([P, S], U8, name="wind_sc_rows", offset=2 * T - S // 2, align_bytes=64)
         nc.vector.tensor_copy(wind_sc_rows[:], wind_sc_win[:].indirect(offs2_sb[:]))
         nc.vector.tensor_copy(spread[:, COL_WIND:COL_END].bitcast(I32), wind_sc_rows[:].bitcast(I32))
         place_rows(1, COL_FUEL, COL_END)
-        wind_win = held("wind_win", [P, T], U16, tag="wind_rows_then_wind")
+        wind_win = laid.tile([P, T], U16, name="wind_win", offset=0, align_bytes=64)
         nc.sync.dma_start(wind_win[:].bitcast(I32), tab2_words[0].bitcast(I32))
+        w3_raw = laid.tile([P, H], I32, name="w3_raw", offset=2 * T, align_bytes=64)
+        nc.sync.dma_start(w3_raw[:], w3_words[0].rearrange("p c i -> p (c i)").bitcast(I32))
+
         fuel_sc = [planes[a][:, COL_FUEL:COL_W1] for a in range(2)]
         w1_sc = [planes[a][:, COL_W1:COL_WIND] for a in range(2)]
         w3_sc = planes[0][:, COL_W3:COL_FUEL]
@@ -138,7 +141,7 @@ def tile_list_wildfire_cell_tasking_kernel(
         for g in range(2):
             for j in range(PACK):
                 nc.sync.dma_start(w4_raw[:, g, j, :], w4_rows[j, :, :, PASS * g : PASS * (g + 1)])
-        bounds = held("bounds", [P, 2, 2, PACK], F32, tag="w3_then_w2_then_bounds")
+        bounds = held("bounds", [P, 2, 2, PACK], F32, tag="wsc_then_w2_then_bounds")
         nc.sync.dma_start(bounds[:, 0], lo.rearrange("(g p t) -> p g t", g=2, t=PACK))
         nc.sync.dma_start(bounds[:, 1], hi.rearrange("(g p t) -> p g t", g=2, t=PACK))
 
@@ -194,7 +197,12 @@ def tile_list_wildfire_cell_tasking_kernel(
         def fuel_sum(half, t):
             for a in range(1 - half, 2):
                 fuel_pass(half, t, True, a)
-            nc.vector.tensor_tensor(fuel[half][:, t, :], banks[(half, t, True)][:], act[(half, t)][:], ALU.add)
+            pieces = 2 if (half, t) == (0, PACK - 1) else 1
+            for i in range(pieces):
+                cols = slice(BANK // pieces * i, BANK // pieces * (i + 1))
+                nc.vector.tensor_tensor(
+                    fuel[half][:, t, cols], banks[(half, t, True)][:, cols], act[(half, t)][:, cols], ALU.add
+                )
 
         wind_codes = {}
 
@@ -226,7 +234,12 @@ def tile_list_wildfire_cell_tasking_kernel(
             )
 
         def quantise_h(blk):
-            nc.vector.quantize_mx(out=h_codes[blk][:].bitcast(FP8X4), scales=h_sc[blk][:], in_=h_bf[blk][:])
+            for first in range(0, BLOCKS[blk][1], H_PIECE):
+                cells = slice(first, first + H_PIECE)
+                nc.vector.quantize_mx(
+                    out=h_codes[blk][:, cells].bitcast(FP8X4), scales=h_sc[blk][:, cells],
+                    in_=h_bf[blk][:, PACK * first : PACK * (first + H_PIECE)],
+                )
 
         def round_w4(g):
             w4_bf[g] = held("w4_bf%d" % g, [P, PACK * PASS], BF16)
@@ -255,7 +268,7 @@ def tile_list_wildfire_cell_tasking_kernel(
                         start=True, stop=True,
                     )
                 sums = task_bank
-                if (blk, g, ts[i]) in EMPTIED:
+                if blk == EMPTIED_BLOCK:
                     sums = ring.tile([P, BANK], F32, name="sums")
                     nc.scalar.copy(sums[:], task_bank[:])
                 for s, t in enumerate(ts[i : i + per_bank]):
@@ -297,6 +310,10 @@ def tile_list_wildfire_cell_tasking_kernel(
         for t in range(PACK):
             fuel_gelu(0, t)
             fuel_sum(0, t)
+        nc.scalar.copy(
+            w3_codes[:].bitcast(U32).rearrange("p (t b e) -> p t b e", t=PACK, e=8),
+            w3_raw[:].bitcast(U32).rearrange("p (b t e) -> p t b e", t=PACK, e=8),
+        )
         round_w4(0)
         for t in range(PACK):
             fuel_gelu(1, t)
@@ -317,13 +334,13 @@ def tile_list_wildfire_cell_tasking_kernel(
         task_rows(0, 1, (0, 1))
         meet_wind(4)
         meet_wind(5)
-        quantise_h(1)
         task_rows(0, 1, (2, 3))
+        quantise_h(1)
         round_y(0, 0, (nc.scalar.copy, nc.scalar.copy))
-        every_slice = tuple(range(PACK))
-        task_rows(1, 0, every_slice)
         meet_wind(6)
         meet_wind(7)
+        every_slice = tuple(range(PACK))
+        task_rows(1, 0, every_slice)
         quantise_h(2)
         task_rows(1, 1, every_slice)
         quantise_y(0, 0)

@@ -227,9 +227,9 @@ def tile_list_wildfire_cell_tasking_kernel(
             blk = max(i for i, (c0, w) in enumerate(BLOCKS) if c0 <= CHUNK * chunk)
             first = PACK * (CHUNK * chunk - BLOCKS[blk][0])
             nc.vector.tensor_tensor(
-                h_bf[blk][:, first : first + BANK].rearrange("p (m l t) -> p m t l", l=4, t=PACK),
-                wind_bank[:].rearrange("p (t m l) -> p m t l", l=4, t=PACK),
-                fuel[half][:, :, cols_in_half].rearrange("p t (m l) -> p m t l", l=4),
+                h_bf[blk][:, first : first + BANK].rearrange("p (m l t) -> p m t l", l=2, t=PACK),
+                wind_bank[:].rearrange("p (t m l) -> p m t l", l=2, t=PACK),
+                fuel[half][:, :, cols_in_half].rearrange("p t (m l) -> p m t l", l=2),
                 ALU.mult,
             )
 

@@ -48,7 +48,7 @@ def tile_list_wildfire_cell_tasking_kernel(
         def held(name, shape, dtype, tag=None):
             return keep.tile(shape, dtype, name=name, tag=tag or name, align_bytes=64)
 
-        wsc_raw = held("wsc_raw", [P, 2, H], U8, tag="wsc_then_w2_then_bounds")
+        wsc_raw = held("wsc_raw", [P, 2, H], U8)
         fuel_sc_win = held("fuel_sc_win", [P, T], U8)
         wind_sc_win = held("wind_sc_win", [P, T], U8)
         planes = [held("planes0", [P, COL_WIND], U8), held("planes1", [P, COL_END], U8)]
@@ -58,11 +58,12 @@ def tile_list_wildfire_cell_tasking_kernel(
 
         offs2_sb = keep.tile([P, S // 16], U16, name="offs2_sb")
         offs_sb = keep.tile([P, S // 16], U16, name="offs_sb")
-        w1_raw = held("w1_raw", [P, H], I32, tag="w1_then_fuel0_then_w4")
-        nc.sync.dma_start(
-            w1_raw[:].rearrange("p (a w) -> p a w", a=2),
-            w1_words.rearrange("a p n -> p a n").bitcast(I32),
-        )
+        w1_raw = [
+            held("w1_raw0", [P, H], U16, tag="w1_then_fuel0_then_w4"),
+            held("w1_raw1", [P, H], U16, tag="w1_then_w2_then_bounds"),
+        ]
+        for a in range(2):
+            nc.sync.dma_start(w1_raw[a][:].bitcast(I32), w1_words[a].bitcast(I32))
         nc.sync.dma_start(offs_sb[:], offs)
         nc.sync.dma_start(offs2_sb[:], offs2)
         w2_raw = {0: held("w2_raw0", [P, PACK, H], F32)}
@@ -73,14 +74,18 @@ def tile_list_wildfire_cell_tasking_kernel(
         nc.sync.dma_start(wsc_raw[0:P:4, 1, :].bitcast(I32), w1_scales.rearrange("a q c -> (a q) c").bitcast(I32))
         nc.sync.dma_start(wind_sc_win[64:P:4, :].bitcast(I32), tab2_scales[0].bitcast(I32))
 
-        w1_codes = held("w1_codes", [P, 2 * 2 * H], U8)
+        w1_codes = held("w1_codes", [P, 2, H], U16)
         w3_codes = held("w3_codes", [P, H], I32)
-        nc.vector.tensor_copy(
-            w1_codes[:].bitcast(I32).rearrange("p (a t b e) -> p a t b e", a=2, t=PACK, e=4),
-            w1_raw[:].rearrange("p (a b t e) -> p a t b e", a=2, t=PACK, e=4),
-        )
+        for a in range(2):
+            nc.scalar.copy(
+                w1_codes[:, a, :].rearrange("p (t m) -> p m t", t=PACK),
+                w1_raw[a][:].rearrange("p (m t) -> p m t", t=PACK),
+            )
         fuel_win0 = held("fuel_win0", [P, T], I32, tag="w1_then_fuel0_then_w4")
         nc.sync.dma_start(fuel_win0[:], tab_words[0].rearrange("p t i -> p (t i)").bitcast(I32))
+
+        w2_raw[1] = held("w2_raw1", [P, PACK, H], F32, tag="w1_then_w2_then_bounds")
+        nc.sync.dma_start(w2_raw[1][:], w2[PASS:, :].rearrange("(p j) c -> p j c", j=PACK))
 
         nc.vector.memset(planes[0][:].bitcast(I32), 0)
         nc.vector.memset(planes[1][:, COL_FUEL:].bitcast(I32), 0)
@@ -88,12 +93,9 @@ def tile_list_wildfire_cell_tasking_kernel(
         spread = held("spread", [P, COL_END], U8)
         for i, col in ((0, COL_W3), (1, COL_W1)):
             nc.vector.tensor_copy(
-                spread[:, col : col + H].bitcast(I32).rearrange("p (t b e) -> p t b e", t=PACK, e=2),
-                wsc_raw[:, i, :].bitcast(I32).rearrange("p (b t e) -> p t b e", t=PACK, e=2),
+                spread[:, col : col + H].rearrange("p (t m) -> p m t", t=PACK),
+                wsc_raw[:, i, :].rearrange("p (m t) -> p m t", t=PACK),
             )
-
-        w2_raw[1] = held("w2_raw1", [P, PACK, H], F32, tag="wsc_then_w2_then_bounds")
-        nc.sync.dma_start(w2_raw[1][:], w2[PASS:, :].rearrange("(p j) c -> p j c", j=PACK))
 
         def place_rows(a, first, end):
             for i in range(4):
@@ -128,20 +130,19 @@ def tile_list_wildfire_cell_tasking_kernel(
         w2_codes, w2_sc = {}, {}
         for a in range(2):
             w2_bf = held("w2_bf%d" % a, [P, PACK * H], BF16)
-            dst = w2_bf[:].rearrange("p (t b u l j) -> p t b u j l", t=PACK, u=2, l=4, j=PACK)
-            src = w2_raw[a][:].rearrange("p j (b t u l) -> p t b u j l", t=PACK, u=2, l=4)
-            for t in range(PACK):
-                nc.scalar.copy(dst[:, t], src[:, t])
+            nc.scalar.copy(
+                w2_bf[:].rearrange("p (t m j) -> p m j t", t=PACK, j=PACK),
+                w2_raw[a][:].rearrange("p j (m t) -> p m j t", t=PACK),
+            )
             w2_codes[a] = held("w2_codes%d" % a, [P, H], U32)
             w2_sc[a] = held("w2_sc%d" % a, [P, H], U8)
             nc.vector.quantize_mx(out=w2_codes[a][:].bitcast(FP8X4), scales=w2_sc[a][:], in_=w2_bf[:])
 
-        w4_rows = w4.rearrange("(b j i) n -> j b i n", j=PACK, i=8)
+        w4_rows = w4.rearrange("(p j) n -> p j n", j=PACK)
         w4_raw = held("w4_raw", [P, 2, PACK, PASS], F32, tag="w1_then_fuel0_then_w4")
         for g in range(2):
-            for j in range(PACK):
-                nc.sync.dma_start(w4_raw[:, g, j, :], w4_rows[j, :, :, PASS * g : PASS * (g + 1)])
-        bounds = held("bounds", [P, 2, 2, PACK], F32, tag="wsc_then_w2_then_bounds")
+            nc.sync.dma_start(w4_raw[:, g], w4_rows[:, :, PASS * g : PASS * (g + 1)])
+        bounds = held("bounds", [P, 2, 2, PACK], F32, tag="w1_then_w2_then_bounds")
         nc.sync.dma_start(bounds[:, 0], lo.rearrange("(g p t) -> p g t", g=2, t=PACK))
         nc.sync.dma_start(bounds[:, 1], hi.rearrange("(g p t) -> p g t", g=2, t=PACK))
 
@@ -166,12 +167,11 @@ def tile_list_wildfire_cell_tasking_kernel(
         def fuel_pass(half, t, plain, a):
             cols = slice(BANK * half, BANK * (half + 1))
             rows = slice(P * t, P * (t + 1))
-            first = a * H + P * t
             if a == 0:
                 ring_tag = "plain" if plain else "gelu"
                 banks[(half, t, plain)] = psum.tile([P, BANK], F32, name="fuel_bank", tag=ring_tag)
             if plain:
-                codes, scales = w1_codes[:, 2 * first : 2 * (first + P)].bitcast(FP4X4), w1_sc[a][:, rows]
+                codes, scales = w1_codes[:, a, rows].bitcast(FP4X4), w1_sc[a][:, rows]
             else:
                 codes, scales = w2_codes[a][:, rows].bitcast(FP8X4), w2_sc[a][:, rows]
             nc.tensor.matmul_mx(
@@ -311,8 +311,8 @@ def tile_list_wildfire_cell_tasking_kernel(
             fuel_gelu(0, t)
             fuel_sum(0, t)
         nc.scalar.copy(
-            w3_codes[:].bitcast(U32).rearrange("p (t b e) -> p t b e", t=PACK, e=8),
-            w3_raw[:].bitcast(U32).rearrange("p (b t e) -> p t b e", t=PACK, e=8),
+            w3_codes[:].bitcast(U32).rearrange("p (t m) -> p m t", t=PACK),
+            w3_raw[:].bitcast(U32).rearrange("p (m t) -> p m t", t=PACK),
         )
         round_w4(0)
         for t in range(PACK):

@@ -24,7 +24,7 @@ BANK = 512
 CHUNK = BANK // PACK
 W4_PIECE = 32
 
-COL_W3, COL_FUEL, COL_W1, COL_WIND, COL_END = 0, H, H + S, 2 * H + S, 2 * H + 2 * S
+COL_W1, COL_W3, COL_WIND, COL_END = S, S + H, S + 2 * H, 2 * S + 2 * H
 
 BLOCKS = ((0, 512), (512, 256), (768, 256))
 
@@ -51,7 +51,7 @@ def tile_list_wildfire_cell_tasking_kernel(
         wsc_raw = held("wsc_raw", [P, 2, H], U8)
         fuel_sc_win = held("fuel_sc_win", [P, T], U8)
         wind_sc_win = held("wind_sc_win", [P, T], U8)
-        planes = [held("planes0", [P, COL_WIND], U8), held("planes1", [P, COL_END], U8)]
+        planes = [held("planes0", [P, COL_W3], U8), held("planes1", [P, COL_END], U8)]
         nc.vector.memset(fuel_sc_win[:].bitcast(I32), 0)
         nc.vector.memset(wsc_raw[:].rearrange("p a c -> p (a c)").bitcast(I32), 0)
         nc.vector.memset(wind_sc_win[:].bitcast(I32), 0)
@@ -70,8 +70,8 @@ def tile_list_wildfire_cell_tasking_kernel(
         nc.sync.dma_start(w2_raw[0][:], w2[:PASS, :].rearrange("(p j) c -> p j c", j=PACK))
 
         nc.sync.dma_start(fuel_sc_win[0:P:4, :].bitcast(I32), tab_scales.rearrange("a q t -> (a q) t").bitcast(I32))
-        nc.sync.dma_start(wsc_raw[0:64:4, 0, :].bitcast(I32), w3_scales[0].bitcast(I32))
-        nc.sync.dma_start(wsc_raw[0:P:4, 1, :].bitcast(I32), w1_scales.rearrange("a q c -> (a q) c").bitcast(I32))
+        nc.sync.dma_start(wsc_raw[64:P:4, 1, :].bitcast(I32), w3_scales[0].bitcast(I32))
+        nc.sync.dma_start(wsc_raw[0:P:4, 0, :].bitcast(I32), w1_scales.rearrange("a q c -> (a q) c").bitcast(I32))
         nc.sync.dma_start(wind_sc_win[64:P:4, :].bitcast(I32), tab2_scales[0].bitcast(I32))
 
         w1_codes = held("w1_codes", [P, 2, H], U16)
@@ -87,41 +87,41 @@ def tile_list_wildfire_cell_tasking_kernel(
         w2_raw[1] = held("w2_raw1", [P, PACK, H], F32, tag="w1_then_w2_then_bounds")
         nc.sync.dma_start(w2_raw[1][:], w2[PASS:, :].rearrange("(p j) c -> p j c", j=PACK))
 
-        nc.vector.memset(planes[0][:].bitcast(I32), 0)
-        nc.vector.memset(planes[1][:, COL_FUEL:].bitcast(I32), 0)
+        for plane in planes:
+            nc.vector.memset(plane[:].bitcast(I32), 0)
 
         spread = held("spread", [P, COL_END], U8)
-        for i, col in ((0, COL_W3), (1, COL_W1)):
+        for i, col in ((0, COL_W1), (1, COL_W3)):
             nc.vector.tensor_copy(
                 spread[:, col : col + H].rearrange("p (t m) -> p m t", t=PACK),
                 wsc_raw[:, i, :].rearrange("p (m t) -> p m t", t=PACK),
             )
 
-        def place_rows(a, first, end):
+        def place_rows(a, end):
             for i in range(4):
                 nc.sync.dma_start(
-                    planes[a][i:P:QUAD, first:end].bitcast(I32),
-                    spread[64 * a + 4 * i : 64 * (a + 1) : 16, first:end].bitcast(I32),
+                    planes[a][i:P:QUAD, :].bitcast(I32),
+                    spread[64 * a + 4 * i : 64 * (a + 1) : 16, :end].bitcast(I32),
                 )
 
         fuel_sc_rows = held("fuel_sc_rows", [P, S], U8, tag="fuel_rows_then_fuel1")
         nc.vector.tensor_copy(fuel_sc_rows[:], fuel_sc_win[:].indirect(offs_sb[:]))
-        nc.vector.tensor_copy(spread[:, COL_FUEL:COL_W1].bitcast(I32), fuel_sc_rows[:].bitcast(I32))
-        place_rows(0, COL_W3, COL_WIND)
+        nc.vector.tensor_copy(spread[:, :COL_W1].bitcast(I32), fuel_sc_rows[:].bitcast(I32))
+        place_rows(0, COL_W3)
         fuel_win1 = held("fuel_win1", [P, T], I32, tag="fuel_rows_then_fuel1")
         nc.sync.dma_start(fuel_win1[:], tab_words[1].rearrange("p t i -> p (t i)").bitcast(I32))
         wind_sc_rows = laid.tile([P, S], U8, name="wind_sc_rows", offset=2 * T - S // 2, align_bytes=64)
         nc.vector.tensor_copy(wind_sc_rows[:], wind_sc_win[:].indirect(offs2_sb[:]))
         nc.vector.tensor_copy(spread[:, COL_WIND:COL_END].bitcast(I32), wind_sc_rows[:].bitcast(I32))
-        place_rows(1, COL_FUEL, COL_END)
+        place_rows(1, COL_END)
         wind_win = laid.tile([P, T], U16, name="wind_win", offset=0, align_bytes=64)
         nc.sync.dma_start(wind_win[:].bitcast(I32), tab2_words[0].bitcast(I32))
         w3_raw = laid.tile([P, H], I32, name="w3_raw", offset=2 * T, align_bytes=64)
         nc.sync.dma_start(w3_raw[:], w3_words[0].rearrange("p c i -> p (c i)").bitcast(I32))
 
-        fuel_sc = [planes[a][:, COL_FUEL:COL_W1] for a in range(2)]
-        w1_sc = [planes[a][:, COL_W1:COL_WIND] for a in range(2)]
-        w3_sc = planes[0][:, COL_W3:COL_FUEL]
+        fuel_sc = [planes[a][:, :COL_W1] for a in range(2)]
+        w1_sc = [planes[a][:, COL_W1:COL_W3] for a in range(2)]
+        w3_sc = planes[1][:, COL_W3:COL_WIND]
         wind_sc = planes[1][:, COL_WIND:COL_END]
 
         fuel_codes = {0: held("fuel_codes0", [P, S], U32)}
@@ -158,7 +158,7 @@ def tile_list_wildfire_cell_tasking_kernel(
         h_sc = [held("h_sc%d" % blk, [P, w], U8) for blk, (c0, w) in enumerate(BLOCKS)]
         w4_codes = [held("w4_codes%d" % g, [P, PASS], U32) for g in range(2)]
         w4_sc = [held("w4_sc%d" % g, [P, PASS], U8) for g in range(2)]
-        y_sc = held("y_sc", [P, 2, S], U8)
+        y_sc = held("y_sc", [P, S], U8)
         fuel = [held("fuel%d" % half, [P, PACK, BANK], F32) for half in range(2)]
         w4_bf, y_f32, y_bf = {}, {}, {}
 
@@ -288,22 +288,20 @@ def tile_list_wildfire_cell_tasking_kernel(
             for i, copy in enumerate(copies):
                 copy(dst[:, share * i : share * (i + 1)], src[:, share * i : share * (i + 1)])
 
-        y_codes = [held("y_codes%d" % blk, [P, 2, w], U32) for blk, (c0, w) in enumerate(BLOCKS)]
+        y_codes = {(half, g): held("y_codes%d_%d" % (half, g), [P, BANK], U32) for half in range(2) for g in range(2)}
 
         def quantise_y(blk, g):
             c0, w = BLOCKS[blk]
+            half, first = divmod(c0, BANK)
             nc.vector.quantize_mx(
-                out=y_codes[blk][:, g, :].bitcast(FP8X4), scales=y_sc[:, g, c0 : c0 + w], in_=y_bf[(blk, g)][:]
+                out=y_codes[(half, g)][:, first : first + w].bitcast(FP8X4), scales=y_sc[4 * g :, c0 : c0 + w],
+                in_=y_bf[(blk, g)][:],
             )
-            if blk == 0:
+            if first + w == BANK:
+                cells = slice(BANK * half, BANK * (half + 1))
                 nc.sync.dma_start(
-                    out_1[g, :, c0 : c0 + w, :].rearrange("p m t -> p (m t)").bitcast(I32),
-                    y_codes[blk][:, g, :].bitcast(I32),
-                )
-            elif g == 1:
-                nc.sync.dma_start(
-                    out_1[:, :, c0 : c0 + w, :].rearrange("g p m t -> p g (m t)").bitcast(I32),
-                    y_codes[blk][:].bitcast(I32),
+                    out_1[g, :, cells, :].rearrange("p m t -> p (m t)").bitcast(I32),
+                    y_codes[(half, g)][:].bitcast(I32),
                 )
 
         gather_wind(0)
@@ -348,15 +346,16 @@ def tile_list_wildfire_cell_tasking_kernel(
         task_rows(2, 1, every_slice)
         round_y(0, 1, (nc.scalar.copy, nc.scalar.copy))
         round_y(1, 0, (nc.scalar.copy,))
-        round_y(1, 1, (nc.scalar.copy,))
         round_y(2, 0, (nc.scalar.copy,))
+        round_y(1, 1, (nc.scalar.copy,))
         quantise_y(0, 1)
         round_y(2, 1, (nc.vector.tensor_copy, nc.scalar.copy))
         quantise_y(1, 0)
-        quantise_y(1, 1)
         quantise_y(2, 0)
+        quantise_y(1, 1)
         quantise_y(2, 1)
 
-        scale_rows = out_2.rearrange("g (q i) m -> i q g m", i=4)
-        for i in range(4):
-            nc.sync.dma_start(scale_rows[i].bitcast(I32), y_sc[i:P:QUAD, :, :].bitcast(I32))
+        for q in range(4):
+            nc.sync.dma_start(
+                out_2[:, 4 * q : 4 * q + 4, :].bitcast(I32), y_sc[QUAD * q : QUAD * q + 8, :].bitcast(I32)
+            )

@@ -256,6 +256,7 @@ def tile_list_wildfire_cell_tasking_kernel(
             if (blk, g) not in y_f32:
                 y_f32[(blk, g)] = held("y%d_%d" % (blk, g), [P, PACK, w], F32)
             y = y_f32[(blk, g)]
+            rows_out = out_0[PASS * g : PASS * (g + 1), c0 : c0 + w].rearrange("(p t) m -> p t m", t=PACK)
             per_bank = BANK // w
             for i in range(0, len(ts), per_bank):
                 ring_tag = "plain" if blk == len(BLOCKS) - 1 else "gelu"
@@ -276,8 +277,9 @@ def tile_list_wildfire_cell_tasking_kernel(
                         y[:, t, :], sums[:, w * s : w * (s + 1)],
                         bounds[:, 0, g, t : t + 1], bounds[:, 1, g, t : t + 1], ALU.max, ALU.min,
                     )
-            rows_out = out_0[PASS * g : PASS * (g + 1), c0 : c0 + w].rearrange("(p t) m -> p t m", t=PACK)
-            nc.sync.dma_start(rows_out[:, ts[0] : ts[-1] + 1, :], y[:, ts[0] : ts[-1] + 1, :])
+                if (i + per_bank) % 2 == 0:
+                    pair = slice(ts[i + per_bank - 1] - 1, ts[i + per_bank - 1] + 1)
+                    nc.sync.dma_start(rows_out[:, pair, :], y[:, pair, :])
 
         def round_y(blk, g, copies):
             c0, w = BLOCKS[blk]

@@ -153,13 +153,13 @@ def tile_list_wildfire_cell_tasking_kernel(
                 fuel_win1[:].bitcast(U32).indirect(offs_sb[:, BANK // 16 * half : BANK // 16 * (half + 1)]),
             )
 
-        h_bf = [held("h_bf%d" % blk, [P, PACK * w], BF16) for blk, (c0, w) in enumerate(BLOCKS)]
+        h_bf = {blk: held("h_bf%d" % blk, [P, PACK * BLOCKS[blk][1]], BF16) for blk in (0, 2)}
         h_codes = [held("h_codes%d" % blk, [P, w], U32) for blk, (c0, w) in enumerate(BLOCKS)]
         h_sc = [held("h_sc%d" % blk, [P, w], U8) for blk, (c0, w) in enumerate(BLOCKS)]
         w4_codes = [held("w4_codes%d" % g, [P, PASS], U32) for g in range(2)]
         w4_sc = [held("w4_sc%d" % g, [P, PASS], U8) for g in range(2)]
         y_sc = held("y_sc", [P, S], U8)
-        fuel = [held("fuel%d" % half, [P, PACK, BANK], F32) for half in range(2)]
+        fuel = {1: held("fuel1", [P, PACK, BANK], F32)}
         w4_bf, y_f32, y_bf = {}, {}, {}
 
         banks = {}
@@ -204,13 +204,10 @@ def tile_list_wildfire_cell_tasking_kernel(
                     fuel[half][:, t, cols], banks[(half, t, True)][:, cols], act[(half, t)][:, cols], ALU.add
                 )
 
-        wind_codes = {}
+        wind_codes = held("wind_codes", [P, S], U16, tag="fuel_rows_then_fuel1")
 
-        def gather_wind(half):
-            tag = ("fuel_rows_then_fuel1", "w4_bf0")[half]
-            wind_codes[half] = held("wind_codes%d" % half, [P, BANK], U16, tag=tag)
-            entries = offs2_sb[:, BANK // 16 * half : BANK // 16 * (half + 1)]
-            nc.vector.tensor_copy(wind_codes[half][:], wind_win[:].indirect(entries))
+        def gather_wind():
+            nc.vector.tensor_copy(wind_codes[:], wind_win[:].indirect(offs2_sb[:]))
 
         def meet_wind(chunk):
             half, part = divmod(chunk, PACK)
@@ -221,7 +218,7 @@ def tile_list_wildfire_cell_tasking_kernel(
                 rows = slice(P * t, P * (t + 1))
                 nc.tensor.matmul_mx(
                     out=wind_bank[:, rows], lhsT=w3_codes[:, rows].bitcast(FP8X4), lhsT_scale=w3_sc[:, rows],
-                    rhs=wind_codes[half][:, cols_in_half].bitcast(FP4X4), rhs_scale=wind_sc[:, cols],
+                    rhs=wind_codes[:, cols].bitcast(FP4X4), rhs_scale=wind_sc[:, cols],
                     start=True, stop=True,
                 )
             blk = max(i for i, (c0, w) in enumerate(BLOCKS) if c0 <= CHUNK * chunk)
@@ -306,7 +303,8 @@ def tile_list_wildfire_cell_tasking_kernel(
                     y_codes[(half, g)][:].bitcast(I32),
                 )
 
-        gather_wind(0)
+        gather_wind()
+        fuel[0] = laid.tile([P, PACK, BANK], F32, name="fuel0", offset=0, align_bytes=64)
         for t in range(PACK):
             fuel_gelu(0, t)
             fuel_sum(0, t)
@@ -322,7 +320,7 @@ def tile_list_wildfire_cell_tasking_kernel(
             meet_wind(chunk)
         quantise_h(0)
         quantise_w4(0)
-        gather_wind(1)
+        h_bf[1] = held("h_bf1", [P, PACK * BLOCKS[1][1]], BF16, tag="w4_bf0")
 
         task_rows(0, 0, (0, 1))
         fuel_sum(1, 0)

@@ -26,6 +26,10 @@ W4_PIECE = 32
 
 COL_W1, COL_W3, COL_WIND, COL_END = S, S + H, S + 2 * H, 2 * S + 2 * H
 
+SIDE_SLICES = (1, 2)
+KIB = 1024
+AT_WIND, AT_W3, AT_FUEL0 = 4 * KIB, 12 * KIB, 16 * KIB
+
 BLOCKS = ((0, 512), (512, 256), (768, 256))
 
 H_PIECE = 256
@@ -42,11 +46,21 @@ def tile_list_wildfire_cell_tasking_kernel(
     with ExitStack() as ctx:
         keep = ctx.enter_context(tc.tile_pool(name="keep", bufs=1))
         laid = ctx.enter_context(tc.tile_pool(name="laid", bufs=1))
-        ring = ctx.enter_context(tc.tile_pool(name="ring", bufs=EMPTIED_BANKS))
-        psum = ctx.enter_context(tc.psum_pool(name="psum", bufs=4))
+        psum = ctx.enter_context(tc.psum_pool(name="psum", bufs=1))
 
         def held(name, shape, dtype, tag=None):
             return keep.tile(shape, dtype, name=name, tag=tag or name, align_bytes=64)
+
+        def lay(name, shape, dtype, at):
+            return laid.tile(shape, dtype, name=name, offset=at, align_bytes=64)
+
+        def bank(b):
+            return psum.tile([P, BANK], F32, name="bank%d" % b, tag="bank%d" % b)
+
+        table_in = held("table_in", [P, 1], F32)
+        table_out = held("table_out", [P, 1], F32)
+        nc.gpsimd.memset(table_in[:], 0.0)
+        nc.scalar.activation(out=table_out[:], in_=table_in[:], func=GELU)
 
         wsc_raw = held("wsc_raw", [P, 2, H], U8)
         fuel_sc_win = held("fuel_sc_win", [P, T], U8)
@@ -59,7 +73,7 @@ def tile_list_wildfire_cell_tasking_kernel(
         offs2_sb = keep.tile([P, S // 16], U16, name="offs2_sb")
         offs_sb = keep.tile([P, S // 16], U16, name="offs_sb")
         w1_raw = [
-            held("w1_raw0", [P, H], U16, tag="w1_then_fuel0_then_w4"),
+            lay("w1_raw0", [P, H], U16, AT_FUEL0),
             held("w1_raw1", [P, H], U16, tag="w1_then_w2_then_bounds"),
         ]
         for a in range(2):
@@ -81,7 +95,7 @@ def tile_list_wildfire_cell_tasking_kernel(
                 w1_codes[:, a, :].rearrange("p (t m) -> p m t", t=PACK),
                 w1_raw[a][:].rearrange("p (m t) -> p m t", t=PACK),
             )
-        fuel_win0 = held("fuel_win0", [P, T], I32, tag="w1_then_fuel0_then_w4")
+        fuel_win0 = lay("fuel_win0", [P, T], I32, AT_FUEL0)
         nc.sync.dma_start(fuel_win0[:], tab_words[0].rearrange("p t i -> p (t i)").bitcast(I32))
 
         w2_raw[1] = held("w2_raw1", [P, PACK, H], F32, tag="w1_then_w2_then_bounds")
@@ -110,13 +124,13 @@ def tile_list_wildfire_cell_tasking_kernel(
         place_rows(0, COL_W3)
         fuel_win1 = held("fuel_win1", [P, T], I32, tag="fuel_rows_then_fuel1")
         nc.sync.dma_start(fuel_win1[:], tab_words[1].rearrange("p t i -> p (t i)").bitcast(I32))
-        wind_sc_rows = laid.tile([P, S], U8, name="wind_sc_rows", offset=2 * T - S // 2, align_bytes=64)
+        wind_sc_rows = lay("wind_sc_rows", [P, S], U8, AT_W3 - S // 2)
         nc.vector.tensor_copy(wind_sc_rows[:], wind_sc_win[:].indirect(offs2_sb[:]))
         nc.vector.tensor_copy(spread[:, COL_WIND:COL_END].bitcast(I32), wind_sc_rows[:].bitcast(I32))
         place_rows(1, COL_END)
-        wind_win = laid.tile([P, T], U16, name="wind_win", offset=0, align_bytes=64)
+        wind_win = lay("wind_win", [P, T], U16, AT_WIND)
         nc.sync.dma_start(wind_win[:].bitcast(I32), tab2_words[0].bitcast(I32))
-        w3_raw = laid.tile([P, H], I32, name="w3_raw", offset=2 * T, align_bytes=64)
+        w3_raw = lay("w3_raw", [P, H], I32, AT_W3)
         nc.sync.dma_start(w3_raw[:], w3_words[0].rearrange("p c i -> p (c i)").bitcast(I32))
 
         fuel_sc = [planes[a][:, :COL_W1] for a in range(2)]
@@ -139,37 +153,36 @@ def tile_list_wildfire_cell_tasking_kernel(
             nc.vector.quantize_mx(out=w2_codes[a][:].bitcast(FP8X4), scales=w2_sc[a][:], in_=w2_bf[:])
 
         w4_rows = w4.rearrange("(p j) n -> p j n", j=PACK)
-        w4_raw = held("w4_raw", [P, 2, PACK, PASS], F32, tag="w1_then_fuel0_then_w4")
+        w4_raw = [lay("w4_raw%d" % g, [P, PACK, PASS], F32, AT_FUEL0 + 8 * KIB * g) for g in range(2)]
         for g in range(2):
-            nc.sync.dma_start(w4_raw[:, g], w4_rows[:, :, PASS * g : PASS * (g + 1)])
+            nc.sync.dma_start(w4_raw[g][:], w4_rows[:, :, PASS * g : PASS * (g + 1)])
         bounds = held("bounds", [P, 2, 2, PACK], F32, tag="w1_then_w2_then_bounds")
         nc.sync.dma_start(bounds[:, 0], lo.rearrange("(g p t) -> p g t", g=2, t=PACK))
         nc.sync.dma_start(bounds[:, 1], hi.rearrange("(g p t) -> p g t", g=2, t=PACK))
 
         fuel_codes[1] = held("fuel_codes1", [P, S], U32, tag="w2_bf1")
-        for half in range(2):
+        for half in (1, 0):
             nc.vector.tensor_copy(
                 fuel_codes[1][:, BANK * half : BANK * (half + 1)],
                 fuel_win1[:].bitcast(U32).indirect(offs_sb[:, BANK // 16 * half : BANK // 16 * (half + 1)]),
             )
 
-        h_bf = {blk: held("h_bf%d" % blk, [P, PACK * BLOCKS[blk][1]], BF16) for blk in (0, 2)}
+        h_bf = {blk: held("h_bf%d" % blk, [P, PACK * BLOCKS[blk][1]], BF16) for blk in (0,)}
         h_codes = [held("h_codes%d" % blk, [P, w], U32) for blk, (c0, w) in enumerate(BLOCKS)]
         h_sc = [held("h_sc%d" % blk, [P, w], U8) for blk, (c0, w) in enumerate(BLOCKS)]
         w4_codes = [held("w4_codes%d" % g, [P, PASS], U32) for g in range(2)]
         w4_sc = [held("w4_sc%d" % g, [P, PASS], U8) for g in range(2)]
         y_sc = held("y_sc", [P, S], U8)
-        fuel = {1: held("fuel1", [P, PACK, BANK], F32)}
+        fuel = {}
         w4_bf, y_f32, y_bf = {}, {}, {}
 
         banks = {}
 
-        def fuel_pass(half, t, plain, a):
+        def fuel_pass(half, t, plain, a, b=None):
             cols = slice(BANK * half, BANK * (half + 1))
             rows = slice(P * t, P * (t + 1))
             if a == 0:
-                ring_tag = "plain" if plain else "gelu"
-                banks[(half, t, plain)] = psum.tile([P, BANK], F32, name="fuel_bank", tag=ring_tag)
+                banks[(half, t, plain)] = bank(b)
             if plain:
                 codes, scales = w1_codes[:, a, rows].bitcast(FP4X4), w1_sc[a][:, rows]
             else:
@@ -180,24 +193,24 @@ def tile_list_wildfire_cell_tasking_kernel(
                 start=(a == 0), stop=(a == 1),
             )
 
+        def both_passes(half, t, plain, b):
+            for a in range(2):
+                fuel_pass(half, t, plain, a, b)
+
         for t in range(PACK):
-            fuel_pass(0, t, False, 0)
-            fuel_pass(0, t, True, 0)
+            fuel_pass(0, t, False, 0, t)
+        for t in SIDE_SLICES:
+            fuel_pass(1, t, True, 0, 5 + t)
+        for t in range(2):
+            fuel_pass(0, t, True, 0, PACK + t)
 
         act = {}
 
-        act_tags = {(0, 0): "w4_bf0", (0, PACK - 1): "w4_bf1"}
-
-        def fuel_gelu(half, t):
-            for a in range(1 - half, 2):
-                fuel_pass(half, t, False, a)
-            act[(half, t)] = held("act%d_%d" % (half, t), [P, BANK], F32, tag=act_tags.get((half, t)))
+        def fuel_gelu(half, t, tile=None):
+            act[(half, t)] = tile if tile is not None else held("act%d_%d" % (half, t), [P, BANK], F32)
             nc.scalar.activation(out=act[(half, t)][:], in_=banks[(half, t, False)][:], func=GELU)
 
-        def fuel_sum(half, t):
-            for a in range(1 - half, 2):
-                fuel_pass(half, t, True, a)
-            pieces = 2 if (half, t) == (0, PACK - 1) else 1
+        def fuel_sum(half, t, pieces=1):
             for i in range(pieces):
                 cols = slice(BANK // pieces * i, BANK // pieces * (i + 1))
                 nc.vector.tensor_tensor(
@@ -209,23 +222,27 @@ def tile_list_wildfire_cell_tasking_kernel(
         def gather_wind():
             nc.vector.tensor_copy(wind_codes[:], wind_win[:].indirect(offs2_sb[:]))
 
-        def meet_wind(chunk):
-            half, part = divmod(chunk, PACK)
+        wind_banks = {}
+
+        def wind_product(chunk, b):
             cols = slice(CHUNK * chunk, CHUNK * (chunk + 1))
-            cols_in_half = slice(CHUNK * part, CHUNK * (part + 1))
-            wind_bank = psum.tile([P, BANK], F32, name="wind_bank", tag="plain")
+            wind_banks[chunk] = bank(b)
             for t in range(PACK):
                 rows = slice(P * t, P * (t + 1))
                 nc.tensor.matmul_mx(
-                    out=wind_bank[:, rows], lhsT=w3_codes[:, rows].bitcast(FP8X4), lhsT_scale=w3_sc[:, rows],
+                    out=wind_banks[chunk][:, rows], lhsT=w3_codes[:, rows].bitcast(FP8X4), lhsT_scale=w3_sc[:, rows],
                     rhs=wind_codes[:, cols].bitcast(FP4X4), rhs_scale=wind_sc[:, cols],
                     start=True, stop=True,
                 )
+
+        def meet_wind(chunk):
+            half, part = divmod(chunk, PACK)
+            cols_in_half = slice(CHUNK * part, CHUNK * (part + 1))
             blk = max(i for i, (c0, w) in enumerate(BLOCKS) if c0 <= CHUNK * chunk)
             first = PACK * (CHUNK * chunk - BLOCKS[blk][0])
             nc.vector.tensor_tensor(
                 h_bf[blk][:, first : first + BANK].rearrange("p (m l t) -> p m t l", l=2, t=PACK),
-                wind_bank[:].rearrange("p (t m l) -> p m t l", l=2, t=PACK),
+                wind_banks[chunk][:].rearrange("p (t m l) -> p m t l", l=2, t=PACK),
                 fuel[half][:, :, cols_in_half].rearrange("p t (m l) -> p m t l", l=2),
                 ALU.mult,
             )
@@ -241,42 +258,46 @@ def tile_list_wildfire_cell_tasking_kernel(
         def round_w4(g):
             w4_bf[g] = held("w4_bf%d" % g, [P, PACK * PASS], BF16)
             dst = w4_bf[g][:].rearrange("p (t m j) -> p m j t", t=PACK, j=PACK)
-            src = w4_raw[:, g].rearrange("p j (m t) -> p m j t", t=PACK)
+            src = w4_raw[g][:].rearrange("p j (m t) -> p m j t", t=PACK)
             for m0 in range(0, P, W4_PIECE):
                 nc.scalar.copy(dst[:, m0 : m0 + W4_PIECE], src[:, m0 : m0 + W4_PIECE])
 
         def quantise_w4(g):
             nc.vector.quantize_mx(out=w4_codes[g][:].bitcast(FP8X4), scales=w4_sc[g][:], in_=w4_bf[g][:])
 
-        def task_rows(blk, g, ts):
+        sums = {}
+
+        def task_product(blk, g, first, b, emptied=None):
             c0, w = BLOCKS[blk]
             if (blk, g) not in y_f32:
                 y_f32[(blk, g)] = held("y%d_%d" % (blk, g), [P, PACK, w], F32)
+            task_bank = bank(b)
+            slices = range(first, first + BANK // w)
+            for s, t in enumerate(slices):
+                rows = slice(P * t, P * (t + 1))
+                nc.tensor.matmul_mx(
+                    out=task_bank[:, w * s : w * (s + 1)], lhsT=w4_codes[g][:, rows].bitcast(FP8X4),
+                    lhsT_scale=w4_sc[g][:, rows], rhs=h_codes[blk][:].bitcast(FP8X4), rhs_scale=h_sc[blk][:],
+                    start=True, stop=True,
+                )
+            source = task_bank
+            if emptied is not None:
+                source = emptied
+                nc.scalar.copy(source[:], task_bank[:])
+            for s, t in enumerate(slices):
+                sums[(blk, g, t)] = source[:, w * s : w * (s + 1)]
+
+        def clamp(blk, g, *ts):
+            c0, w = BLOCKS[blk]
             y = y_f32[(blk, g)]
             rows_out = out_0[PASS * g : PASS * (g + 1), c0 : c0 + w].rearrange("(p t) m -> p t m", t=PACK)
-            per_bank = BANK // w
-            for i in range(0, len(ts), per_bank):
-                ring_tag = "plain" if blk == len(BLOCKS) - 1 else "gelu"
-                task_bank = psum.tile([P, BANK], F32, name="task_bank", tag=ring_tag)
-                for s, t in enumerate(ts[i : i + per_bank]):
-                    rows = slice(P * t, P * (t + 1))
-                    nc.tensor.matmul_mx(
-                        out=task_bank[:, w * s : w * (s + 1)], lhsT=w4_codes[g][:, rows].bitcast(FP8X4),
-                        lhsT_scale=w4_sc[g][:, rows], rhs=h_codes[blk][:].bitcast(FP8X4), rhs_scale=h_sc[blk][:],
-                        start=True, stop=True,
-                    )
-                sums = task_bank
-                if blk == EMPTIED_BLOCK:
-                    sums = ring.tile([P, BANK], F32, name="sums")
-                    nc.scalar.copy(sums[:], task_bank[:])
-                for s, t in enumerate(ts[i : i + per_bank]):
-                    nc.vector.tensor_scalar(
-                        y[:, t, :], sums[:, w * s : w * (s + 1)],
-                        bounds[:, 0, g, t : t + 1], bounds[:, 1, g, t : t + 1], ALU.max, ALU.min,
-                    )
-                if (i + per_bank) % 2 == 0:
-                    pair = slice(ts[i + per_bank - 1] - 1, ts[i + per_bank - 1] + 1)
-                    nc.sync.dma_start(rows_out[:, pair, :], y[:, pair, :])
+            for t in ts:
+                nc.vector.tensor_scalar(
+                    y[:, t, :], sums[(blk, g, t)], bounds[:, 0, g, t : t + 1], bounds[:, 1, g, t : t + 1],
+                    ALU.max, ALU.min,
+                )
+                if t % 2 == 1:
+                    nc.sync.dma_start(rows_out[:, t - 1 : t + 1, :], y[:, t - 1 : t + 1, :])
 
         def round_y(blk, g, copies):
             c0, w = BLOCKS[blk]
@@ -303,51 +324,100 @@ def tile_list_wildfire_cell_tasking_kernel(
                     y_codes[(half, g)][:].bitcast(I32),
                 )
 
+        plain = held("plain", [P, len(SIDE_SLICES), BANK], F32)
+        for i, t in enumerate(SIDE_SLICES):
+            fuel_pass(1, t, True, 1)
+            nc.scalar.copy(plain[:, i, :], banks[(1, t, True)][:])
+        act_tags = {0: "w4_bf0", PACK - 1: "w4_bf1"}
+        for t in range(PACK):
+            fuel_pass(0, t, False, 1)
+            fuel_gelu(0, t, held("act0_%d" % t, [P, BANK], F32, tag=act_tags.get(t)))
+        fuel_pass(0, 0, True, 1)
+        fuel_pass(0, 1, True, 1)
+        both_passes(1, 1, False, 6)
+        fuel_gelu(1, 1)
+        both_passes(1, 2, False, 0)
+        fuel_gelu(1, 2)
+        both_passes(0, 2, True, 7)
+        both_passes(0, 3, True, 1)
         gather_wind()
-        fuel[0] = laid.tile([P, PACK, BANK], F32, name="fuel0", offset=0, align_bytes=64)
-        for t in range(PACK):
-            fuel_gelu(0, t)
-            fuel_sum(0, t)
-        nc.scalar.copy(
-            w3_codes[:].bitcast(U32).rearrange("p (t m) -> p m t", t=PACK),
-            w3_raw[:].bitcast(U32).rearrange("p (m t) -> p m t", t=PACK),
+        w3_codes = held("w3_codes", [P, H], I32)
+        nc.gpsimd.tensor_copy(
+            w3_codes[:].rearrange("p (t m l) -> p m t l", t=PACK, l=4),
+            w3_raw[:].rearrange("p (m l t) -> p m t l", t=PACK, l=4),
         )
+        fuel[0] = lay("fuel0", [P, PACK, BANK], F32, 0)
+        fuel[1] = lay("fuel1", [P, PACK, BANK], F32, 8 * KIB)
+        for i, t in enumerate(SIDE_SLICES):
+            nc.gpsimd.tensor_tensor(fuel[1][:, t, :], plain[:, i, :], act[(1, t)][:], ALU.add)
+        wind_product(0, 2)
+        wind_product(1, 3)
+        fuel_sum(0, 0)
+        wind_product(2, 4)
+        fuel_sum(0, 1)
+        wind_product(3, 5)
+        fuel_sum(0, 2)
+        both_passes(1, 0, False, 7)
+        fuel_sum(0, 3, 2)
+        both_passes(1, 3, False, 1)
         round_w4(0)
-        for t in range(PACK):
-            fuel_gelu(1, t)
-        round_w4(1)
-        for chunk in range(PACK):
-            meet_wind(chunk)
+        fuel_gelu(1, 0, lay("act1_0", [P, BANK], F32, AT_FUEL0))
+        fuel_gelu(1, 3, lay("act1_3", [P, BANK], F32, AT_FUEL0 + 2 * KIB))
+        meet_wind(0)
+        both_passes(1, 0, True, 2)
+        meet_wind(1)
+        both_passes(1, 3, True, 3)
+        meet_wind(2)
+        wind_product(4, 4)
+        meet_wind(3)
+        wind_product(5, 5)
         quantise_h(0)
         quantise_w4(0)
-        h_bf[1] = held("h_bf1", [P, PACK * BLOCKS[1][1]], BF16, tag="w4_bf0")
-
-        task_rows(0, 0, (0, 1))
+        round_w4(1)
+        emptied = [lay("sums%d" % i, [P, BANK], F32, AT_FUEL0 + 8 * KIB + 2 * KIB * i) for i in range(PACK)]
+        emptied += [held("sums%d" % i, [P, BANK], F32) for i in range(PACK, 7)]
         fuel_sum(1, 0)
-        fuel_sum(1, 1)
-        quantise_w4(1)
-        task_rows(0, 0, (2, 3))
-        fuel_sum(1, 2)
+        wind_product(6, 2)
         fuel_sum(1, 3)
-        task_rows(0, 1, (0, 1))
+        wind_product(7, 3)
+        task_product(0, 0, 0, 6)
+        for t, b in ((1, 0), (2, 7), (3, 1)):
+            task_product(0, 0, t, b, emptied[t - 1])
+        clamp(0, 0, 0)
+        quantise_w4(1)
+        for t, b in enumerate((6, 0, 7, 1)):
+            task_product(0, 1, t, b, emptied[3 + t])
+        h_bf[1] = held("h_bf1", [P, PACK * BLOCKS[1][1]], BF16, tag="w4_bf1")
+        clamp(0, 0, 1)
         meet_wind(4)
+        clamp(0, 0, 2)
         meet_wind(5)
-        task_rows(0, 1, (2, 3))
-        quantise_h(1)
+        clamp(0, 0, 3)
         round_y(0, 0, (nc.scalar.copy, nc.scalar.copy))
+        quantise_h(1)
+        task_product(1, 0, 0, 4)
+        task_product(1, 0, 2, 5)
+        every_slice = range(PACK)
+        clamp(0, 1, *every_slice)
+        round_y(0, 1, (nc.scalar.copy, nc.scalar.copy))
+        h_bf[2] = held("h_bf2", [P, PACK * BLOCKS[2][1]], BF16, tag="sums5")
+        clamp(1, 0, 0, 1)
         meet_wind(6)
         meet_wind(7)
-        every_slice = tuple(range(PACK))
-        task_rows(1, 0, every_slice)
-        quantise_h(2)
-        task_rows(1, 1, every_slice)
-        quantise_y(0, 0)
-        task_rows(2, 0, every_slice)
-        task_rows(2, 1, every_slice)
-        round_y(0, 1, (nc.scalar.copy, nc.scalar.copy))
+        task_product(1, 1, 0, 2)
+        task_product(1, 1, 2, 3)
+        clamp(1, 0, 2, 3)
         round_y(1, 0, (nc.scalar.copy,))
-        round_y(2, 0, (nc.scalar.copy,))
+        quantise_h(2)
+        for g, b0, b1 in ((0, 6, 0), (1, 7, 1)):
+            task_product(2, g, 0, b0)
+            task_product(2, g, 2, b1)
+        clamp(1, 1, *every_slice)
         round_y(1, 1, (nc.scalar.copy,))
+        quantise_y(0, 0)
+        clamp(2, 0, *every_slice)
+        round_y(2, 0, (nc.scalar.copy,))
+        clamp(2, 1, *every_slice)
         quantise_y(0, 1)
         round_y(2, 1, (nc.vector.tensor_copy, nc.scalar.copy))
         quantise_y(1, 0)

@@ -255,11 +255,10 @@ def tile_list_wildfire_cell_tasking_kernel(
                     in_=h_bf[blk][:, PACK * first : PACK * (first + H_PIECE)],
                 )
 
-        def round_w4(g):
-            w4_bf[g] = held("w4_bf%d" % g, [P, PACK * PASS], BF16)
+        def round_w4(g, first=0):
             dst = w4_bf[g][:].rearrange("p (t m j) -> p m j t", t=PACK, j=PACK)
             src = w4_raw[g][:].rearrange("p j (m t) -> p m j t", t=PACK)
-            for m0 in range(0, P, W4_PIECE):
+            for m0 in range(first, P, W4_PIECE):
                 nc.scalar.copy(dst[:, m0 : m0 + W4_PIECE], src[:, m0 : m0 + W4_PIECE])
 
         def quantise_w4(g):
@@ -331,11 +330,13 @@ def tile_list_wildfire_cell_tasking_kernel(
         act_tags = {0: "w4_bf0", PACK - 1: "w4_bf1"}
         for t in range(PACK):
             fuel_pass(0, t, False, 1)
+        for t in range(PACK - 1):
             fuel_gelu(0, t, held("act0_%d" % t, [P, BANK], F32, tag=act_tags.get(t)))
+        both_passes(1, 1, False, 6)
         fuel_pass(0, 0, True, 1)
         fuel_pass(0, 1, True, 1)
-        both_passes(1, 1, False, 6)
         fuel_gelu(1, 1)
+        fuel_gelu(0, PACK - 1, held("act0_3", [P, BANK], F32, tag="w4_bf1"))
         both_passes(1, 2, False, 0)
         fuel_gelu(1, 2)
         both_passes(0, 2, True, 7)
@@ -360,7 +361,13 @@ def tile_list_wildfire_cell_tasking_kernel(
         both_passes(1, 0, False, 7)
         fuel_sum(0, 3, 2)
         both_passes(1, 3, False, 1)
+        w4_bf[0] = held("w4_bf0", [P, PACK * PASS], BF16)
         round_w4(0)
+        w4_bf[1] = held("w4_bf1", [P, PACK * PASS], BF16)
+        nc.gpsimd.tensor_copy(
+            w4_bf[1][:].rearrange("p (t m j) -> p t m j", t=PACK, j=PACK)[:, :, :W4_PIECE],
+            w4_raw[1][:].rearrange("p j (m t) -> p t m j", t=PACK)[:, :, :W4_PIECE],
+        )
         fuel_gelu(1, 0, lay("act1_0", [P, BANK], F32, AT_FUEL0))
         fuel_gelu(1, 3, lay("act1_3", [P, BANK], F32, AT_FUEL0 + 2 * KIB))
         meet_wind(0)
@@ -373,22 +380,20 @@ def tile_list_wildfire_cell_tasking_kernel(
         wind_product(5, 5)
         quantise_h(0)
         quantise_w4(0)
-        round_w4(1)
+        round_w4(1, W4_PIECE)
         emptied = [lay("sums%d" % i, [P, BANK], F32, AT_FUEL0 + 8 * KIB + 2 * KIB * i) for i in range(PACK)]
-        emptied += [held("sums%d" % i, [P, BANK], F32) for i in range(PACK, 7)]
+        emptied += [held("sums%d" % i, [P, BANK], F32) for i in range(PACK, 8)]
         fuel_sum(1, 0)
         wind_product(6, 2)
         fuel_sum(1, 3)
         wind_product(7, 3)
-        task_product(0, 0, 0, 6)
-        for t, b in ((1, 0), (2, 7), (3, 1)):
-            task_product(0, 0, t, b, emptied[t - 1])
-        clamp(0, 0, 0)
+        for t, b in enumerate((6, 0, 7, 1)):
+            task_product(0, 0, t, b, emptied[t])
         quantise_w4(1)
         for t, b in enumerate((6, 0, 7, 1)):
-            task_product(0, 1, t, b, emptied[3 + t])
+            task_product(0, 1, t, b, emptied[PACK + t])
         h_bf[1] = held("h_bf1", [P, PACK * BLOCKS[1][1]], BF16, tag="w4_bf1")
-        clamp(0, 0, 1)
+        clamp(0, 0, 0, 1)
         meet_wind(4)
         clamp(0, 0, 2)
         meet_wind(5)
@@ -399,11 +404,19 @@ def tile_list_wildfire_cell_tasking_kernel(
         task_product(1, 0, 2, 5)
         every_slice = range(PACK)
         clamp(0, 1, *every_slice)
-        round_y(0, 1, (nc.scalar.copy, nc.scalar.copy))
-        h_bf[2] = held("h_bf2", [P, PACK * BLOCKS[2][1]], BF16, tag="sums5")
-        clamp(1, 0, 0, 1)
+        y_bf[(0, 1)] = held("y_bf0_1", [P, PACK * BANK], BF16)
+        nc.gpsimd.tensor_copy(
+            y_bf[(0, 1)][:, :BANK].rearrange("p (m t) -> p m t", t=PACK),
+            y_f32[(0, 1)][:, :, :CHUNK].rearrange("p t m -> p m t"),
+        )
+        nc.scalar.copy(
+            y_bf[(0, 1)][:, BANK:].rearrange("p (m l t) -> p m t l", l=4, t=PACK),
+            y_f32[(0, 1)][:, :, CHUNK:].rearrange("p t (m l) -> p m t l", l=4),
+        )
+        h_bf[2] = held("h_bf2", [P, PACK * BLOCKS[2][1]], BF16, tag="sums6")
         meet_wind(6)
         meet_wind(7)
+        clamp(1, 0, 0, 1)
         task_product(1, 1, 0, 2)
         task_product(1, 1, 2, 3)
         clamp(1, 0, 2, 3)
@@ -419,7 +432,7 @@ def tile_list_wildfire_cell_tasking_kernel(
         round_y(2, 0, (nc.scalar.copy,))
         clamp(2, 1, *every_slice)
         quantise_y(0, 1)
-        round_y(2, 1, (nc.vector.tensor_copy, nc.scalar.copy))
+        round_y(2, 1, (nc.scalar.copy,))
         quantise_y(1, 0)
         quantise_y(2, 0)
         quantise_y(1, 1)

from contextlib import ExitStack

import concourse.mybir as mybir

K, K2, H, N, T, S = 1024, 512, 512, 1024, 4096, 1024
FLOPS = 2 * S * (2 * K * H + K2 * H + H * N)

F32 = mybir.dt.float32
BF16 = mybir.dt.bfloat16
I32 = mybir.dt.int32
U32 = mybir.dt.uint32
U16 = mybir.dt.uint16
U8 = mybir.dt.uint8
FP8X4 = mybir.dt.float8_e4m3fn_x4
FP4X4 = mybir.dt.float4_e2m1fn_x4
ALU = mybir.AluOpType
GELU = mybir.ActivationFunctionType.Gelu_apprx_tanh

P = 128
PACK = 4
PASS = P * PACK
QUAD = 32
BANK = 512
CHUNK = BANK // PACK
W4_PIECE = 32

COL_W1, COL_W3, COL_WIND, COL_END = S, S + H, S + 2 * H, 2 * S + 2 * H

SIDE_SLICES = (1, 2)
KIB = 1024
AT_WIND, AT_W3, AT_FUEL0 = 4 * KIB, 12 * KIB, 16 * KIB

BLOCKS = ((0, 512), (512, 256), (768, 256))

H_PIECE = 256

EMPTIED_BLOCK = 0
EMPTIED_BANKS = 2 * PACK


def tile_list_wildfire_cell_tasking_kernel(
    tc, tab_words, tab_scales, tab2_words, tab2_scales, offs, offs2,
    w1_words, w1_scales, w2, w3_words, w3_scales, w4, lo, hi, out_0, out_1, out_2,
):
    nc = tc.nc
    with ExitStack() as ctx:
        keep = ctx.enter_context(tc.tile_pool(name="keep", bufs=1))
        laid = ctx.enter_context(tc.tile_pool(name="laid", bufs=1))
        psum = ctx.enter_context(tc.psum_pool(name="psum", bufs=1))

        def held(name, shape, dtype, tag=None):
            return keep.tile(shape, dtype, name=name, tag=tag or name, align_bytes=64)

        def lay(name, shape, dtype, at):
            return laid.tile(shape, dtype, name=name, offset=at, align_bytes=64)

        def bank(b):
            return psum.tile([P, BANK], F32, name="bank%d" % b, tag="bank%d" % b)

        table_in = held("table_in", [P, 1], F32)
        table_out = held("table_out", [P, 1], F32)
        nc.gpsimd.memset(table_in[:], 0.0)
        nc.scalar.activation(out=table_out[:], in_=table_in[:], func=GELU)

        wsc_raw = held("wsc_raw", [P, 2, H], U8)
        fuel_sc_win = held("fuel_sc_win", [P, T], U8)
        wind_sc_win = held("wind_sc_win", [P, T], U8)
        planes = [held("planes0", [P, COL_W3], U8), held("planes1", [P, COL_END], U8)]
        nc.vector.memset(fuel_sc_win[:].bitcast(I32), 0)
        nc.vector.memset(wsc_raw[:].rearrange("p a c -> p (a c)").bitcast(I32), 0)
        nc.vector.memset(wind_sc_win[:].bitcast(I32), 0)

        offs2_sb = keep.tile([P, S // 16], U16, name="offs2_sb")
        offs_sb = keep.tile([P, S // 16], U16, name="offs_sb")
        w1_raw = [
            lay("w1_raw0", [P, H], U16, AT_FUEL0),
            held("w1_raw1", [P, H], U16, tag="w1_then_w2_then_bounds"),
        ]
        for a in range(2):
            nc.sync.dma_start(w1_raw[a][:].bitcast(I32), w1_words[a].bitcast(I32))
        nc.sync.dma_start(offs_sb[:], offs)
        nc.sync.dma_start(offs2_sb[:], offs2)
        w2_raw = {0: held("w2_raw0", [P, PACK, H], F32)}
        nc.sync.dma_start(w2_raw[0][:], w2[:PASS, :].rearrange("(p j) c -> p j c", j=PACK))

        nc.sync.dma_start(fuel_sc_win[0:P:4, :].bitcast(I32), tab_scales.rearrange("a q t -> (a q) t").bitcast(I32))
        nc.sync.dma_start(wsc_raw[64:P:4, 1, :].bitcast(I32), w3_scales[0].bitcast(I32))
        nc.sync.dma_start(wsc_raw[0:P:4, 0, :].bitcast(I32), w1_scales.rearrange("a q c -> (a q) c").bitcast(I32))
        nc.sync.dma_start(wind_sc_win[64:P:4, :].bitcast(I32), tab2_scales[0].bitcast(I32))

        w1_codes = held("w1_codes", [P, 2, H], U16)
        w3_codes = held("w3_codes", [P, H], I32)
        for a in range(2):
            nc.scalar.copy(
                w1_codes[:, a, :].rearrange("p (t m) -> p m t", t=PACK),
                w1_raw[a][:].rearrange("p (m t) -> p m t", t=PACK),
            )
        fuel_win0 = lay("fuel_win0", [P, T], I32, AT_FUEL0)
        nc.sync.dma_start(fuel_win0[:], tab_words[0].rearrange("p t i -> p (t i)").bitcast(I32))

        w2_raw[1] = held("w2_raw1", [P, PACK, H], F32, tag="w1_then_w2_then_bounds")
        nc.sync.dma_start(w2_raw[1][:], w2[PASS:, :].rearrange("(p j) c -> p j c", j=PACK))

        for plane in planes:
            nc.vector.memset(plane[:].bitcast(I32), 0)

        spread = held("spread", [P, COL_END], U8)
        for i, col in ((0, COL_W1), (1, COL_W3)):
            nc.vector.tensor_copy(
                spread[:, col : col + H].rearrange("p (t m) -> p m t", t=PACK),
                wsc_raw[:, i, :].rearrange("p (m t) -> p m t", t=PACK),
            )

        def place_rows(a, end):
            for i in range(4):
                nc.sync.dma_start(
                    planes[a][i:P:QUAD, :].bitcast(I32),
                    spread[64 * a + 4 * i : 64 * (a + 1) : 16, :end].bitcast(I32),
                )

        fuel_sc_rows = held("fuel_sc_rows", [P, S], U8, tag="fuel_rows_then_fuel1")
        nc.vector.tensor_copy(fuel_sc_rows[:], fuel_sc_win[:].indirect(offs_sb[:]))
        nc.vector.tensor_copy(spread[:, :COL_W1].bitcast(I32), fuel_sc_rows[:].bitcast(I32))
        place_rows(0, COL_W3)
        fuel_win1 = held("fuel_win1", [P, T], I32, tag="fuel_rows_then_fuel1")
        nc.sync.dma_start(fuel_win1[:], tab_words[1].rearrange("p t i -> p (t i)").bitcast(I32))
        wind_sc_rows = lay("wind_sc_rows", [P, S], U8, AT_W3 - S // 2)
        nc.vector.tensor_copy(wind_sc_rows[:], wind_sc_win[:].indirect(offs2_sb[:]))
        nc.vector.tensor_copy(spread[:, COL_WIND:COL_END].bitcast(I32), wind_sc_rows[:].bitcast(I32))
        place_rows(1, COL_END)
        wind_win = lay("wind_win", [P, T], U16, AT_WIND)
        nc.sync.dma_start(wind_win[:].bitcast(I32), tab2_words[0].bitcast(I32))
        w3_raw = lay("w3_raw", [P, H], I32, AT_W3)
        nc.sync.dma_start(w3_raw[:], w3_words[0].rearrange("p c i -> p (c i)").bitcast(I32))

        fuel_sc = [planes[a][:, :COL_W1] for a in range(2)]
        w1_sc = [planes[a][:, COL_W1:COL_W3] for a in range(2)]
        w3_sc = planes[1][:, COL_W3:COL_WIND]
        wind_sc = planes[1][:, COL_WIND:COL_END]

        fuel_codes = {0: held("fuel_codes0", [P, S], U32)}
        nc.vector.tensor_copy(fuel_codes[0][:], fuel_win0[:].bitcast(U32).indirect(offs_sb[:]))

        w2_codes, w2_sc = {}, {}
        for a in range(2):
            w2_bf = held("w2_bf%d" % a, [P, PACK * H], BF16)
            nc.scalar.copy(
                w2_bf[:].rearrange("p (t m j) -> p m j t", t=PACK, j=PACK),
                w2_raw[a][:].rearrange("p j (m t) -> p m j t", t=PACK),
            )
            w2_codes[a] = held("w2_codes%d" % a, [P, H], U32)
            w2_sc[a] = held("w2_sc%d" % a, [P, H], U8)
            nc.vector.quantize_mx(out=w2_codes[a][:].bitcast(FP8X4), scales=w2_sc[a][:], in_=w2_bf[:])

        w4_rows = w4.rearrange("(p j) n -> p j n", j=PACK)
        w4_raw = [lay("w4_raw%d" % g, [P, PACK, PASS], F32, AT_FUEL0 + 8 * KIB * g) for g in range(2)]
        for g in range(2):
            nc.sync.dma_start(w4_raw[g][:], w4_rows[:, :, PASS * g : PASS * (g + 1)])
        bounds = held("bounds", [P, 2, 2, PACK], F32, tag="w1_then_w2_then_bounds")
        nc.sync.dma_start(bounds[:, 0], lo.rearrange("(g p t) -> p g t", g=2, t=PACK))
        nc.sync.dma_start(bounds[:, 1], hi.rearrange("(g p t) -> p g t", g=2, t=PACK))

        fuel_codes[1] = held("fuel_codes1", [P, S], U32, tag="w2_bf1")
        for half in (1, 0):
            nc.vector.tensor_copy(
                fuel_codes[1][:, BANK * half : BANK * (half + 1)],
                fuel_win1[:].bitcast(U32).indirect(offs_sb[:, BANK // 16 * half : BANK // 16 * (half + 1)]),
            )

        h_bf = {blk: held("h_bf%d" % blk, [P, PACK * BLOCKS[blk][1]], BF16) for blk in (0,)}
        h_codes = [held("h_codes%d" % blk, [P, w], U32) for blk, (c0, w) in enumerate(BLOCKS)]
        h_sc = [held("h_sc%d" % blk, [P, w], U8) for blk, (c0, w) in enumerate(BLOCKS)]
        w4_codes = [held("w4_codes%d" % g, [P, PASS], U32) for g in range(2)]
        w4_sc = [held("w4_sc%d" % g, [P, PASS], U8) for g in range(2)]
        y_sc = held("y_sc", [P, S], U8)
        fuel = {}
        w4_bf, y_f32, y_bf = {}, {}, {}

        banks = {}

        def fuel_pass(half, t, plain, a, b=None):
            cols = slice(BANK * half, BANK * (half + 1))
            rows = slice(P * t, P * (t + 1))
            if a == 0:
                banks[(half, t, plain)] = bank(b)
            if plain:
                codes, scales = w1_codes[:, a, rows].bitcast(FP4X4), w1_sc[a][:, rows]
            else:
                codes, scales = w2_codes[a][:, rows].bitcast(FP8X4), w2_sc[a][:, rows]
            nc.tensor.matmul_mx(
                out=banks[(half, t, plain)][:], lhsT=codes, lhsT_scale=scales,
                rhs=fuel_codes[a][:, cols].bitcast(FP8X4), rhs_scale=fuel_sc[a][:, cols],
                start=(a == 0), stop=(a == 1),
            )

        def both_passes(half, t, plain, b):
            for a in range(2):
                fuel_pass(half, t, plain, a, b)

        for t in range(PACK):
            fuel_pass(0, t, False, 0, t)
        for t in SIDE_SLICES:
            fuel_pass(1, t, True, 0, 5 + t)
        for t in range(2):
            fuel_pass(0, t, True, 0, PACK + t)

        act = {}

        def fuel_gelu(half, t, tile=None):
            act[(half, t)] = tile if tile is not None else held("act%d_%d" % (half, t), [P, BANK], F32)
            nc.scalar.activation(out=act[(half, t)][:], in_=banks[(half, t, False)][:], func=GELU)

        def fuel_sum(half, t, pieces=1):
            for i in range(pieces):
                cols = slice(BANK // pieces * i, BANK // pieces * (i + 1))
                nc.vector.tensor_tensor(
                    fuel[half][:, t, cols], banks[(half, t, True)][:, cols], act[(half, t)][:, cols], ALU.add
                )

        wind_codes = held("wind_codes", [P, S], U16, tag="fuel_rows_then_fuel1")

        def gather_wind():
            nc.vector.tensor_copy(wind_codes[:], wind_win[:].indirect(offs2_sb[:]))

        wind_banks = {}

        def wind_product(chunk, b):
            cols = slice(CHUNK * chunk, CHUNK * (chunk + 1))
            wind_banks[chunk] = bank(b)
            for t in range(PACK):
                rows = slice(P * t, P * (t + 1))
                nc.tensor.matmul_mx(
                    out=wind_banks[chunk][:, rows], lhsT=w3_codes[:, rows].bitcast(FP8X4), lhsT_scale=w3_sc[:, rows],
                    rhs=wind_codes[:, cols].bitcast(FP4X4), rhs_scale=wind_sc[:, cols],
                    start=True, stop=True,
                )

        def meet_wind(chunk):
            half, part = divmod(chunk, PACK)
            cols_in_half = slice(CHUNK * part, CHUNK * (part + 1))
            blk = max(i for i, (c0, w) in enumerate(BLOCKS) if c0 <= CHUNK * chunk)
            first = PACK * (CHUNK * chunk - BLOCKS[blk][0])
            nc.vector.tensor_tensor(
                h_bf[blk][:, first : first + BANK].rearrange("p (m l t) -> p m t l", l=2, t=PACK),
                wind_banks[chunk][:].rearrange("p (t m l) -> p m t l", l=2, t=PACK),
                fuel[half][:, :, cols_in_half].rearrange("p t (m l) -> p m t l", l=2),
                ALU.mult,
            )

        def quantise_h(blk):
            for first in range(0, BLOCKS[blk][1], H_PIECE):
                cells = slice(first, first + H_PIECE)
                nc.vector.quantize_mx(
                    out=h_codes[blk][:, cells].bitcast(FP8X4), scales=h_sc[blk][:, cells],
                    in_=h_bf[blk][:, PACK * first : PACK * (first + H_PIECE)],
                )

        def round_w4(g, first=0):
            dst = w4_bf[g][:].rearrange("p (t m j) -> p m j t", t=PACK, j=PACK)
            src = w4_raw[g][:].rearrange("p j (m t) -> p m j t", t=PACK)
            for m0 in range(first, P, W4_PIECE):
                nc.scalar.copy(dst[:, m0 : m0 + W4_PIECE], src[:, m0 : m0 + W4_PIECE])

        def quantise_w4(g):
            nc.vector.quantize_mx(out=w4_codes[g][:].bitcast(FP8X4), scales=w4_sc[g][:], in_=w4_bf[g][:])

        sums = {}

        def task_product(blk, g, first, b, emptied=None):
            c0, w = BLOCKS[blk]
            if (blk, g) not in y_f32:
                y_f32[(blk, g)] = held("y%d_%d" % (blk, g), [P, PACK, w], F32)
            task_bank = bank(b)
            slices = range(first, first + BANK // w)
            for s, t in enumerate(slices):
                rows = slice(P * t, P * (t + 1))
                nc.tensor.matmul_mx(
                    out=task_bank[:, w * s : w * (s + 1)], lhsT=w4_codes[g][:, rows].bitcast(FP8X4),
                    lhsT_scale=w4_sc[g][:, rows], rhs=h_codes[blk][:].bitcast(FP8X4), rhs_scale=h_sc[blk][:],
                    start=True, stop=True,
                )
            source = task_bank
            if emptied is not None:
                source = emptied
                nc.scalar.copy(source[:], task_bank[:])
            for s, t in enumerate(slices):
                sums[(blk, g, t)] = source[:, w * s : w * (s + 1)]

        def clamp(blk, g, *ts):
            c0, w = BLOCKS[blk]
            y = y_f32[(blk, g)]
            rows_out = out_0[PASS * g : PASS * (g + 1), c0 : c0 + w].rearrange("(p t) m -> p t m", t=PACK)
            for t in ts:
                nc.vector.tensor_scalar(
                    y[:, t, :], sums[(blk, g, t)], bounds[:, 0, g, t : t + 1], bounds[:, 1, g, t : t + 1],
                    ALU.max, ALU.min,
                )
                if t % 2 == 1:
                    nc.sync.dma_start(rows_out[:, t - 1 : t + 1, :], y[:, t - 1 : t + 1, :])

        def round_y(blk, g, copies):
            c0, w = BLOCKS[blk]
            y_bf[(blk, g)] = held("y_bf%d_%d" % (blk, g), [P, PACK * w], BF16)
            dst = y_bf[(blk, g)][:].rearrange("p (m l t) -> p m t l", l=4, t=PACK)
            src = y_f32[(blk, g)][:].rearrange("p t (m l) -> p m t l", l=4)
            share = w // 4 // len(copies)
            for i, copy in enumerate(copies):
                copy(dst[:, share * i : share * (i + 1)], src[:, share * i : share * (i + 1)])

        y_codes = {(half, g): held("y_codes%d_%d" % (half, g), [P, BANK], U32) for half in range(2) for g in range(2)}

        def quantise_y(blk, g):
            c0, w = BLOCKS[blk]
            half, first = divmod(c0, BANK)
            nc.vector.quantize_mx(
                out=y_codes[(half, g)][:, first : first + w].bitcast(FP8X4), scales=y_sc[4 * g :, c0 : c0 + w],
                in_=y_bf[(blk, g)][:],
            )
            if first + w == BANK:
                cells = slice(BANK * half, BANK * (half + 1))
                nc.sync.dma_start(
                    out_1[g, :, cells, :].rearrange("p m t -> p (m t)").bitcast(I32),
                    y_codes[(half, g)][:].bitcast(I32),
                )

        plain = held("plain", [P, len(SIDE_SLICES), BANK], F32)
        for i, t in enumerate(SIDE_SLICES):
            fuel_pass(1, t, True, 1)
            nc.scalar.copy(plain[:, i, :], banks[(1, t, True)][:])
        act_tags = {0: "w4_bf0", PACK - 1: "w4_bf1"}
        for t in range(PACK):
            fuel_pass(0, t, False, 1)
        for t in range(PACK - 1):
            fuel_gelu(0, t, held("act0_%d" % t, [P, BANK], F32, tag=act_tags.get(t)))
        both_passes(1, 1, False, 6)
        fuel_pass(0, 0, True, 1)
        fuel_pass(0, 1, True, 1)
        fuel_gelu(1, 1)
        fuel_gelu(0, PACK - 1, held("act0_3", [P, BANK], F32, tag="w4_bf1"))
        both_passes(1, 2, False, 0)
        fuel_gelu(1, 2)
        both_passes(0, 2, True, 7)
        both_passes(0, 3, True, 1)
        gather_wind()
        w3_codes = held("w3_codes", [P, H], I32)
        nc.gpsimd.tensor_copy(
            w3_codes[:].rearrange("p (t m l) -> p m t l", t=PACK, l=4),
            w3_raw[:].rearrange("p (m l t) -> p m t l", t=PACK, l=4),
        )
        fuel[0] = lay("fuel0", [P, PACK, BANK], F32, 0)
        fuel[1] = lay("fuel1", [P, PACK, BANK], F32, 8 * KIB)
        for i, t in enumerate(SIDE_SLICES):
            nc.gpsimd.tensor_tensor(fuel[1][:, t, :], plain[:, i, :], act[(1, t)][:], ALU.add)
        wind_product(0, 2)
        wind_product(1, 3)
        fuel_sum(0, 0)
        wind_product(2, 4)
        fuel_sum(0, 1)
        wind_product(3, 5)
        fuel_sum(0, 2)
        both_passes(1, 0, False, 7)
        fuel_sum(0, 3, 2)
        both_passes(1, 3, False, 1)
        w4_bf[0] = held("w4_bf0", [P, PACK * PASS], BF16)
        round_w4(0)
        w4_bf[1] = held("w4_bf1", [P, PACK * PASS], BF16)
        nc.gpsimd.tensor_copy(
            w4_bf[1][:].rearrange("p (t m j) -> p t m j", t=PACK, j=PACK)[:, :, :W4_PIECE],
            w4_raw[1][:].rearrange("p j (m t) -> p t m j", t=PACK)[:, :, :W4_PIECE],
        )
        fuel_gelu(1, 0, lay("act1_0", [P, BANK], F32, AT_FUEL0))
        fuel_gelu(1, 3, lay("act1_3", [P, BANK], F32, AT_FUEL0 + 2 * KIB))
        meet_wind(0)
        both_passes(1, 0, True, 2)
        meet_wind(1)
        both_passes(1, 3, True, 3)
        meet_wind(2)
        wind_product(4, 4)
        meet_wind(3)
        wind_product(5, 5)
        quantise_h(0)
        quantise_w4(0)
        round_w4(1, W4_PIECE)
        emptied = [lay("sums%d" % i, [P, BANK], F32, AT_FUEL0 + 8 * KIB + 2 * KIB * i) for i in range(PACK)]
        emptied += [held("sums%d" % i, [P, BANK], F32) for i in range(PACK, 8)]
        fuel_sum(1, 0)
        wind_product(6, 2)
        fuel_sum(1, 3)
        wind_product(7, 3)
        for t, b in enumerate((6, 0, 7, 1)):
            task_product(0, 0, t, b, emptied[t])
        quantise_w4(1)
        for t, b in enumerate((6, 0, 7, 1)):
            task_product(0, 1, t, b, emptied[PACK + t])
        h_bf[1] = held("h_bf1", [P, PACK * BLOCKS[1][1]], BF16, tag="w4_bf1")
        clamp(0, 0, 0, 1)
        meet_wind(4)
        clamp(0, 0, 2)
        meet_wind(5)
        clamp(0, 0, 3)
        round_y(0, 0, (nc.scalar.copy, nc.scalar.copy))
        quantise_h(1)
        task_product(1, 0, 0, 4)
        task_product(1, 0, 2, 5)
        every_slice = range(PACK)
        clamp(0, 1, *every_slice)
        y_bf[(0, 1)] = held("y_bf0_1", [P, PACK * BANK], BF16)
        nc.gpsimd.tensor_copy(
            y_bf[(0, 1)][:, :BANK].rearrange("p (m t) -> p m t", t=PACK),
            y_f32[(0, 1)][:, :, :CHUNK].rearrange("p t m -> p m t"),
        )
        nc.scalar.copy(
            y_bf[(0, 1)][:, BANK:].rearrange("p (m l t) -> p m t l", l=4, t=PACK),
            y_f32[(0, 1)][:, :, CHUNK:].rearrange("p t (m l) -> p m t l", l=4),
        )
        h_bf[2] = held("h_bf2", [P, PACK * BLOCKS[2][1]], BF16, tag="sums6")
        meet_wind(6)
        meet_wind(7)
        clamp(1, 0, 0, 1)
        task_product(1, 1, 0, 2)
        task_product(1, 1, 2, 3)
        clamp(1, 0, 2, 3)
        round_y(1, 0, (nc.scalar.copy,))
        quantise_h(2)
        for g, b0, b1 in ((0, 6, 0), (1, 7, 1)):
            task_product(2, g, 0, b0)
            task_product(2, g, 2, b1)
        clamp(1, 1, *every_slice)
        round_y(1, 1, (nc.scalar.copy,))
        quantise_y(0, 0)
        clamp(2, 0, *every_slice)
        round_y(2, 0, (nc.scalar.copy,))
        clamp(2, 1, *every_slice)
        quantise_y(0, 1)
        round_y(2, 1, (nc.scalar.copy,))
        quantise_y(1, 0)
        quantise_y(2, 0)
        quantise_y(1, 1)
        quantise_y(2, 1)

        for q in range(4):
            nc.sync.dma_start(
                out_2[:, 4 * q : 4 * q + 4, :].bitcast(I32), y_sc[QUAD * q : QUAD * q + 8, :].bitcast(I32)
            )
